import numpy as np
import ml_dtypes


def mxq(x, axis, fmt="e4m3"):
    dtype, down = {"e4m3": (ml_dtypes.float8_e4m3fn, 7), "e5m2": (ml_dtypes.float8_e5m2, 14)}[fmt]
    v = np.moveaxis(np.asarray(x, np.float32).astype(ml_dtypes.bfloat16).astype(np.float64), axis, -1)
    blocks = v.reshape(v.shape[:-1] + (-1, 32))
    amax = np.abs(blocks).max(-1, keepdims=True)
    byte = np.maximum(np.where(amax > 0, np.frexp(amax)[1] - 1 + 127, 0) - down, 1)
    scale = np.exp2(byte - 127.0)
    codes = (blocks / scale).astype(np.float32).astype(dtype).astype(np.float64)
    return np.moveaxis((codes * scale).reshape(v.shape), -1, axis)


WIDE = False


def mx_kscale(k):
    if not WIDE:
        return np.ones(k)
    levels = np.array([10, -10, 5, -5, 0])
    if k % 512:
        return np.exp2(np.random.permutation(np.resize(levels, k // 32))).repeat(32)
    a = np.empty((k // 512, 16))
    for p in range(k // 512):
        a[p, :8] = np.random.permutation(np.resize(levels, 8))
        for g in range(8):
            far = levels[np.abs(levels - a[p, g]) >= 10]
            a[p, g + 8] = far[np.random.randint(len(far))]
    return np.exp2(a.ravel()).repeat(32)


BF16 = ml_dtypes.bfloat16


def bf(x):
    return np.asarray(x, np.float32).astype(BF16)


def f64(x):
    return np.asarray(x).astype(np.float64)


E2M1 = np.array([0.0, 0.5, 1.0, 1.5, 2.0, 3.0, 4.0, 6.0, -0.0, -0.5, -1.0, -1.5, -2.0, -3.0, -4.0, -6.0])


def pack_weight(w, fmt):
    k, n = w.shape
    w = f64(bf(w)).reshape(k // 32, 32, n)
    amax = np.abs(w).max(1)
    if fmt == "e4m3":
        byte = np.frexp(amax)[1] - 1 + 127 - 7
    else:
        mant, ex = np.frexp(amax / 6.0)
        byte = np.where(mant > 0.5, ex, ex - 1) + 127
    byte = np.clip(np.where(amax > 0, byte, 1), 1, 254)
    scaled = (w * np.exp2(127.0 - byte)[:, None, :]).reshape(k, n).astype(np.float32)
    by_word = np.ascontiguousarray(scaled.reshape(k // 512, 128, 4, n).transpose(0, 1, 3, 2))
    if fmt == "e4m3":
        words = by_word.astype(ml_dtypes.float8_e4m3fn).view(np.uint8)
    else:
        c = by_word.astype(ml_dtypes.float4_e2m1fn).view(np.uint8) & 0xF
        words = c[..., 0::2] | (c[..., 1::2] << 4)
    return np.ascontiguousarray(words), np.ascontiguousarray(byte.astype(np.uint8).reshape(k // 512, 16, n))


def unpack_weight(words, scales, fmt):
    g, p, n, _ = words.shape
    if fmt == "e4m3":
        vals = np.ascontiguousarray(words).view(ml_dtypes.float8_e4m3fn).astype(np.float64)
    else:
        nib = np.empty((g, p, n, 4), np.uint8)
        nib[..., 0::2] = words & 0xF
        nib[..., 1::2] = words >> 4
        vals = E2M1[nib]
    vals = vals * np.repeat(np.exp2(scales.astype(np.float64) - 127.0), 8, axis=1)[..., None]
    return vals.transpose(0, 1, 3, 2).reshape(g * 512, n)
def pack4(w):
    words, scales = pack_weight(w, "e2m1")
    return words.reshape(words.shape[0], 128, -1), scales


def unpack4(words, scales):
    return unpack_weight(words.reshape(words.shape[0], 128, -1, 2), scales, "e2m1")


R, F, T, D, C = 1024, 1024, 2048, 1536, 512


def draw0():
    s, u = mx_kscale(F), mx_kscale(D)
    v = mx_kscale(T)
    w_p = np.random.standard_normal((D, C)) / np.sqrt(D) / T ** 0.25 / u[:, None]
    w_p_words, w_p_scales = pack4(w_p)
    return {"w_f": bf(np.random.standard_normal((R, F)) / np.sqrt(F) / T ** 0.25 * s),
            "y_f": bf(np.random.standard_normal((F, T)) / s[:, None]),
            "z_p": bf(np.random.standard_normal((D, T)) * u[:, None] / v),
            "w_p_words": w_p_words,
            "w_p_scales": w_p_scales,
            "level": bf(0.3 * np.random.standard_normal(R) / T ** 0.25),
            "lam": bf(np.random.uniform(0.5, 1.5, T) * v),
            "rho": bf(1 + 0.1 * np.random.standard_normal(R))}


def core(w_f, y_f, z_p, w_p_words, w_p_scales, level, lam, rho):
    fut = mxq(f64(w_f), 1, "e4m3") @ mxq(f64(y_f), 0, "e4m3")
    fut = (fut + f64(level)[:, None]) * f64(lam)
    past = mxq(f64(z_p), 0, "e4m3").T @ unpack4(w_p_words, w_p_scales)
    h = mxq(fut, 1, "e4m3") @ mxq(past, 0, "e4m3")
    return h * f64(rho)[:, None]


def e4m3fn_bytes(y):
    return np.clip(np.asarray(y, np.float64), -448.0, 448.0).astype(np.float32).astype(ml_dtypes.float8_e4m3fn).view(np.uint8)


def e4m3fn_values(b):
    return np.asarray(b, np.uint8).view(ml_dtypes.float8_e4m3fn).astype(np.float64)


def setup_inputs():
    d = draw0()
    x0 = np.asarray(d['y_f']).astype(np.float64)
    s = (np.max(np.abs(x0), axis=(1,), keepdims=True) / 448.0).astype(np.float32)
    out = {}
    for k, v in d.items():
        if k == 'y_f':
            out['y_f_bytes'] = e4m3fn_bytes(x0 / s.astype(np.float64))
            out['y_f_scale'] = s
        else:
            out[k] = v
    return out


def reference(w_f, y_f_bytes, y_f_scale, z_p, w_p_words, w_p_scales, level, lam, rho):
    return core(w_f, e4m3fn_values(y_f_bytes) * y_f_scale.astype(np.float64), z_p, w_p_words, w_p_scales, level, lam, rho)

@@ -1,0 +1,646 @@
+from contextlib import ExitStack
+
+import concourse.mybir as mybir
+from concourse.masks import make_identity
+
+R, F, T, D, C = 1024, 1024, 2048, 1536, 512
+FLOPS = 2 * (R * F * T + T * D * C + R * T * C)
+
+F32 = mybir.dt.float32
+BF16 = mybir.dt.bfloat16
+U32 = mybir.dt.uint32
+I32 = mybir.dt.int32
+U8 = mybir.dt.uint8
+FP8 = mybir.dt.float8_e4m3fn
+FP8X4 = mybir.dt.float8_e4m3fn_x4
+FP4X4 = mybir.dt.float4_e2m1fn_x4
+ADD = mybir.AluOpType.add
+MULT = mybir.AluOpType.mult
+COPY = mybir.ActivationFunctionType.Copy
+
+P = 128
+GROUPS = T // 512
+FP = F // 512
+DP = D // 512
+RT = R // P
+OPEN = 4
+
+
+def tile_weighted_hankel_subspace_s11_kernel(
+    tc, w_f, y_f_bytes, y_f_scale, z_p, w_p_words, w_p_scales, level, lam, rho, out
+):
+    nc = tc.nc
+    with ExitStack() as ctx:
+        keep = ctx.enter_context(tc.tile_pool(name="keep", bufs=1))
+        work = ctx.enter_context(tc.tile_pool(name="work", bufs=2))
+        psum = ctx.enter_context(tc.psum_pool(name="psum", bufs=1))
+
+        ident = keep.tile([P, P], F32, name="ident")
+
+        make_identity(nc, ident[:])
+        y_scale = keep.tile([P, FP, 4], F32, name="y_scale")
+        lev16 = keep.tile([P, RT], BF16, name="lev16")
+        rho16 = keep.tile([P, RT], BF16, name="rho16")
+        lev = keep.tile([P, RT], F32, name="lev")
+        rhos = keep.tile([P, RT], F32, name="rhos")
+        lam_row = keep.tile([P, T], BF16, name="lam_row")
+        ones = keep.tile([P, P], BF16, name="ones")
+        nc.gpsimd.memset(lam_row[:], 0.0)
+        nc.gpsimd.memset(ones[:], 1.0)
+        lam_ord = keep.tile([P, T], BF16, name="lam_ord")
+        wf = keep.tile([P, RT, F], BF16, name="wf", align_bytes=64)
+        wi = keep.tile([P, FP, R, 4], BF16, name="wi", align_bytes=64)
+        wcode = keep.tile([P, FP, R], U32, name="wcode", align_bytes=64)
+        wscale = keep.tile([P, FP, R], U8, name="wscale", align_bytes=64)
+        pw = keep.tile([P, DP, 2 * C], U8, name="pw", align_bytes=64)
+        pws = keep.tile([P, DP, C], U8, name="pws", align_bytes=64)
+        acode = keep.tile([P, GROUPS, R], U32, name="acode", align_bytes=64)
+        ascale = keep.tile([P, GROUPS, R], U8, name="ascale", align_bytes=64)
+        bcode = keep.tile([P, GROUPS, C], U32, name="bcode", align_bytes=64)
+        bscale = keep.tile([P, GROUPS, C], U8, name="bscale", align_bytes=64)
+
+        y_view = y_f_bytes.rearrange("(g p t) n -> g p t n", g=FP, p=P, t=4)
+        z_view = z_p.rearrange("(g p t) n -> g p t n", g=DP, p=P, t=4)
+        w_view = w_f.rearrange("(p c) f -> p c f", c=RT)
+        out_view = out.rearrange("(p c) n -> p c n", c=RT)
+
+        tiles = {}
+
+        def load_y(g, f):
+            if f == 0:
+                tiles["yb", g] = work.tile([P, FP, 4, 512], U8, name="yb", align_bytes=64)
+            step = 2 if (g, f) == (0, 0) else 4
+            for t in range(0, 4, step):
+                nc.sync.dma_start(
+                    out=tiles["yb", g][:, f, t : t + step, :], in_=y_view[f][:, t : t + step, 512 * g : 512 * g + 512]
+                )
+
+        def load_z(g, d):
+            zr = work.tile([P, 4, 512], BF16, name="zr", bufs=8, align_bytes=64)
+            nc.sync.dma_start(out=zr[:], in_=z_view[d][:, :, 512 * g : 512 * g + 512])
+            tiles["zr", g, d] = zr
+
+        def load_w(c0, n):
+            nc.sync.dma_start(out=wf[:, c0 : c0 + n, :], in_=w_view[:, c0 : c0 + n, :])
+
+        def widen(g, f, t, eng):
+            if t == 0:
+                tiles["yw", g, f] = work.tile([P, 4, 512], BF16, name="yw", bufs=3, align_bytes=64)
+            src = tiles["yb", g][:, f, t, :].bitcast(FP8)
+            dst = tiles["yw", g, f][:, t, :]
+            s = y_scale[:, f, t : t + 1]
+            if eng == "S":
+                nc.scalar.activation(out=dst, in_=src, func=COPY, scale=s)
+            else:
+                nc.vector.tensor_scalar(out=dst, in0=src, scalar1=s, scalar2=None, op0=MULT)
+
+        def ilv_y(g, f, u, eng):
+            if u == 0:
+                tiles["yi", g, f] = work.tile([P, 512, 4], BF16, name="yi", bufs=3, align_bytes=64)
+            dst = tiles["yi", g, f][:, 256 * u : 256 * u + 256, :].rearrange("p (q e) t -> p q t e", e=2)
+            src = tiles["yw", g, f][:].rearrange("p t (q u e) -> p u q t e", u=2, e=2)[:, u]
+            if eng == "S":
+                nc.scalar.copy(out=dst, in_=src)
+            else:
+                nc.vector.tensor_copy(out=dst, in_=src)
+
+        def quant_y(g, f):
+            if f == 0:
+                tiles["yc", g] = work.tile([P, FP, 512], U32, name="yc", align_bytes=64)
+                tiles["ys", g] = work.tile([P, FP, 512], U8, name="ys", align_bytes=64)
+            nc.vector.quantize_mx(
+                out=tiles["yc", g][:, f, :].bitcast(FP8X4),
+                scales=tiles["ys", g][:, f, :],
+                in_=tiles["yi", g, f][:].rearrange("p n t -> p (n t)"),
+            )
+
+        def ilv_z(g, d, h, eng):
+            if h == 0:
+                tiles["zi", g, d] = work.tile([P, 4, 128, 4], BF16, name="zi", bufs=4, align_bytes=64)
+            dst = tiles["zi", g, d][:].rearrange("p s m j -> p m j s")[:, 64 * h : 64 * h + 64]
+            src = tiles["zr", g, d][:].rearrange("p j (m s) -> p m j s", s=4)[:, 64 * h : 64 * h + 64]
+            if eng == "S":
+                nc.scalar.copy(out=dst, in_=src)
+            else:
+                nc.vector.tensor_copy(out=dst, in_=src)
+
+        def quant_z(g, d):
+            if d == 0:
+                tiles["zc", g] = work.tile([P, DP, 512], U32, name="zc", align_bytes=64)
+                tiles["zs", g] = work.tile([P, DP, 512], U8, name="zs", align_bytes=64)
+            nc.vector.quantize_mx(
+                out=tiles["zc", g][:, d, :].bitcast(FP8X4),
+                scales=tiles["zs", g][:, d, :],
+                in_=tiles["zi", g, d][:].rearrange("p s m j -> p (s m j)"),
+            )
+
+        def w_transpose(c):
+            tag = W_TAGS[c]
+            wt = psum.tile([P, FP, 2, P], F32, name=tag, bufs=PS[tag])
+            words = wf[:, c, :].bitcast(F32)
+            for f in range(FP):
+                for u in range(2):
+                    nc.tensor.transpose(wt[:, f, u, :], words[:, 256 * f + u : 256 * (f + 1) : 2], ident[:])
+            tiles["wt", c] = wt
+
+        def w_copy(c, eng):
+            dst = wi[:].rearrange("p f r j -> p (f r j)").bitcast(F32)
+            dst = dst.rearrange("p (f r u) -> p f r u", f=FP, u=2)[:, :, P * c : P * c + P, :]
+            src = tiles["wt", c][:].rearrange("p f u r -> p f r u")
+            if eng == "S":
+                nc.scalar.copy(out=dst, in_=src)
+            else:
+                nc.vector.tensor_copy(out=dst, in_=src)
+
+        def w_quant(f, r0, n):
+            nc.vector.quantize_mx(
+                out=wcode[:, f, r0 : r0 + n].bitcast(FP8X4),
+                scales=wscale[:, f, r0 : r0 + n],
+                in_=wi[:, f, r0 : r0 + n, :].rearrange("p r j -> p (r j)"),
+            )
+
+        PS = {"fut": 2, "past": 2}
+        W_TAGS = ["fut", "past", "fut", "past", "fut", "past", "fut", "past"]
+        H_TAGS = ["h0", "h1", "h2", "h3", "fut", "past", "fut", "past"]
+
+        def past(g, cc):
+            pp = psum.tile([P, 4, 128], F32, name="past", bufs=PS["past"])
+            for s in range(4):
+                for d in range(DP):
+                    nc.tensor.matmul_mx(
+                        out=pp[:, s, :],
+                        lhsT=tiles["zc", g][:, d, 128 * s : 128 * s + 128].bitcast(FP8X4),
+                        lhsT_scale=tiles["zs", g][:, d, 128 * s : 128 * s + 128],
+                        rhs=pw[:, d, 256 * cc : 256 * cc + 256].bitcast(FP4X4),
+                        rhs_scale=pws[:, d, 128 * cc : 128 * cc + 128],
+                        start=(d == 0),
+                        stop=(d == DP - 1),
+                    )
+            tiles["pp", g, cc] = pp
+
+        def past_copy(g, cc, eng):
+            if cc == 0:
+                tiles["pi", g] = work.tile([P, 512, 4], BF16, name="pi", align_bytes=64)
+            dst = tiles["pi", g][:, 128 * cc : 128 * cc + 128, :]
+            src = tiles["pp", g, cc][:].rearrange("p s n -> p n s")
+            if eng == "S":
+                nc.scalar.copy(out=dst, in_=src)
+            else:
+                nc.vector.tensor_copy(out=dst, in_=src)
+
+        def quant_past(g):
+            nc.vector.quantize_mx(
+                out=bcode[:, g, :].bitcast(FP8X4),
+                scales=bscale[:, g, :],
+                in_=tiles["pi", g][:].rearrange("p n s -> p (n s)"),
+            )
+
+        def fut(g, c):
+            fp = psum.tile([P, 512], F32, name="fut", bufs=PS["fut"])
+            for f in range(FP):
+                nc.tensor.matmul_mx(
+                    out=fp[:],
+                    lhsT=wcode[:, f, P * c : P * c + P].bitcast(FP8X4),
+                    lhsT_scale=wscale[:, f, P * c : P * c + P],
+                    rhs=tiles["yc", g][:, f, :].bitcast(FP8X4),
+                    rhs_scale=tiles["ys", g][:, f, :],
+                    start=(f == 0),
+                    stop=(f == FP - 1),
+                )
+            tiles["fp", g, c] = fp
+
+        def a_op(g, c):
+            at = work.tile([P, 512], BF16, name="at", bufs=7, align_bytes=64)
+            nc.vector.scalar_tensor_tensor(
+                out=at[:],
+                in0=tiles["fp", g, c][:],
+                scalar=lev[:, c : c + 1],
+                in1=lam_ord[:, 512 * g : 512 * g + 512],
+                op0=ADD,
+                op1=MULT,
+            )
+            tiles["at", g, c] = at
+
+        def tr(q):
+            for k in range(2):
+                tp = psum.tile([P, 2, 2, P], F32, name="past", bufs=PS["past"])
+                for i in range(2):
+                    j = 4 * q + 2 * k + i
+                    words = tiles["at", j // RT, j % RT][:].bitcast(F32)
+                    for u in range(2):
+                        nc.tensor.transpose(tp[:, i, u, :], words[:, P * u : P * u + P], ident[:])
+                tiles["tp", 2 * q + k] = tp
+
+        def tr_copy(q, eng):
+            g, c0 = q // 4, 2 * (q % 4)
+            if c0 == 0:
+                tiles["ai", g] = work.tile([P, R, 4], BF16, name="ai", align_bytes=64)
+            dst = tiles["ai", g][:].rearrange("p r j -> p (r j)").bitcast(F32)
+            dst = dst.rearrange("p (c r u) -> p c r u", r=P, u=2)[:, c0 : c0 + 2]
+            src = tiles["tp", q][:].rearrange("p c u r -> p c r u")
+            if eng == "S":
+                nc.scalar.copy(out=dst, in_=src)
+            else:
+                nc.vector.tensor_copy(out=dst, in_=src)
+
+        def quant_a(q, n):
+            g, r0 = q // 4, 256 * (q % 4)
+            nc.vector.quantize_mx(
+                out=acode[:, g, r0 : r0 + 256 * n].bitcast(FP8X4),
+                scales=ascale[:, g, r0 : r0 + 256 * n],
+                in_=tiles["ai", g][:, r0 : r0 + 256 * n, :].rearrange("p r j -> p (r j)"),
+            )
+
+        def h_pass(c, g):
+            tag = H_TAGS[c]
+            if g == 0:
+                tiles["h", c] = psum.tile([P, C], F32, name=tag, bufs=PS.get(tag, 1))
+            nc.tensor.matmul_mx(
+                out=tiles["h", c][:],
+                lhsT=acode[:, g, P * c : P * c + P].bitcast(FP8X4),
+                lhsT_scale=ascale[:, g, P * c : P * c + P],
+                rhs=bcode[:, g, :].bitcast(FP8X4),
+                rhs_scale=bscale[:, g, :],
+                start=(g == 0),
+                stop=(g == GROUPS - 1),
+            )
+
+        def h_out(c, eng):
+            if c == 0:
+                tiles["ho"] = keep.tile([P, RT, C], F32, name="wf", align_bytes=64)
+            ho = tiles["ho"][:, c, :]
+            if eng == "S":
+                nc.scalar.activation(out=ho, in_=tiles["h", c][:], func=COPY, scale=rhos[:, c : c + 1])
+            else:
+                nc.vector.tensor_scalar(
+                    out=ho, in0=tiles["h", c][:], scalar1=rhos[:, c : c + 1], scalar2=None, op0=MULT
+                )
+            nc.sync.dma_start(out=out_view[:, c, :], in_=ho)
+
+        def load_lam():
+            nc.sync.dma_start(out=lam_row[0:1, :], in_=lam.rearrange("(o n) -> o n", o=1))
+
+        def spread_lam(i):
+            lp = psum.tile([P, 2, 512], BF16, name="h%d" % i)
+            for k in range(2):
+                g = 2 * i + k
+                nc.tensor.matmul(out=lp[:, k, :], lhsT=ones[:], rhs=lam_row[:, 512 * g : 512 * g + 512], start=True, stop=True)
+            tiles["lp", i] = lp
+
+        def order_lam(i, k, eng):
+            g = 2 * i + k
+            dst = lam_ord[:, 512 * g : 512 * g + 512].rearrange("p (u q e) -> p u q e", u=2, e=2)
+            src = tiles["lp", i][:, k, :].rearrange("p (q u e) -> p u q e", u=2, e=2)
+            if eng == "S":
+                nc.scalar.copy(out=dst, in_=src)
+            else:
+                nc.vector.tensor_copy(out=dst, in_=src)
+
+
+        def small_loads():
+            nc.scalar.dma_start(out=y_scale[:], in_=y_f_scale.rearrange("(g p t) o -> p g (t o)", g=FP, p=P, t=4))
+            nc.scalar.dma_start(out=lev16[:], in_=level.rearrange("(p c) -> p c", c=RT))
+            nc.scalar.dma_start(out=rho16[:], in_=rho.rearrange("(p c) -> p c", c=RT))
+
+        def load_pw():
+            nc.sync.dma_start(out=pw[:], in_=w_p_words.rearrange("d p n -> p d n"))
+
+        def clear_pws():
+            nc.vector.memset(pws[:].rearrange("p d n -> p (d n)").bitcast(I32), 0)
+
+        def load_pws():
+            for q in range(4):
+                nc.sync.dma_start(
+                    out=pws[32 * q : 32 * q + 4, :, :].bitcast(I32),
+                    in_=w_p_scales[:, 4 * q : 4 * q + 4, :].rearrange("d q n -> q d n").bitcast(I32),
+                )
+
+        def widen_small():
+            nc.vector.tensor_copy(out=lev[:], in_=lev16[:])
+            nc.vector.tensor_copy(out=rhos[:], in_=rho16[:])
+
+        with tc.manual_schedule():
+            small_loads()
+            load_y(0, 0)
+            widen(0, 0, 0, "S")
+            widen(0, 0, 1, "V")
+            widen(0, 0, 3, "V")
+            load_y(0, 1)
+            widen(0, 0, 2, "S")
+            load_y(1, 0)
+            load_w(0, 2)
+            widen(0, 1, 0, "S")
+            load_w(2, 2)
+            widen(0, 1, 1, "S")
+            load_z(0, 0)
+            w_transpose(1)
+            widen(0, 1, 3, "S")
+            load_w(4, 2)
+            load_y(1, 1)
+            load_lam()
+            load_z(0, 1)
+            w_transpose(0)
+            w_transpose(2)
+            load_w(6, 2)
+            clear_pws()
+            load_z(0, 2)
+            w_transpose(3)
+            widen(0, 1, 2, "V")
+            widen(1, 0, 0, "S")
+            widen(1, 0, 3, "S")
+            load_y(2, 0)
+            load_pw()
+            widen(1, 0, 1, "V")
+            widen(1, 0, 2, "S")
+            w_copy(0, "S")
+            ilv_y(0, 0, 0, "V")
+            ilv_y(0, 1, 0, "V")
+            w_copy(1, "S")
+            w_transpose(5)
+            ilv_y(0, 1, 1, "V")
+            ilv_y(0, 0, 1, "V")
+            load_pws()
+            ilv_y(1, 0, 0, "V")
+            quant_y(0, 0)
+            load_z(1, 0)
+            ilv_y(1, 0, 1, "V")
+            ilv_z(0, 0, 0, "V")
+            quant_y(0, 1)
+            load_z(1, 1)
+            w_copy(2, "S")
+            quant_y(1, 0)
+            w_copy(3, "S")
+            ilv_z(0, 0, 1, "S")
+            widen(1, 1, 0, "S")
+            w_quant(1, 0, 256)
+            w_copy(5, "S")
+            w_quant(0, 256, 256)
+            w_transpose(4)
+            widen(1, 1, 1, "S")
+            w_quant(0, 0, 256)
+            widen(1, 1, 2, "S")
+            quant_z(0, 0)
+            widen_small()
+            widen(1, 1, 3, "S")
+            w_quant(1, 256, 256)
+            ilv_z(0, 1, 0, "V")
+            w_copy(4, "S")
+            ilv_y(1, 1, 0, "V")
+            ilv_z(0, 1, 1, "V")
+            w_quant(1, 512, 256)
+            spread_lam(0)
+            order_lam(0, 0, "S")
+            w_quant(0, 512, 256)
+            spread_lam(1)
+            ilv_y(1, 1, 1, "S")
+            order_lam(1, 1, "S")
+            w_transpose(6)
+            w_copy(6, "S")
+            load_y(2, 1)
+            fut(0, 0)
+            w_transpose(7)
+            ilv_z(0, 2, 0, "V")
+            fut(0, 1)
+            load_z(1, 2)
+            a_op(0, 0)
+            a_op(0, 1)
+            load_z(2, 0)
+            fut(0, 2)
+            order_lam(1, 0, "S")
+            ilv_z(0, 2, 1, "S")
+            widen(2, 0, 0, "S")
+            load_y(3, 0)
+            widen(2, 0, 1, "S")
+            widen(2, 0, 2, "S")
+            order_lam(0, 1, "S")
+            quant_z(0, 1)
+            load_z(2, 1)
+            fut(0, 3)
+            load_z(2, 2)
+            a_op(0, 2)
+            a_op(0, 3)
+            quant_z(0, 2)
+            widen(2, 0, 3, "S")
+            quant_y(1, 1)
+            load_y(3, 1)
+            w_copy(7, "S")
+            ilv_y(2, 0, 0, "S")
+            ilv_y(2, 0, 1, "V")
+            w_quant(0, 768, 256)
+            w_quant(1, 768, 256)
+            fut(0, 4)
+            a_op(0, 4)
+            fut(0, 5)
+            past(0, 0)
+            past_copy(0, 0, "S")
+            past(0, 1)
+            a_op(0, 5)
+            fut(0, 6)
+            past_copy(0, 1, "S")
+            ilv_z(1, 0, 0, "S")
+            tr(0)
+            fut(0, 7)
+            ilv_z(1, 0, 1, "V")
+            tr_copy(0, "S")
+            a_op(0, 6)
+            tr_copy(1, "S")
+            ilv_z(1, 1, 0, "V")
+            fut(1, 0)
+            quant_y(2, 0)
+            a_op(0, 7)
+            past(0, 2)
+            widen(2, 1, 0, "S")
+            quant_z(1, 0)
+            past(0, 3)
+            a_op(1, 0)
+            ilv_z(1, 1, 1, "S")
+            quant_a(0, 2)
+            widen(2, 1, 2, "S")
+            fut(1, 1)
+            past_copy(0, 2, "S")
+            fut(1, 2)
+            load_z(3, 0)
+            ilv_z(1, 2, 0, "V")
+            past_copy(0, 3, "S")
+            ilv_z(2, 0, 0, "S")
+            ilv_z(1, 2, 1, "V")
+            a_op(1, 1)
+            tr(1)
+            tr_copy(2, "S")
+            widen(2, 1, 1, "S")
+            tr_copy(3, "S")
+            load_z(3, 1)
+            quant_z(1, 2)
+            a_op(1, 2)
+            fut(1, 3)
+            widen(2, 1, 3, "S")
+            ilv_z(2, 1, 0, "S")
+            quant_z(1, 1)
+            a_op(1, 3)
+            fut(1, 4)
+            past(1, 0)
+            past(1, 1)
+            past_copy(1, 0, "S")
+            past_copy(1, 1, "S")
+            fut(1, 5)
+            ilv_z(2, 0, 1, "V")
+            load_z(3, 2)
+            quant_past(0)
+            a_op(1, 4)
+            ilv_z(2, 1, 1, "V")
+            ilv_y(2, 1, 0, "V")
+            a_op(1, 5)
+            ilv_z(2, 2, 0, "S")
+            fut(1, 6)
+            tr(2)
+            tr_copy(4, "S")
+            ilv_y(2, 1, 1, "V")
+            tr_copy(5, "S")
+            fut(1, 7)
+            a_op(1, 6)
+            quant_y(2, 1)
+            a_op(1, 7)
+            past(1, 2)
+            fut(2, 0)
+            h_pass(1, 0)
+            past(1, 3)
+            widen(3, 0, 0, "S")
+            widen(3, 1, 0, "S")
+            quant_z(2, 0)
+            widen(3, 0, 3, "S")
+            fut(2, 1)
+            a_op(2, 0)
+            fut(2, 2)
+            widen(3, 1, 1, "S")
+            past_copy(1, 2, "S")
+            past_copy(1, 3, "S")
+            widen(3, 1, 2, "S")
+            widen(3, 0, 2, "S")
+            widen(3, 0, 1, "S")
+            tr(3)
+            ilv_z(2, 2, 1, "V")
+            ilv_z(3, 0, 0, "V")
+            tr_copy(6, "S")
+            a_op(2, 1)
+            h_pass(0, 0)
+            quant_z(2, 2)
+            a_op(2, 2)
+            quant_z(2, 1)
+            fut(2, 3)
+            h_pass(3, 0)
+            quant_a(4, 2)
+            tr_copy(7, "S")
+            quant_a(2, 2)
+            a_op(2, 3)
+            fut(2, 4)
+            a_op(2, 4)
+            past(2, 0)
+            past(2, 1)
+            fut(2, 5)
+            widen(3, 1, 3, "S")
+            ilv_y(3, 0, 0, "S")
+            past_copy(2, 0, "S")
+            fut(2, 6)
+            quant_past(1)
+            ilv_y(3, 1, 0, "V")
+            past_copy(2, 1, "S")
+            tr(4)
+            a_op(2, 5)
+            fut(2, 7)
+            ilv_z(3, 1, 0, "S")
+            h_pass(1, 1)
+            ilv_y(3, 0, 1, "V")
+            tr_copy(8, "S")
+            ilv_y(3, 1, 1, "S")
+            a_op(2, 6)
+            past(2, 2)
+            h_pass(2, 0)
+            h_pass(0, 1)
+            tr_copy(9, "S")
+            ilv_z(3, 0, 1, "S")
+            ilv_z(3, 2, 0, "V")
+            a_op(2, 7)
+            quant_y(3, 0)
+            h_pass(3, 1)
+            quant_y(3, 1)
+            ilv_z(3, 1, 1, "V")
+            quant_z(3, 0)
+            past(2, 3)
+            fut(3, 0)
+            past_copy(2, 2, "S")
+            fut(3, 1)
+            h_pass(2, 1)
+            past_copy(2, 3, "S")
+            ilv_z(3, 2, 1, "S")
+            a_op(3, 0)
+            tr(5)
+            tr_copy(10, "S")
+            a_op(3, 1)
+            fut(3, 2)
+            quant_z(3, 1)
+            fut(3, 3)
+            quant_z(3, 2)
+            tr_copy(11, "S")
+            past(3, 0)
+            past(3, 1)
+            quant_past(2)
+            a_op(3, 2)
+            past_copy(3, 0, "S")
+            a_op(3, 3)
+            quant_a(10, 2)
+            quant_a(6, 2)
+            fut(3, 4)
+            fut(3, 5)
+            a_op(3, 4)
+            quant_a(8, 2)
+            a_op(3, 5)
+            past_copy(3, 1, "S")
+            tr(6)
+            fut(3, 6)
+            tr_copy(12, "V")
+            h_pass(3, 2)
+            tr_copy(13, "S")
+            fut(3, 7)
+            quant_a(12, 2)
+            past(3, 2)
+            a_op(3, 6)
+            past(3, 3)
+            h_pass(0, 2)
+            h_pass(1, 2)
+            h_pass(2, 2)
+            a_op(3, 7)
+            past_copy(3, 3, "S")
+            past_copy(3, 2, "V")
+            h_pass(4, 0)
+            tr(7)
+            h_pass(4, 1)
+            tr_copy(14, "S")
+            quant_past(3)
+            tr_copy(15, "V")
+            h_pass(0, 3)
+            h_out(0, "S")
+            h_pass(2, 3)
+            h_out(2, "S")
+            h_pass(1, 3)
+            h_pass(6, 0)
+            h_pass(3, 3)
+            quant_a(14, 2)
+            h_pass(4, 2)
+            h_pass(6, 1)
+            h_pass(6, 2)
+            h_pass(4, 3)
+            h_pass(5, 0)
+            h_pass(5, 1)
+            h_out(1, "V")
+            h_pass(5, 2)
+            h_pass(5, 3)
+            h_pass(6, 3)
+            h_out(3, "V")
+            h_out(4, "V")
+            h_out(5, "S")
+            h_pass(7, 0)
+            h_pass(7, 1)
+            h_pass(7, 2)
+            h_pass(7, 3)
+            h_out(6, "V")
+            h_out(7, "V")

@@ -24,6 +24,13 @@ FP = F // 512
 DP = D // 512
 RT = R // P
 OPEN = 4
+Y_G = 0
+Z_S = (256, 240, 224, 256)
+Z_LATE = (384, 240, 224, 384)
+HEAD_V = 6
+Q_AT = 1
+W_FIRST = 3
+HEAD_S = 2
 
 
 def tile_weighted_hankel_subspace_s11_kernel(
@@ -36,8 +43,6 @@ def tile_weighted_hankel_subspace_s11_kernel(
         psum = ctx.enter_context(tc.psum_pool(name="psum", bufs=1))
 
         ident = keep.tile([P, P], F32, name="ident")
-
-        make_identity(nc, ident[:])
         y_scale = keep.tile([P, FP, 4], F32, name="y_scale")
         lev16 = keep.tile([P, RT], BF16, name="lev16")
         rho16 = keep.tile([P, RT], BF16, name="rho16")
@@ -45,13 +50,9 @@ def tile_weighted_hankel_subspace_s11_kernel(
         rhos = keep.tile([P, RT], F32, name="rhos")
         lam_row = keep.tile([P, T], BF16, name="lam_row")
         ones = keep.tile([P, P], BF16, name="ones")
-        nc.gpsimd.memset(lam_row[:], 0.0)
-        nc.gpsimd.memset(ones[:], 1.0)
         lam_ord = keep.tile([P, T], BF16, name="lam_ord")
-        wf = keep.tile([P, RT, F], BF16, name="wf", align_bytes=64)
-        wi = keep.tile([P, FP, R, 4], BF16, name="wi", align_bytes=64)
-        wcode = keep.tile([P, FP, R], U32, name="wcode", align_bytes=64)
-        wscale = keep.tile([P, FP, R], U8, name="wscale", align_bytes=64)
+        wcode = keep.tile([P, RT, FP, P], U32, name="wcode", align_bytes=64)
+        wscale = keep.tile([P, RT, FP, P], U8, name="wscale", align_bytes=64)
         pw = keep.tile([P, DP, 2 * C], U8, name="pw", align_bytes=64)
         pws = keep.tile([P, DP, C], U8, name="pws", align_bytes=64)
         acode = keep.tile([P, GROUPS, R], U32, name="acode", align_bytes=64)
@@ -65,44 +66,56 @@ def tile_weighted_hankel_subspace_s11_kernel(
         out_view = out.rearrange("(p c) n -> p c n", c=RT)
 
         tiles = {}
+        turns = []
+
+        def next_bank(shape, dtype):
+            tag = "turn%d" % (len(turns) % 4)
+            turns.append(tag)
+            return psum.tile(shape, dtype, name=tag)
+
+        def copy(eng, dst, src):
+            if eng == "S":
+                nc.scalar.copy(out=dst, in_=src)
+            else:
+                nc.vector.tensor_copy(out=dst, in_=src)
 
         def load_y(g, f):
-            if f == 0:
-                tiles["yb", g] = work.tile([P, FP, 4, 512], U8, name="yb", align_bytes=64)
-            step = 2 if (g, f) == (0, 0) else 4
-            for t in range(0, 4, step):
-                nc.sync.dma_start(
-                    out=tiles["yb", g][:, f, t : t + step, :], in_=y_view[f][:, t : t + step, 512 * g : 512 * g + 512]
-                )
+            yb = work.tile([P, 4, 512], U8, name="yb", bufs=6, align_bytes=64)
+            nc.sync.dma_start(out=yb[:], in_=y_view[f][:, :, 512 * g : 512 * g + 512])
+            tiles["yb", g, f] = yb
 
         def load_z(g, d):
-            zr = work.tile([P, 4, 512], BF16, name="zr", bufs=8, align_bytes=64)
+            zr = work.tile([P, 4, 512], BF16, name="zr", bufs=9, align_bytes=64)
             nc.sync.dma_start(out=zr[:], in_=z_view[d][:, :, 512 * g : 512 * g + 512])
             tiles["zr", g, d] = zr
 
-        def load_w(c0, n):
-            nc.sync.dma_start(out=wf[:, c0 : c0 + n, :], in_=w_view[:, c0 : c0 + n, :])
+        def load_w(pair):
+            wf = work.tile([P, 2, F], BF16, name="wf", bufs=4, align_bytes=64)
+            nc.sync.dma_start(out=wf[:], in_=w_view[:, 2 * pair : 2 * pair + 2, :])
+            tiles["wf", pair] = wf
 
         def widen(g, f, t, eng):
-            if t == 0:
-                tiles["yw", g, f] = work.tile([P, 4, 512], BF16, name="yw", bufs=3, align_bytes=64)
-            src = tiles["yb", g][:, f, t, :].bitcast(FP8)
-            dst = tiles["yw", g, f][:, t, :]
+            if ("yw", g) not in tiles:
+                tiles["yw", g] = work.tile([P, FP, 4, 512], BF16, name="yw", align_bytes=64)
+            src = tiles["yb", g, f][:, t, :].bitcast(FP8)
+            dst = tiles["yw", g][:, f, t, :]
             s = y_scale[:, f, t : t + 1]
             if eng == "S":
                 nc.scalar.activation(out=dst, in_=src, func=COPY, scale=s)
             else:
                 nc.vector.tensor_scalar(out=dst, in0=src, scalar1=s, scalar2=None, op0=MULT)
 
-        def ilv_y(g, f, u, eng):
-            if u == 0:
-                tiles["yi", g, f] = work.tile([P, 512, 4], BF16, name="yi", bufs=3, align_bytes=64)
-            dst = tiles["yi", g, f][:, 256 * u : 256 * u + 256, :].rearrange("p (q e) t -> p q t e", e=2)
-            src = tiles["yw", g, f][:].rearrange("p t (q u e) -> p u q t e", u=2, e=2)[:, u]
-            if eng == "S":
-                nc.scalar.copy(out=dst, in_=src)
+        def ilv_y(g, f0, f1, n0, n1, eng):
+            if ("yi", g) not in tiles:
+                tiles["yi", g] = work.tile([P, FP, 512, 4], BF16, name="yi", bufs=1, align_bytes=64)
+            dst = tiles["yi", g][:, f0:f1, n0:n1]
+            src = tiles["yw", g][:, f0:f1, :, n0:n1]
+            if eng == "G":
+                nc.gpsimd.tensor_scalar(
+                    out=dst, in0=src.rearrange("p f t n -> p f n t"), scalar1=1.0, scalar2=0.0, op0=MULT, op1=ADD
+                )
             else:
-                nc.vector.tensor_copy(out=dst, in_=src)
+                copy(eng, dst.rearrange("p f (c i) t -> p f c t i", i=4), src.rearrange("p f t (c i) -> p f c t i", i=4))
 
         def quant_y(g, f):
             if f == 0:
@@ -111,18 +124,15 @@ def tile_weighted_hankel_subspace_s11_kernel(
             nc.vector.quantize_mx(
                 out=tiles["yc", g][:, f, :].bitcast(FP8X4),
                 scales=tiles["ys", g][:, f, :],
-                in_=tiles["yi", g, f][:].rearrange("p n t -> p (n t)"),
+                in_=tiles["yi", g][:, f].rearrange("p n t -> p (n t)"),
             )
 
-        def ilv_z(g, d, h, eng):
-            if h == 0:
-                tiles["zi", g, d] = work.tile([P, 4, 128, 4], BF16, name="zi", bufs=4, align_bytes=64)
-            dst = tiles["zi", g, d][:].rearrange("p s m j -> p m j s")[:, 64 * h : 64 * h + 64]
-            src = tiles["zr", g, d][:].rearrange("p j (m s) -> p m j s", s=4)[:, 64 * h : 64 * h + 64]
-            if eng == "S":
-                nc.scalar.copy(out=dst, in_=src)
-            else:
-                nc.vector.tensor_copy(out=dst, in_=src)
+        def ilv_z(g, d, m0, m1, eng):
+            if ("zi", g, d) not in tiles:
+                tiles["zi", g, d] = work.tile([P, 4, 128, 4], BF16, name="zi", bufs=6, align_bytes=64)
+            dst = tiles["zi", g, d][:].rearrange("p s m j -> p m j s")[:, m0:m1]
+            src = tiles["zr", g, d][:].rearrange("p j (m s) -> p m j s", s=4)[:, m0:m1]
+            copy(eng, dst, src)
 
         def quant_z(g, d):
             if d == 0:
@@ -135,40 +145,30 @@ def tile_weighted_hankel_subspace_s11_kernel(
             )
 
         def w_transpose(c):
-            tag = W_TAGS[c]
-            wt = psum.tile([P, FP, 2, P], F32, name=tag, bufs=PS[tag])
-            words = wf[:, c, :].bitcast(F32)
+            wt = psum.tile([P, FP, 2, P], F32, name="h%d" % c) if c < OPEN else next_bank([P, FP, 2, P], F32)
+            words = tiles["wf", c // 2][:, c % 2, :].bitcast(F32)
             for f in range(FP):
                 for u in range(2):
                     nc.tensor.transpose(wt[:, f, u, :], words[:, 256 * f + u : 256 * (f + 1) : 2], ident[:])
             tiles["wt", c] = wt
 
         def w_copy(c, eng):
-            dst = wi[:].rearrange("p f r j -> p (f r j)").bitcast(F32)
-            dst = dst.rearrange("p (f r u) -> p f r u", f=FP, u=2)[:, :, P * c : P * c + P, :]
-            src = tiles["wt", c][:].rearrange("p f u r -> p f r u")
-            if eng == "S":
-                nc.scalar.copy(out=dst, in_=src)
-            else:
-                nc.vector.tensor_copy(out=dst, in_=src)
+            if c % 2 == 0:
+                tiles["wi", c // 2] = work.tile([P, 2, FP, P, 2], F32, name="ai", bufs=4, align_bytes=64)
+            copy(eng, tiles["wi", c // 2][:, c % 2], tiles["wt", c][:].rearrange("p f u r -> p f r u"))
 
-        def w_quant(f, r0, n):
+        def w_quant(pair):
             nc.vector.quantize_mx(
-                out=wcode[:, f, r0 : r0 + n].bitcast(FP8X4),
-                scales=wscale[:, f, r0 : r0 + n],
-                in_=wi[:, f, r0 : r0 + n, :].rearrange("p r j -> p (r j)"),
+                out=wcode[:, 2 * pair : 2 * pair + 2].rearrange("p c f r -> p (c f r)").bitcast(FP8X4),
+                scales=wscale[:, 2 * pair : 2 * pair + 2].rearrange("p c f r -> p (c f r)"),
+                in_=tiles["wi", pair][:].rearrange("p c f r u -> p (c f r u)").bitcast(BF16),
             )
 
-        PS = {"fut": 2, "past": 2}
-        W_TAGS = ["fut", "past", "fut", "past", "fut", "past", "fut", "past"]
-        H_TAGS = ["h0", "h1", "h2", "h3", "fut", "past", "fut", "past"]
-
-        def past(g, cc):
-            pp = psum.tile([P, 4, 128], F32, name="past", bufs=PS["past"])
+        def past(g, cc, pp):
             for s in range(4):
                 for d in range(DP):
                     nc.tensor.matmul_mx(
-                        out=pp[:, s, :],
+                        out=pp[:, 2 * (s % 2) + s // 2, :],
                         lhsT=tiles["zc", g][:, d, 128 * s : 128 * s + 128].bitcast(FP8X4),
                         lhsT_scale=tiles["zs", g][:, d, 128 * s : 128 * s + 128],
                         rhs=pw[:, d, 256 * cc : 256 * cc + 256].bitcast(FP4X4),
@@ -182,26 +182,22 @@ def tile_weighted_hankel_subspace_s11_kernel(
             if cc == 0:
                 tiles["pi", g] = work.tile([P, 512, 4], BF16, name="pi", align_bytes=64)
             dst = tiles["pi", g][:, 128 * cc : 128 * cc + 128, :]
-            src = tiles["pp", g, cc][:].rearrange("p s n -> p n s")
-            if eng == "S":
-                nc.scalar.copy(out=dst, in_=src)
-            else:
-                nc.vector.tensor_copy(out=dst, in_=src)
+            copy(eng, dst, tiles["pp", g, cc][:].rearrange("p s n -> p n s"))
 
-        def quant_past(g):
+        def quant_past(g, n0, n1):
             nc.vector.quantize_mx(
-                out=bcode[:, g, :].bitcast(FP8X4),
-                scales=bscale[:, g, :],
-                in_=tiles["pi", g][:].rearrange("p n s -> p (n s)"),
+                out=bcode[:, g, n0:n1].bitcast(FP8X4),
+                scales=bscale[:, g, n0:n1],
+                in_=tiles["pi", g][:, n0:n1, :].rearrange("p n s -> p (n s)"),
             )
 
         def fut(g, c):
-            fp = psum.tile([P, 512], F32, name="fut", bufs=PS["fut"])
+            fp = next_bank([P, 512], F32)
             for f in range(FP):
                 nc.tensor.matmul_mx(
                     out=fp[:],
-                    lhsT=wcode[:, f, P * c : P * c + P].bitcast(FP8X4),
-                    lhsT_scale=wscale[:, f, P * c : P * c + P],
+                    lhsT=wcode[:, c, f, :].bitcast(FP8X4),
+                    lhsT_scale=wscale[:, c, f, :],
                     rhs=tiles["yc", g][:, f, :].bitcast(FP8X4),
                     rhs_scale=tiles["ys", g][:, f, :],
                     start=(f == 0),
@@ -210,103 +206,86 @@ def tile_weighted_hankel_subspace_s11_kernel(
             tiles["fp", g, c] = fp
 
         def a_op(g, c):
-            at = work.tile([P, 512], BF16, name="at", bufs=7, align_bytes=64)
+            at = work.tile([P, 512], BF16, name="at", bufs=RT, align_bytes=64)
             nc.vector.scalar_tensor_tensor(
-                out=at[:],
-                in0=tiles["fp", g, c][:],
+                out=at[:].rearrange("p (u q) -> p u q", u=2),
+                in0=tiles["fp", g, c][:].rearrange("p (q u) -> p u q", u=2),
                 scalar=lev[:, c : c + 1],
-                in1=lam_ord[:, 512 * g : 512 * g + 512],
+                in1=lam_ord[:, 512 * g : 512 * g + 512].rearrange("p (u q) -> p u q", u=2),
                 op0=ADD,
                 op1=MULT,
             )
             tiles["at", g, c] = at
 
-        def tr(q):
-            for k in range(2):
-                tp = psum.tile([P, 2, 2, P], F32, name="past", bufs=PS["past"])
-                for i in range(2):
-                    j = 4 * q + 2 * k + i
-                    words = tiles["at", j // RT, j % RT][:].bitcast(F32)
-                    for u in range(2):
-                        nc.tensor.transpose(tp[:, i, u, :], words[:, P * u : P * u + P], ident[:])
-                tiles["tp", 2 * q + k] = tp
+        def tr(g, pair):
+            tp = next_bank([P, 2, 2, P], F32)
+            for i in range(2):
+                words = tiles["at", g, 2 * pair + i][:].bitcast(F32)
+                for u in range(2):
+                    nc.tensor.transpose(tp[:, i, u, :], words[:, P * u : P * u + P], ident[:])
+            tiles["tp", g, pair] = tp
 
-        def tr_copy(q, eng):
-            g, c0 = q // 4, 2 * (q % 4)
-            if c0 == 0:
-                tiles["ai", g] = work.tile([P, R, 4], BF16, name="ai", align_bytes=64)
-            dst = tiles["ai", g][:].rearrange("p r j -> p (r j)").bitcast(F32)
-            dst = dst.rearrange("p (c r u) -> p c r u", r=P, u=2)[:, c0 : c0 + 2]
-            src = tiles["tp", q][:].rearrange("p c u r -> p c r u")
-            if eng == "S":
-                nc.scalar.copy(out=dst, in_=src)
-            else:
-                nc.vector.tensor_copy(out=dst, in_=src)
+        def tr_copy(g, pair, eng):
+            if pair % 2 == 0:
+                tiles["ai", g, pair // 2] = work.tile([P, 4, P, 2], F32, name="ai", bufs=4, align_bytes=64)
+            i = 2 * (pair % 2)
+            copy(eng, tiles["ai", g, pair // 2][:, i : i + 2], tiles["tp", g, pair][:].rearrange("p c u r -> p c r u"))
 
-        def quant_a(q, n):
-            g, r0 = q // 4, 256 * (q % 4)
+        def quant_a(g, half):
             nc.vector.quantize_mx(
-                out=acode[:, g, r0 : r0 + 256 * n].bitcast(FP8X4),
-                scales=ascale[:, g, r0 : r0 + 256 * n],
-                in_=tiles["ai", g][:, r0 : r0 + 256 * n, :].rearrange("p r j -> p (r j)"),
+                out=acode[:, g, 512 * half : 512 * half + 512].bitcast(FP8X4),
+                scales=ascale[:, g, 512 * half : 512 * half + 512],
+                in_=tiles["ai", g, half][:].rearrange("p c r u -> p (c r u)").bitcast(BF16),
             )
 
-        def h_pass(c, g):
-            tag = H_TAGS[c]
+        def h_pass(half, pair, g, tag=None):
             if g == 0:
-                tiles["h", c] = psum.tile([P, C], F32, name=tag, bufs=PS.get(tag, 1))
-            nc.tensor.matmul_mx(
-                out=tiles["h", c][:],
-                lhsT=acode[:, g, P * c : P * c + P].bitcast(FP8X4),
-                lhsT_scale=ascale[:, g, P * c : P * c + P],
-                rhs=bcode[:, g, :].bitcast(FP8X4),
-                rhs_scale=bscale[:, g, :],
-                start=(g == 0),
-                stop=(g == GROUPS - 1),
-            )
-
-        def h_out(c, eng):
-            if c == 0:
-                tiles["ho"] = keep.tile([P, RT, C], F32, name="wf", align_bytes=64)
-            ho = tiles["ho"][:, c, :]
-            if eng == "S":
-                nc.scalar.activation(out=ho, in_=tiles["h", c][:], func=COPY, scale=rhos[:, c : c + 1])
-            else:
-                nc.vector.tensor_scalar(
-                    out=ho, in0=tiles["h", c][:], scalar1=rhos[:, c : c + 1], scalar2=None, op0=MULT
+                tiles["h", half, pair] = psum.tile([P, 2, 256], F32, name=tag or "h%d" % pair)
+            for i in range(2):
+                c = 2 * pair + i
+                nc.tensor.matmul_mx(
+                    out=tiles["h", half, pair][:, i, :],
+                    lhsT=acode[:, g, P * c : P * c + P].bitcast(FP8X4),
+                    lhsT_scale=ascale[:, g, P * c : P * c + P],
+                    rhs=bcode[:, g, 256 * half : 256 * half + 256].bitcast(FP8X4),
+                    rhs_scale=bscale[:, g, 256 * half : 256 * half + 256],
+                    start=(g == 0 and i == 0),
+                    stop=(g == GROUPS - 1 and i == 1),
                 )
-            nc.sync.dma_start(out=out_view[:, c, :], in_=ho)
+
+        def h_out(half, pair, eng):
+            ho = work.tile([P, 2, 256], F32, name="zr", bufs=9, align_bytes=64)
+            for i in range(2):
+                c = 2 * pair + i
+                src = tiles["h", half, pair][:, i, :]
+                if eng == "S":
+                    nc.scalar.activation(out=ho[:, i, :], in_=src, func=COPY, scale=rhos[:, c : c + 1])
+                else:
+                    nc.vector.tensor_scalar(
+                        out=ho[:, i, :], in0=src, scalar1=rhos[:, c : c + 1], scalar2=None, op0=MULT
+                    )
+            nc.sync.dma_start(out=out_view[:, 2 * pair : 2 * pair + 2, 256 * half : 256 * half + 256], in_=ho[:])
 
         def load_lam():
             nc.sync.dma_start(out=lam_row[0:1, :], in_=lam.rearrange("(o n) -> o n", o=1))
 
-        def spread_lam(i):
-            lp = psum.tile([P, 2, 512], BF16, name="h%d" % i)
+        def spread_lam(i, eng):
+            lp = next_bank([P, 2, 512], BF16)
             for k in range(2):
                 g = 2 * i + k
-                nc.tensor.matmul(out=lp[:, k, :], lhsT=ones[:], rhs=lam_row[:, 512 * g : 512 * g + 512], start=True, stop=True)
-            tiles["lp", i] = lp
+                row = lam_row[:, 512 * g : 512 * g + 512].rearrange("p (q u) -> p u q", u=2)
+                nc.tensor.matmul(out=lp[:, k, :], lhsT=ones[:], rhs=row, start=True, stop=True)
+            copy(eng, lam_ord[:, 1024 * i : 1024 * i + 1024], lp[:].rearrange("p k n -> p (k n)"))
 
-        def order_lam(i, k, eng):
-            g = 2 * i + k
-            dst = lam_ord[:, 512 * g : 512 * g + 512].rearrange("p (u q e) -> p u q e", u=2, e=2)
-            src = tiles["lp", i][:, k, :].rearrange("p (q u e) -> p u q e", u=2, e=2)
-            if eng == "S":
-                nc.scalar.copy(out=dst, in_=src)
-            else:
-                nc.vector.tensor_copy(out=dst, in_=src)
-
-
-        def small_loads():
+        def load_scale():
             nc.scalar.dma_start(out=y_scale[:], in_=y_f_scale.rearrange("(g p t) o -> p g (t o)", g=FP, p=P, t=4))
-            nc.scalar.dma_start(out=lev16[:], in_=level.rearrange("(p c) -> p c", c=RT))
-            nc.scalar.dma_start(out=rho16[:], in_=rho.rearrange("(p c) -> p c", c=RT))
+
+        def load_rows():
+            nc.sync.dma_start(out=lev16[:], in_=level.rearrange("(p c) -> p c", c=RT))
+            nc.sync.dma_start(out=rho16[:], in_=rho.rearrange("(p c) -> p c", c=RT))
 
         def load_pw():
             nc.sync.dma_start(out=pw[:], in_=w_p_words.rearrange("d p n -> p d n"))
-
-        def clear_pws():
-            nc.vector.memset(pws[:].rearrange("p d n -> p (d n)").bitcast(I32), 0)
 
         def load_pws():
             for q in range(4):
@@ -319,328 +298,135 @@ def tile_weighted_hankel_subspace_s11_kernel(
             nc.vector.tensor_copy(out=lev[:], in_=lev16[:])
             nc.vector.tensor_copy(out=rhos[:], in_=rho16[:])
 
+        planes = [(f, t) for f in range(FP) for t in range(4)]
+        last = GROUPS - 1
+
+        def z_part(g, lo, hi, eng):
+            for d in range(DP):
+                m0, m1 = max(lo - P * d, 0), min(hi - P * d, P)
+                if m0 < m1:
+                    ilv_z(g, d, m0, m1, eng)
+
         with tc.manual_schedule():
-            small_loads()
-            load_y(0, 0)
-            widen(0, 0, 0, "S")
-            widen(0, 0, 1, "V")
-            widen(0, 0, 3, "V")
-            load_y(0, 1)
-            widen(0, 0, 2, "S")
-            load_y(1, 0)
-            load_w(0, 2)
-            widen(0, 1, 0, "S")
-            load_w(2, 2)
-            widen(0, 1, 1, "S")
-            load_z(0, 0)
-            w_transpose(1)
-            widen(0, 1, 3, "S")
-            load_w(4, 2)
-            load_y(1, 1)
+            nc.vector.memset(lam_row[:].bitcast(I32), 0)
+            make_identity(nc, ident[:])
+            nc.vector.memset(ones[:], 1.0)
+            nc.vector.memset(pws[:].rearrange("p d n -> p (d n)").bitcast(I32), 0)
+            load_scale()
+            for f in range(FP):
+                load_y(0, f)
             load_lam()
-            load_z(0, 1)
-            w_transpose(0)
-            w_transpose(2)
-            load_w(6, 2)
-            clear_pws()
-            load_z(0, 2)
-            w_transpose(3)
-            widen(0, 1, 2, "V")
-            widen(1, 0, 0, "S")
-            widen(1, 0, 3, "S")
-            load_y(2, 0)
+            load_w(0)
+            load_w(1)
+            load_y(1, 0)
+            load_w(2)
+            load_rows()
+            load_w(3)
+            load_y(1, 1)
+            for d in range(DP):
+                load_z(0, d)
             load_pw()
-            widen(1, 0, 1, "V")
-            widen(1, 0, 2, "S")
-            w_copy(0, "S")
-            ilv_y(0, 0, 0, "V")
-            ilv_y(0, 1, 0, "V")
-            w_copy(1, "S")
-            w_transpose(5)
-            ilv_y(0, 1, 1, "V")
-            ilv_y(0, 0, 1, "V")
             load_pws()
-            ilv_y(1, 0, 0, "V")
-            quant_y(0, 0)
-            load_z(1, 0)
-            ilv_y(1, 0, 1, "V")
-            ilv_z(0, 0, 0, "V")
-            quant_y(0, 1)
-            load_z(1, 1)
-            w_copy(2, "S")
-            quant_y(1, 0)
-            w_copy(3, "S")
-            ilv_z(0, 0, 1, "S")
-            widen(1, 1, 0, "S")
-            w_quant(1, 0, 256)
-            w_copy(5, "S")
-            w_quant(0, 256, 256)
-            w_transpose(4)
-            widen(1, 1, 1, "S")
-            w_quant(0, 0, 256)
-            widen(1, 1, 2, "S")
-            quant_z(0, 0)
+            for f in range(FP):
+                load_y(2, f)
+            for g in (1, 2):
+                for d in range(DP):
+                    load_z(g, d)
+
+            for f, t in planes:
+                widen(0, f, t, "SSVV"[t])
+            for f in range(FP):
+                load_y(3, f)
+            spread_lam(0, "S")
+            for f in range(FP):
+                ilv_y(0, f, f + 1, 0, 512, "V")
+            for c in range(6):
+                if c == 4:
+                    spread_lam(1, "S")
+                w_transpose(c)
+                w_copy(c, "S")
+                if c == 3:
+                    for f in range(FP):
+                        quant_y(0, f)
+                    w_quant(0)
+                    for f, t in planes[:HEAD_S]:
+                        widen(1, f, t, "S")
+            for f, t in planes[HEAD_S:HEAD_V]:
+                widen(1, f, t, "V")
+            w_quant(1)
             widen_small()
-            widen(1, 1, 3, "S")
-            w_quant(1, 256, 256)
-            ilv_z(0, 1, 0, "V")
-            w_copy(4, "S")
-            ilv_y(1, 1, 0, "V")
-            ilv_z(0, 1, 1, "V")
-            w_quant(1, 512, 256)
-            spread_lam(0)
-            order_lam(0, 0, "S")
-            w_quant(0, 512, 256)
-            spread_lam(1)
-            ilv_y(1, 1, 1, "S")
-            order_lam(1, 1, "S")
-            w_transpose(6)
-            w_copy(6, "S")
-            load_y(2, 1)
-            fut(0, 0)
-            w_transpose(7)
-            ilv_z(0, 2, 0, "V")
-            fut(0, 1)
-            load_z(1, 2)
-            a_op(0, 0)
-            a_op(0, 1)
-            load_z(2, 0)
-            fut(0, 2)
-            order_lam(1, 0, "S")
-            ilv_z(0, 2, 1, "S")
-            widen(2, 0, 0, "S")
-            load_y(3, 0)
-            widen(2, 0, 1, "S")
-            widen(2, 0, 2, "S")
-            order_lam(0, 1, "S")
-            quant_z(0, 1)
-            load_z(2, 1)
-            fut(0, 3)
-            load_z(2, 2)
-            a_op(0, 2)
-            a_op(0, 3)
-            quant_z(0, 2)
-            widen(2, 0, 3, "S")
-            quant_y(1, 1)
-            load_y(3, 1)
-            w_copy(7, "S")
-            ilv_y(2, 0, 0, "S")
-            ilv_y(2, 0, 1, "V")
-            w_quant(0, 768, 256)
-            w_quant(1, 768, 256)
-            fut(0, 4)
-            a_op(0, 4)
-            fut(0, 5)
-            past(0, 0)
-            past_copy(0, 0, "S")
-            past(0, 1)
-            a_op(0, 5)
-            fut(0, 6)
-            past_copy(0, 1, "S")
-            ilv_z(1, 0, 0, "S")
-            tr(0)
-            fut(0, 7)
-            ilv_z(1, 0, 1, "V")
-            tr_copy(0, "S")
-            a_op(0, 6)
-            tr_copy(1, "S")
-            ilv_z(1, 1, 0, "V")
-            fut(1, 0)
-            quant_y(2, 0)
-            a_op(0, 7)
-            past(0, 2)
-            widen(2, 1, 0, "S")
-            quant_z(1, 0)
-            past(0, 3)
-            a_op(1, 0)
-            ilv_z(1, 1, 1, "S")
-            quant_a(0, 2)
-            widen(2, 1, 2, "S")
-            fut(1, 1)
-            past_copy(0, 2, "S")
-            fut(1, 2)
-            load_z(3, 0)
-            ilv_z(1, 2, 0, "V")
-            past_copy(0, 3, "S")
-            ilv_z(2, 0, 0, "S")
-            ilv_z(1, 2, 1, "V")
-            a_op(1, 1)
-            tr(1)
-            tr_copy(2, "S")
-            widen(2, 1, 1, "S")
-            tr_copy(3, "S")
-            load_z(3, 1)
-            quant_z(1, 2)
-            a_op(1, 2)
-            fut(1, 3)
-            widen(2, 1, 3, "S")
-            ilv_z(2, 1, 0, "S")
-            quant_z(1, 1)
-            a_op(1, 3)
-            fut(1, 4)
-            past(1, 0)
-            past(1, 1)
-            past_copy(1, 0, "S")
-            past_copy(1, 1, "S")
-            fut(1, 5)
-            ilv_z(2, 0, 1, "V")
-            load_z(3, 2)
-            quant_past(0)
-            a_op(1, 4)
-            ilv_z(2, 1, 1, "V")
-            ilv_y(2, 1, 0, "V")
-            a_op(1, 5)
-            ilv_z(2, 2, 0, "S")
-            fut(1, 6)
-            tr(2)
-            tr_copy(4, "S")
-            ilv_y(2, 1, 1, "V")
-            tr_copy(5, "S")
-            fut(1, 7)
-            a_op(1, 6)
-            quant_y(2, 1)
-            a_op(1, 7)
-            past(1, 2)
-            fut(2, 0)
-            h_pass(1, 0)
-            past(1, 3)
-            widen(3, 0, 0, "S")
-            widen(3, 1, 0, "S")
-            quant_z(2, 0)
-            widen(3, 0, 3, "S")
-            fut(2, 1)
-            a_op(2, 0)
-            fut(2, 2)
-            widen(3, 1, 1, "S")
-            past_copy(1, 2, "S")
-            past_copy(1, 3, "S")
-            widen(3, 1, 2, "S")
-            widen(3, 0, 2, "S")
-            widen(3, 0, 1, "S")
-            tr(3)
-            ilv_z(2, 2, 1, "V")
-            ilv_z(3, 0, 0, "V")
-            tr_copy(6, "S")
-            a_op(2, 1)
-            h_pass(0, 0)
-            quant_z(2, 2)
-            a_op(2, 2)
-            quant_z(2, 1)
-            fut(2, 3)
-            h_pass(3, 0)
-            quant_a(4, 2)
-            tr_copy(7, "S")
-            quant_a(2, 2)
-            a_op(2, 3)
-            fut(2, 4)
-            a_op(2, 4)
-            past(2, 0)
-            past(2, 1)
-            fut(2, 5)
-            widen(3, 1, 3, "S")
-            ilv_y(3, 0, 0, "S")
-            past_copy(2, 0, "S")
-            fut(2, 6)
-            quant_past(1)
-            ilv_y(3, 1, 0, "V")
-            past_copy(2, 1, "S")
-            tr(4)
-            a_op(2, 5)
-            fut(2, 7)
-            ilv_z(3, 1, 0, "S")
-            h_pass(1, 1)
-            ilv_y(3, 0, 1, "V")
-            tr_copy(8, "S")
-            ilv_y(3, 1, 1, "S")
-            a_op(2, 6)
-            past(2, 2)
-            h_pass(2, 0)
-            h_pass(0, 1)
-            tr_copy(9, "S")
-            ilv_z(3, 0, 1, "S")
-            ilv_z(3, 2, 0, "V")
-            a_op(2, 7)
-            quant_y(3, 0)
-            h_pass(3, 1)
-            quant_y(3, 1)
-            ilv_z(3, 1, 1, "V")
-            quant_z(3, 0)
-            past(2, 3)
-            fut(3, 0)
-            past_copy(2, 2, "S")
-            fut(3, 1)
-            h_pass(2, 1)
-            past_copy(2, 3, "S")
-            ilv_z(3, 2, 1, "S")
-            a_op(3, 0)
-            tr(5)
-            tr_copy(10, "S")
-            a_op(3, 1)
-            fut(3, 2)
-            quant_z(3, 1)
-            fut(3, 3)
-            quant_z(3, 2)
-            tr_copy(11, "S")
-            past(3, 0)
-            past(3, 1)
-            quant_past(2)
-            a_op(3, 2)
-            past_copy(3, 0, "S")
-            a_op(3, 3)
-            quant_a(10, 2)
-            quant_a(6, 2)
-            fut(3, 4)
-            fut(3, 5)
-            a_op(3, 4)
-            quant_a(8, 2)
-            a_op(3, 5)
-            past_copy(3, 1, "S")
-            tr(6)
-            fut(3, 6)
-            tr_copy(12, "V")
-            h_pass(3, 2)
-            tr_copy(13, "S")
-            fut(3, 7)
-            quant_a(12, 2)
-            past(3, 2)
-            a_op(3, 6)
-            past(3, 3)
-            h_pass(0, 2)
-            h_pass(1, 2)
-            h_pass(2, 2)
-            a_op(3, 7)
-            past_copy(3, 3, "S")
-            past_copy(3, 2, "V")
-            h_pass(4, 0)
-            tr(7)
-            h_pass(4, 1)
-            tr_copy(14, "S")
-            quant_past(3)
-            tr_copy(15, "V")
-            h_pass(0, 3)
-            h_out(0, "S")
-            h_pass(2, 3)
-            h_out(2, "S")
-            h_pass(1, 3)
-            h_pass(6, 0)
-            h_pass(3, 3)
-            quant_a(14, 2)
-            h_pass(4, 2)
-            h_pass(6, 1)
-            h_pass(6, 2)
-            h_pass(4, 3)
-            h_pass(5, 0)
-            h_pass(5, 1)
-            h_out(1, "V")
-            h_pass(5, 2)
-            h_pass(5, 3)
-            h_pass(6, 3)
-            h_out(3, "V")
-            h_out(4, "V")
-            h_out(5, "S")
-            h_pass(7, 0)
-            h_pass(7, 1)
-            h_pass(7, 2)
-            h_pass(7, 3)
-            h_out(6, "V")
-            h_out(7, "V")
+
+            for g in range(GROUPS):
+                if g < last and Y_G:
+                    ilv_y(g + 1, 0, FP, 0, Y_G, "G")
+                if g > 0:
+                    z_part(g, 0, Z_S[g], "S")
+                for c in range(RT):
+                    fut(g, c)
+                    a_op(g, c)
+                    if g == 0 and c == 1:
+                        for f, t in planes[HEAD_V : HEAD_V + 2]:
+                            widen(1, f, t, "S")
+                        for cw in (6, 7):
+                            w_transpose(cw)
+                            w_copy(cw, "S")
+                        for f, t in planes[HEAD_V + 2 :]:
+                            widen(1, f, t, "S")
+                        z_part(0, 0, Z_S[0], "S")
+                    if g == 0 and c in (1, 3):
+                        w_quant(2 + c // 2)
+                    if g > 0 and c == Q_AT:
+                        quant_past(g - 1, 0, C)
+                for pair in range(4):
+                    if pair == 2 and g > 0:
+                        for hp in range(4):
+                            h_pass(0, hp, g - 1)
+                    tr(g, pair)
+                    tr_copy(g, pair, "S")
+                z_part(g, Z_S[g], Z_LATE[g], "V")
+                for d in range(DP):
+                    quant_z(g, d)
+                if g == last:
+                    break
+                if g == 0:
+                    for d in range(DP):
+                        load_z(last, d)
+                if Y_G < 512:
+                    ilv_y(g + 1, 0, FP, Y_G, 512, "V")
+                quant_a(g, 0)
+                for f in range(FP):
+                    quant_y(g + 1, f)
+                quant_a(g, 1)
+                z_part(g + 1, Z_LATE[g + 1], DP * P, "V")
+                later = planes if g + 2 < GROUPS else []
+                for f, t in later[:W_FIRST]:
+                    widen(g + 2, f, t, "S")
+                for cc in range(4):
+                    past(g, cc, next_bank([P, 4, 128], F32))
+                    past_copy(g, cc, "S")
+                    for f, t in later[W_FIRST + cc : W_FIRST + 1 + cc]:
+                        widen(g + 2, f, t, "S")
+                for f, t in later[W_FIRST + 4 :]:
+                    widen(g + 2, f, t, "S")
+
+            for half in range(2):
+                quant_a(last, half)
+            for pair in range(2):
+                for g in range(last):
+                    h_pass(1, pair, g, turns[pair - 4])
+            for cc in range(4):
+                past(last, cc, psum.tile([P, 4, 128], F32, name=turns[cc % 2 - 2]))
+                past_copy(last, cc, "SV"[cc % 2])
+                if cc % 2:
+                    quant_past(last, 128 * (cc - 1), 128 * (cc + 1))
+            for pair in range(4):
+                h_pass(0, pair, last)
+                h_out(0, pair, "SV"[pair % 2])
+            for g in range(last):
+                h_pass(1, 2, g, turns[-2])
+            for pair in range(4):
+                if pair == 3:
+                    for g in range(last):
+                        h_pass(1, 3, g, turns[-1])
+                h_pass(1, pair, last)
+                h_out(1, pair, "SV"[pair % 2])

@@ -24,13 +24,16 @@ FP = F // 512
 DP = D // 512
 RT = R // P
 OPEN = 4
-Y_G = 0
-Z_S = (256, 240, 224, 256)
+Z_S = (192, 240, 224, 384)
 Z_LATE = (384, 240, 224, 384)
-HEAD_V = 6
+HEAD_S = 2
+HEAD_V = 4
 Q_AT = 1
 W_FIRST = 3
-HEAD_S = 2
+Z0_AT = 1
+Z_EARLY = 128
+Q_LAST = 1
+H_LAST = 2
 
 
 def tile_weighted_hankel_subspace_s11_kernel(
@@ -79,9 +82,10 @@ def tile_weighted_hankel_subspace_s11_kernel(
             else:
                 nc.vector.tensor_copy(out=dst, in_=src)
 
-        def load_y(g, f):
+        def load_y(g, f, step=4):
             yb = work.tile([P, 4, 512], U8, name="yb", bufs=6, align_bytes=64)
-            nc.sync.dma_start(out=yb[:], in_=y_view[f][:, :, 512 * g : 512 * g + 512])
+            for t in range(0, 4, step):
+                nc.sync.dma_start(out=yb[:, t : t + step], in_=y_view[f][:, t : t + step, 512 * g : 512 * g + 512])
             tiles["yb", g, f] = yb
 
         def load_z(g, d):
@@ -253,12 +257,12 @@ def tile_weighted_hankel_subspace_s11_kernel(
                     stop=(g == GROUPS - 1 and i == 1),
                 )
 
-        def h_out(half, pair, eng):
+        def h_out(half, pair, engs):
             ho = work.tile([P, 2, 256], F32, name="zr", bufs=9, align_bytes=64)
             for i in range(2):
                 c = 2 * pair + i
                 src = tiles["h", half, pair][:, i, :]
-                if eng == "S":
+                if engs[i] == "S":
                     nc.scalar.activation(out=ho[:, i, :], in_=src, func=COPY, scale=rhos[:, c : c + 1])
                 else:
                     nc.vector.tensor_scalar(
@@ -313,8 +317,8 @@ def tile_weighted_hankel_subspace_s11_kernel(
             nc.vector.memset(ones[:], 1.0)
             nc.vector.memset(pws[:].rearrange("p d n -> p (d n)").bitcast(I32), 0)
             load_scale()
-            for f in range(FP):
-                load_y(0, f)
+            load_y(0, 0, 2)
+            load_y(0, 1)
             load_lam()
             load_w(0)
             load_w(1)
@@ -334,7 +338,7 @@ def tile_weighted_hankel_subspace_s11_kernel(
                     load_z(g, d)
 
             for f, t in planes:
-                widen(0, f, t, "SSVV"[t])
+                widen(0, f, t, "SVSV"[t])
             for f in range(FP):
                 load_y(3, f)
             spread_lam(0, "S")
@@ -357,10 +361,8 @@ def tile_weighted_hankel_subspace_s11_kernel(
             widen_small()
 
             for g in range(GROUPS):
-                if g < last and Y_G:
-                    ilv_y(g + 1, 0, FP, 0, Y_G, "G")
                 if g > 0:
-                    z_part(g, 0, Z_S[g], "S")
+                    z_part(g, Z_EARLY if g == last else 0, Z_S[g], "S")
                 for c in range(RT):
                     fut(g, c)
                     a_op(g, c)
@@ -372,18 +374,21 @@ def tile_weighted_hankel_subspace_s11_kernel(
                             w_copy(cw, "S")
                         for f, t in planes[HEAD_V + 2 :]:
                             widen(1, f, t, "S")
-                        z_part(0, 0, Z_S[0], "S")
+                        z_part(0, P, P + Z_S[0], "S")
                     if g == 0 and c in (1, 3):
                         w_quant(2 + c // 2)
-                    if g > 0 and c == Q_AT:
+                    if g == 0 and c == Z0_AT:
+                        ilv_z(0, 0, 0, P, "V")
+                    if 0 < g and c == (Q_AT if g < last else Q_LAST):
                         quant_past(g - 1, 0, C)
-                for pair in range(4):
-                    if pair == 2 and g > 0:
+                for pair in range(5):
+                    if pair == (2 if g < last else H_LAST) and g > 0:
                         for hp in range(4):
                             h_pass(0, hp, g - 1)
-                    tr(g, pair)
-                    tr_copy(g, pair, "S")
-                z_part(g, Z_S[g], Z_LATE[g], "V")
+                    if pair < 4:
+                        tr(g, pair)
+                        tr_copy(g, pair, "S")
+                z_part(g, Z_S[g] + (P if g == 0 else 0), Z_LATE[g], "V")
                 for d in range(DP):
                     quant_z(g, d)
                 if g == last:
@@ -391,8 +396,7 @@ def tile_weighted_hankel_subspace_s11_kernel(
                 if g == 0:
                     for d in range(DP):
                         load_z(last, d)
-                if Y_G < 512:
-                    ilv_y(g + 1, 0, FP, Y_G, 512, "V")
+                ilv_y(g + 1, 0, FP, 0, 512, "V")
                 quant_a(g, 0)
                 for f in range(FP):
                     quant_y(g + 1, f)
@@ -403,30 +407,42 @@ def tile_weighted_hankel_subspace_s11_kernel(
                     widen(g + 2, f, t, "S")
                 for cc in range(4):
                     past(g, cc, next_bank([P, 4, 128], F32))
+                    if g + 1 == last:
+                        z_part(last, cc * Z_EARLY // 4, (cc + 1) * Z_EARLY // 4, "S")
                     past_copy(g, cc, "S")
                     for f, t in later[W_FIRST + cc : W_FIRST + 1 + cc]:
                         widen(g + 2, f, t, "S")
                 for f, t in later[W_FIRST + 4 :]:
                     widen(g + 2, f, t, "S")
 
-            for half in range(2):
-                quant_a(last, half)
-            for pair in range(2):
-                for g in range(last):
-                    h_pass(1, pair, g, turns[pair - 4])
-            for cc in range(4):
-                past(last, cc, psum.tile([P, 4, 128], F32, name=turns[cc % 2 - 2]))
+            quant_a(last, 0)
+            quant_a(last, 1)
+            late_banks = (turns[-4], turns[-3], turns[-2], turns[-1])
+
+            def last_bank(cc):
+                past(last, cc, psum.tile([P, 4, 128], F32, name=late_banks[cc % 2]))
                 past_copy(last, cc, "SV"[cc % 2])
                 if cc % 2:
                     quant_past(last, 128 * (cc - 1), 128 * (cc + 1))
-            for pair in range(4):
-                h_pass(0, pair, last)
-                h_out(0, pair, "SV"[pair % 2])
-            for g in range(last):
-                h_pass(1, 2, g, turns[-2])
-            for pair in range(4):
-                if pair == 3:
-                    for g in range(last):
-                        h_pass(1, 3, g, turns[-1])
-                h_pass(1, pair, last)
-                h_out(1, pair, "SV"[pair % 2])
+
+            def catch_up(pair):
+                for g in range(last):
+                    h_pass(1, pair, g, late_banks[(pair + 2) % 4])
+
+            def finish(half, pair):
+                h_pass(half, pair, last)
+                h_out(half, pair, "VSSVSVSV"[4 * half + pair] * 2)
+
+            last_bank(0)
+            last_bank(1)
+            catch_up(0)
+            for cc in (2, 3):
+                last_bank(cc)
+                finish(0, 2 * cc - 4)
+                finish(0, 2 * cc - 3)
+            catch_up(1)
+            finish(1, 0)
+            for pair in range(1, 4):
+                if pair > 1:
+                    catch_up(pair)
+                finish(1, pair)

@@ -134,8 +134,8 @@ def tile_weighted_hankel_subspace_s11_kernel(
         def ilv_z(g, d, m0, m1, eng):
             if ("zi", g, d) not in tiles:
                 tiles["zi", g, d] = work.tile([P, 4, 128, 4], BF16, name="zi", bufs=6, align_bytes=64)
-            dst = tiles["zi", g, d][:].rearrange("p s m j -> p m j s")[:, m0:m1]
-            src = tiles["zr", g, d][:].rearrange("p j (m s) -> p m j s", s=4)[:, m0:m1]
+            dst = tiles["zi", g, d][:].rearrange("p s (m e) j -> p m j e s", e=2)[:, m0 // 2 : m1 // 2]
+            src = tiles["zr", g, d][:].rearrange("p j (m e s) -> p m j e s", e=2, s=4)[:, m0 // 2 : m1 // 2]
             copy(eng, dst, src)
 
         def quant_z(g, d):
@@ -242,33 +242,31 @@ def tile_weighted_hankel_subspace_s11_kernel(
                 in_=tiles["ai", g, half][:].rearrange("p c r u -> p (c r u)").bitcast(BF16),
             )
 
-        def h_pass(half, pair, g, tag=None):
+        def h_pass(half, cs, g, tag=None):
             if g == 0:
-                tiles["h", half, pair] = psum.tile([P, 2, 256], F32, name=tag or "h%d" % pair)
-            for i in range(2):
-                c = 2 * pair + i
+                tiles["h", half, cs] = psum.tile([P, len(cs), 256], F32, name=tag or "h%d" % (cs[0] // 2))
+            for i, c in enumerate(cs):
                 nc.tensor.matmul_mx(
-                    out=tiles["h", half, pair][:, i, :],
+                    out=tiles["h", half, cs][:, i, :],
                     lhsT=acode[:, g, P * c : P * c + P].bitcast(FP8X4),
                     lhsT_scale=ascale[:, g, P * c : P * c + P],
                     rhs=bcode[:, g, 256 * half : 256 * half + 256].bitcast(FP8X4),
                     rhs_scale=bscale[:, g, 256 * half : 256 * half + 256],
                     start=(g == 0 and i == 0),
-                    stop=(g == GROUPS - 1 and i == 1),
+                    stop=(g == GROUPS - 1 and i == len(cs) - 1),
                 )
 
-        def h_out(half, pair, engs):
-            ho = work.tile([P, 2, 256], F32, name="zr", bufs=9, align_bytes=64)
-            for i in range(2):
-                c = 2 * pair + i
-                src = tiles["h", half, pair][:, i, :]
-                if engs[i] == "S":
+        def h_out(half, cs, eng):
+            ho = work.tile([P, len(cs), 256], F32, name="zr", bufs=9, align_bytes=64)
+            for i, c in enumerate(cs):
+                src = tiles["h", half, cs][:, i, :]
+                if eng == "S":
                     nc.scalar.activation(out=ho[:, i, :], in_=src, func=COPY, scale=rhos[:, c : c + 1])
                 else:
                     nc.vector.tensor_scalar(
                         out=ho[:, i, :], in0=src, scalar1=rhos[:, c : c + 1], scalar2=None, op0=MULT
                     )
-            nc.sync.dma_start(out=out_view[:, 2 * pair : 2 * pair + 2, 256 * half : 256 * half + 256], in_=ho[:])
+            nc.sync.dma_start(out=out_view[:, cs[0] : cs[-1] + 1, 256 * half : 256 * half + 256], in_=ho[:])
 
         def load_lam():
             nc.sync.dma_start(out=lam_row[0:1, :], in_=lam.rearrange("(o n) -> o n", o=1))
@@ -304,6 +302,7 @@ def tile_weighted_hankel_subspace_s11_kernel(
 
         planes = [(f, t) for f in range(FP) for t in range(4)]
         last = GROUPS - 1
+        pairs = [(c, c + 1) for c in range(0, RT, 2)]
 
         def z_part(g, lo, hi, eng):
             for d in range(DP):
@@ -337,15 +336,17 @@ def tile_weighted_hankel_subspace_s11_kernel(
                 for d in range(DP):
                     load_z(g, d)
 
-            for f, t in planes:
-                widen(0, f, t, "SVSV"[t])
+            for t in range(4):
+                widen(0, 0, t, "SVVV"[t])
+            ilv_y(0, 0, 1, 0, 512, "V")
+            for t in range(4):
+                widen(0, 1, t, "SSVV"[t])
             for f in range(FP):
                 load_y(3, f)
             spread_lam(0, "S")
-            for f in range(FP):
-                ilv_y(0, f, f + 1, 0, 512, "V")
+            ilv_y(0, 1, 2, 0, 512, "V")
             for c in range(6):
-                if c == 4:
+                if c == 2:
                     spread_lam(1, "S")
                 w_transpose(c)
                 w_copy(c, "S")
@@ -383,8 +384,8 @@ def tile_weighted_hankel_subspace_s11_kernel(
                         quant_past(g - 1, 0, C)
                 for pair in range(5):
                     if pair == (2 if g < last else H_LAST) and g > 0:
-                        for hp in range(4):
-                            h_pass(0, hp, g - 1)
+                        for cs in pairs:
+                            h_pass(0, cs, g - 1)
                     if pair < 4:
                         tr(g, pair)
                         tr_copy(g, pair, "S")
@@ -417,32 +418,34 @@ def tile_weighted_hankel_subspace_s11_kernel(
 
             quant_a(last, 0)
             quant_a(last, 1)
-            late_banks = (turns[-4], turns[-3], turns[-2], turns[-1])
+            free = (turns[-4], turns[-3], turns[-2], turns[-1])
 
             def last_bank(cc):
-                past(last, cc, psum.tile([P, 4, 128], F32, name=late_banks[cc % 2]))
+                past(last, cc, psum.tile([P, 4, 128], F32, name=free[cc % 2]))
                 past_copy(last, cc, "SV"[cc % 2])
                 if cc % 2:
                     quant_past(last, 128 * (cc - 1), 128 * (cc + 1))
 
-            def catch_up(pair):
+            def catch_up(cs, tag):
                 for g in range(last):
-                    h_pass(1, pair, g, late_banks[(pair + 2) % 4])
+                    h_pass(1, cs, g, tag)
 
-            def finish(half, pair):
-                h_pass(half, pair, last)
-                h_out(half, pair, "VSSVSVSV"[4 * half + pair] * 2)
+            def finish(half, cs, eng):
+                h_pass(half, cs, last)
+                h_out(half, cs, eng)
 
             last_bank(0)
             last_bank(1)
-            catch_up(0)
+            catch_up(pairs[0], free[2])
             for cc in (2, 3):
                 last_bank(cc)
-                finish(0, 2 * cc - 4)
-                finish(0, 2 * cc - 3)
-            catch_up(1)
-            finish(1, 0)
-            for pair in range(1, 4):
-                if pair > 1:
-                    catch_up(pair)
-                finish(1, pair)
+                finish(0, pairs[2 * cc - 4], "VS"[cc % 2])
+                finish(0, pairs[2 * cc - 3], "SV"[cc % 2])
+            catch_up(pairs[1], free[3])
+            finish(1, pairs[0], "S")
+            finish(1, pairs[1], "V")
+            catch_up(pairs[2], free[0])
+            finish(1, pairs[2], "S")
+            for i, c in enumerate(pairs[3]):
+                catch_up((c,), (free[1], "h0")[i])
+                finish(1, (c,), "VS"[i])

@@ -24,8 +24,8 @@ FP = F // 512
 DP = D // 512
 RT = R // P
 OPEN = 4
-Z_S = (192, 240, 224, 384)
-Z_LATE = (384, 240, 224, 384)
+Z_S = (176, 208, 176, 384)
+Z_LATE = (384, 208, 176, 384)
 HEAD_S = 2
 HEAD_V = 4
 Q_AT = 1
@@ -34,6 +34,9 @@ Z0_AT = 1
 Z_EARLY = 128
 Q_LAST = 1
 H_LAST = 2
+W3_AT = 1
+Y_G = (224, 224, 0)
+W_F = (7, 3, 3)
 
 
 def tile_weighted_hankel_subspace_s11_kernel(
@@ -89,7 +92,7 @@ def tile_weighted_hankel_subspace_s11_kernel(
             tiles["yb", g, f] = yb
 
         def load_z(g, d):
-            zr = work.tile([P, 4, 512], BF16, name="zr", bufs=9, align_bytes=64)
+            zr = work.tile([P, 4, 512], BF16, name="zr", bufs=8, align_bytes=64)
             nc.sync.dma_start(out=zr[:], in_=z_view[d][:, :, 512 * g : 512 * g + 512])
             tiles["zr", g, d] = zr
 
@@ -121,31 +124,31 @@ def tile_weighted_hankel_subspace_s11_kernel(
             else:
                 copy(eng, dst.rearrange("p f (c i) t -> p f c t i", i=4), src.rearrange("p f t (c i) -> p f c t i", i=4))
 
-        def quant_y(g, f):
-            if f == 0:
+        def quant_y(g, f0, f1):
+            if f0 == 0:
                 tiles["yc", g] = work.tile([P, FP, 512], U32, name="yc", align_bytes=64)
                 tiles["ys", g] = work.tile([P, FP, 512], U8, name="ys", align_bytes=64)
             nc.vector.quantize_mx(
-                out=tiles["yc", g][:, f, :].bitcast(FP8X4),
-                scales=tiles["ys", g][:, f, :],
-                in_=tiles["yi", g][:, f].rearrange("p n t -> p (n t)"),
+                out=tiles["yc", g][:, f0:f1].rearrange("p f n -> p (f n)").bitcast(FP8X4),
+                scales=tiles["ys", g][:, f0:f1].rearrange("p f n -> p (f n)"),
+                in_=tiles["yi", g][:, f0:f1].rearrange("p f n t -> p (f n t)"),
             )
 
         def ilv_z(g, d, m0, m1, eng):
-            if ("zi", g, d) not in tiles:
-                tiles["zi", g, d] = work.tile([P, 4, 128, 4], BF16, name="zi", bufs=6, align_bytes=64)
-            dst = tiles["zi", g, d][:].rearrange("p s (m e) j -> p m j e s", e=2)[:, m0 // 2 : m1 // 2]
+            if ("zi", g) not in tiles:
+                tiles["zi", g] = work.tile([P, DP, 4, 128, 4], BF16, name="zi", align_bytes=64)
+            dst = tiles["zi", g][:, d].rearrange("p s (m e) j -> p m j e s", e=2)[:, m0 // 2 : m1 // 2]
             src = tiles["zr", g, d][:].rearrange("p j (m e s) -> p m j e s", e=2, s=4)[:, m0 // 2 : m1 // 2]
             copy(eng, dst, src)
 
-        def quant_z(g, d):
-            if d == 0:
+        def quant_z(g, d0, d1):
+            if ("zc", g) not in tiles:
                 tiles["zc", g] = work.tile([P, DP, 512], U32, name="zc", align_bytes=64)
                 tiles["zs", g] = work.tile([P, DP, 512], U8, name="zs", align_bytes=64)
             nc.vector.quantize_mx(
-                out=tiles["zc", g][:, d, :].bitcast(FP8X4),
-                scales=tiles["zs", g][:, d, :],
-                in_=tiles["zi", g, d][:].rearrange("p s m j -> p (s m j)"),
+                out=tiles["zc", g][:, d0:d1].rearrange("p d n -> p (d n)").bitcast(FP8X4),
+                scales=tiles["zs", g][:, d0:d1].rearrange("p d n -> p (d n)"),
+                in_=tiles["zi", g][:, d0:d1].rearrange("p d s m j -> p (d s m j)"),
             )
 
         def w_transpose(c):
@@ -158,7 +161,10 @@ def tile_weighted_hankel_subspace_s11_kernel(
 
         def w_copy(c, eng):
             if c % 2 == 0:
-                tiles["wi", c // 2] = work.tile([P, 2, FP, P, 2], F32, name="ai", bufs=4, align_bytes=64)
+                if c == RT - 2:
+                    tiles["wi", c // 2] = work.tile([P, 2, FP, P, 2], F32, name="yi", bufs=1, align_bytes=64)
+                else:
+                    tiles["wi", c // 2] = work.tile([P, 2, FP, P, 2], F32, name="wi", align_bytes=64)
             copy(eng, tiles["wi", c // 2][:, c % 2], tiles["wt", c][:].rearrange("p f u r -> p f r u"))
 
         def w_quant(pair):
@@ -184,7 +190,10 @@ def tile_weighted_hankel_subspace_s11_kernel(
 
         def past_copy(g, cc, eng):
             if cc == 0:
-                tiles["pi", g] = work.tile([P, 512, 4], BF16, name="pi", align_bytes=64)
+                if g == 0:
+                    tiles["pi", g] = work.tile([P, 512, 4], BF16, name="yi", bufs=1, align_bytes=64)
+                else:
+                    tiles["pi", g] = work.tile([P, 512, 4], BF16, name="pi", align_bytes=64)
             dst = tiles["pi", g][:, 128 * cc : 128 * cc + 128, :]
             copy(eng, dst, tiles["pp", g, cc][:].rearrange("p s n -> p n s"))
 
@@ -230,16 +239,16 @@ def tile_weighted_hankel_subspace_s11_kernel(
             tiles["tp", g, pair] = tp
 
         def tr_copy(g, pair, eng):
-            if pair % 2 == 0:
-                tiles["ai", g, pair // 2] = work.tile([P, 4, P, 2], F32, name="ai", bufs=4, align_bytes=64)
-            i = 2 * (pair % 2)
-            copy(eng, tiles["ai", g, pair // 2][:, i : i + 2], tiles["tp", g, pair][:].rearrange("p c u r -> p c r u"))
+            if pair == 0:
+                tiles["ai", g] = work.tile([P, RT, P, 2], F32, name="ai", align_bytes=64)
+            dst = tiles["ai", g][:, 2 * pair : 2 * pair + 2]
+            copy(eng, dst, tiles["tp", g, pair][:].rearrange("p c u r -> p c r u"))
 
-        def quant_a(g, half):
+        def quant_a(g, c0, c1):
             nc.vector.quantize_mx(
-                out=acode[:, g, 512 * half : 512 * half + 512].bitcast(FP8X4),
-                scales=ascale[:, g, 512 * half : 512 * half + 512],
-                in_=tiles["ai", g, half][:].rearrange("p c r u -> p (c r u)").bitcast(BF16),
+                out=acode[:, g, P * c0 : P * c1].bitcast(FP8X4),
+                scales=ascale[:, g, P * c0 : P * c1],
+                in_=tiles["ai", g][:, c0:c1].rearrange("p c r u -> p (c r u)").bitcast(BF16),
             )
 
         def h_pass(half, cs, g, tag=None):
@@ -257,7 +266,7 @@ def tile_weighted_hankel_subspace_s11_kernel(
                 )
 
         def h_out(half, cs, eng):
-            ho = work.tile([P, len(cs), 256], F32, name="zr", bufs=9, align_bytes=64)
+            ho = work.tile([P, len(cs), 256], F32, name="zr", bufs=8, align_bytes=64)
             for i, c in enumerate(cs):
                 src = tiles["h", half, cs][:, i, :]
                 if eng == "S":
@@ -332,9 +341,8 @@ def tile_weighted_hankel_subspace_s11_kernel(
             load_pws()
             for f in range(FP):
                 load_y(2, f)
-            for g in (1, 2):
-                for d in range(DP):
-                    load_z(g, d)
+            for gz, d in [(1, 0), (1, 1), (1, 2), (2, 0), (2, 1)]:
+                load_z(gz, d)
 
             for t in range(4):
                 widen(0, 0, t, "SVVV"[t])
@@ -352,7 +360,7 @@ def tile_weighted_hankel_subspace_s11_kernel(
                 w_copy(c, "S")
                 if c == 3:
                     for f in range(FP):
-                        quant_y(0, f)
+                        quant_y(0, f, f + 1)
                     w_quant(0)
                     for f, t in planes[:HEAD_S]:
                         widen(1, f, t, "S")
@@ -376,12 +384,15 @@ def tile_weighted_hankel_subspace_s11_kernel(
                         for f, t in planes[HEAD_V + 2 :]:
                             widen(1, f, t, "S")
                         z_part(0, P, P + Z_S[0], "S")
-                    if g == 0 and c in (1, 3):
-                        w_quant(2 + c // 2)
-                    if g == 0 and c == Z0_AT:
+                    if g == 0 and c == 1:
+                        w_quant(2)
                         ilv_z(0, 0, 0, P, "V")
-                    if 0 < g and c == (Q_AT if g < last else Q_LAST):
+                    if g == 0 and c == W3_AT:
+                        w_quant(3)
+                    if g > 0 and c == Q_AT:
                         quant_past(g - 1, 0, C)
+                    if (g, c) in ((0, W3_AT), (1, Q_AT)):
+                        ilv_y(g + 1, 0, FP, 0, Y_G[g], "G")
                 for pair in range(5):
                     if pair == (2 if g < last else H_LAST) and g > 0:
                         for cs in pairs:
@@ -390,20 +401,31 @@ def tile_weighted_hankel_subspace_s11_kernel(
                         tr(g, pair)
                         tr_copy(g, pair, "S")
                 z_part(g, Z_S[g] + (P if g == 0 else 0), Z_LATE[g], "V")
-                for d in range(DP):
-                    quant_z(g, d)
+                if 0 < g < last:
+                    quant_z(g, 2, DP)
+                quant_z(g, 0, 2)
+                if g in (0, last):
+                    quant_z(g, 2, DP)
                 if g == last:
                     break
                 if g == 0:
-                    for d in range(DP):
+                    load_z(2, 2)
+                    for d in range(2):
                         load_z(last, d)
-                ilv_y(g + 1, 0, FP, 0, 512, "V")
-                quant_a(g, 0)
-                for f in range(FP):
-                    quant_y(g + 1, f)
-                quant_a(g, 1)
+                if g == 1:
+                    load_z(last, 2)
+                ilv_y(g + 1, 0, FP, Y_G[g], 512, "V")
+                first = RT if g == 1 else RT // 2
+                quant_a(g, 0, first)
+                if first == RT:
+                    quant_y(g + 1, 0, FP)
+                else:
+                    for f in range(FP):
+                        quant_y(g + 1, f, f + 1)
+                    quant_a(g, first, RT)
                 z_part(g + 1, Z_LATE[g + 1], DP * P, "V")
                 later = planes if g + 2 < GROUPS else []
+                W_FIRST = W_F[g]
                 for f, t in later[:W_FIRST]:
                     widen(g + 2, f, t, "S")
                 for cc in range(4):
@@ -416,8 +438,8 @@ def tile_weighted_hankel_subspace_s11_kernel(
                 for f, t in later[W_FIRST + 4 :]:
                     widen(g + 2, f, t, "S")
 
-            quant_a(last, 0)
-            quant_a(last, 1)
+            quant_a(last, 0, RT // 2)
+            quant_a(last, RT // 2, RT)
             free = (turns[-4], turns[-3], turns[-2], turns[-1])
 
             def last_bank(cc):

@@ -24,19 +24,18 @@ FP = F // 512
 DP = D // 512
 RT = R // P
 OPEN = 4
-Z_S = (176, 208, 176, 384)
-Z_LATE = (384, 208, 176, 384)
-HEAD_S = 2
-HEAD_V = 4
-Q_AT = 1
-W_FIRST = 3
-Z0_AT = 1
-Z_EARLY = 128
-Q_LAST = 1
-H_LAST = 2
-W3_AT = 1
-Y_G = (224, 224, 0)
-W_F = (7, 3, 3)
+AHEAD = (5, 4, 4, 4)
+AI = 4
+HEAD_W = "VVVV"
+Y_G = (0, 112, 320, 384)
+Z0_S = (0, 0, 0, 224, 384)
+Z_S = (0, 256, 96, 192)
+Z_LEAD = 64
+T_AT = 3
+AT = 13
+QA = (0, 0, 0, 0)
+Z_G = 128
+Y1_S = 256
 
 
 def tile_weighted_hankel_subspace_s11_kernel(
@@ -75,7 +74,7 @@ def tile_weighted_hankel_subspace_s11_kernel(
         turns = []
 
         def next_bank(shape, dtype):
-            tag = "turn%d" % (len(turns) % 4)
+            tag = "bank%d" % (len(turns) % 8)
             turns.append(tag)
             return psum.tile(shape, dtype, name=tag)
 
@@ -97,7 +96,7 @@ def tile_weighted_hankel_subspace_s11_kernel(
             tiles["zr", g, d] = zr
 
         def load_w(pair):
-            wf = work.tile([P, 2, F], BF16, name="wf", bufs=4, align_bytes=64)
+            wf = work.tile([P, 2, F], BF16, name="zr", bufs=8, align_bytes=64)
             nc.sync.dma_start(out=wf[:], in_=w_view[:, 2 * pair : 2 * pair + 2, :])
             tiles["wf", pair] = wf
 
@@ -125,7 +124,7 @@ def tile_weighted_hankel_subspace_s11_kernel(
                 copy(eng, dst.rearrange("p f (c i) t -> p f c t i", i=4), src.rearrange("p f t (c i) -> p f c t i", i=4))
 
         def quant_y(g, f0, f1):
-            if f0 == 0:
+            if ("yc", g) not in tiles:
                 tiles["yc", g] = work.tile([P, FP, 512], U32, name="yc", align_bytes=64)
                 tiles["ys", g] = work.tile([P, FP, 512], U8, name="ys", align_bytes=64)
             nc.vector.quantize_mx(
@@ -135,11 +134,29 @@ def tile_weighted_hankel_subspace_s11_kernel(
             )
 
         def ilv_z(g, d, m0, m1, eng):
-            if ("zi", g) not in tiles:
-                tiles["zi", g] = work.tile([P, DP, 4, 128, 4], BF16, name="zi", align_bytes=64)
-            dst = tiles["zi", g][:, d].rearrange("p s (m e) j -> p m j e s", e=2)[:, m0 // 2 : m1 // 2]
-            src = tiles["zr", g, d][:].rearrange("p j (m e s) -> p m j e s", e=2, s=4)[:, m0 // 2 : m1 // 2]
-            copy(eng, dst, src)
+            if ("zi", g, d // 2) not in tiles:
+                if (g, d // 2) == (1, 0):
+                    zi = work.tile([P, 2, 4, 128, 4], BF16, name="yi", bufs=1, align_bytes=64)
+                elif d < 2:
+                    zi = work.tile([P, 2, 4, 128, 4], BF16, name="zi", align_bytes=64)
+                else:
+                    zi = work.tile([P, 1, 4, 128, 4], BF16, name="zi_last", align_bytes=64)
+                tiles["zi", g, d // 2] = zi
+            dst = tiles["zi", g, d // 2][:, d % 2]
+            src = tiles["zr", g, d][:]
+            if eng == "G":
+                nc.gpsimd.tensor_scalar(
+                    out=dst[:, :, m0:m1],
+                    in0=src.rearrange("p j (m s) -> p s m j", s=4)[:, :, m0:m1],
+                    scalar1=1.0,
+                    scalar2=0.0,
+                    op0=MULT,
+                    op1=ADD,
+                )
+            else:
+                dst = dst.rearrange("p s (m e) j -> p m j e s", e=2)[:, m0 // 2 : m1 // 2]
+                src = src.rearrange("p j (m e s) -> p m j e s", e=2, s=4)[:, m0 // 2 : m1 // 2]
+                copy(eng, dst, src)
 
         def quant_z(g, d0, d1):
             if ("zc", g) not in tiles:
@@ -148,11 +165,11 @@ def tile_weighted_hankel_subspace_s11_kernel(
             nc.vector.quantize_mx(
                 out=tiles["zc", g][:, d0:d1].rearrange("p d n -> p (d n)").bitcast(FP8X4),
                 scales=tiles["zs", g][:, d0:d1].rearrange("p d n -> p (d n)"),
-                in_=tiles["zi", g][:, d0:d1].rearrange("p d s m j -> p (d s m j)"),
+                in_=tiles["zi", g, d0 // 2][:].rearrange("p d s m j -> p (d s m j)"),
             )
 
         def w_transpose(c):
-            wt = psum.tile([P, FP, 2, P], F32, name="h%d" % c) if c < OPEN else next_bank([P, FP, 2, P], F32)
+            wt = next_bank([P, FP, 2, P], F32)
             words = tiles["wf", c // 2][:, c % 2, :].bitcast(F32)
             for f in range(FP):
                 for u in range(2):
@@ -190,10 +207,7 @@ def tile_weighted_hankel_subspace_s11_kernel(
 
         def past_copy(g, cc, eng):
             if cc == 0:
-                if g == 0:
-                    tiles["pi", g] = work.tile([P, 512, 4], BF16, name="yi", bufs=1, align_bytes=64)
-                else:
-                    tiles["pi", g] = work.tile([P, 512, 4], BF16, name="pi", align_bytes=64)
+                tiles["pi", g] = work.tile([P, 512, 4], BF16, name="pi", align_bytes=64)
             dst = tiles["pi", g][:, 128 * cc : 128 * cc + 128, :]
             copy(eng, dst, tiles["pp", g, cc][:].rearrange("p s n -> p n s"))
 
@@ -219,7 +233,7 @@ def tile_weighted_hankel_subspace_s11_kernel(
             tiles["fp", g, c] = fp
 
         def a_op(g, c):
-            at = work.tile([P, 512], BF16, name="at", bufs=RT, align_bytes=64)
+            at = work.tile([P, 512], BF16, name="at", bufs=AT, align_bytes=64)
             nc.vector.scalar_tensor_tensor(
                 out=at[:].rearrange("p (u q) -> p u q", u=2),
                 in0=tiles["fp", g, c][:].rearrange("p (q u) -> p u q", u=2),
@@ -240,7 +254,7 @@ def tile_weighted_hankel_subspace_s11_kernel(
 
         def tr_copy(g, pair, eng):
             if pair == 0:
-                tiles["ai", g] = work.tile([P, RT, P, 2], F32, name="ai", align_bytes=64)
+                tiles["ai", g] = work.tile([P, RT, P, 2], F32, name="ai", bufs=AI, align_bytes=64)
             dst = tiles["ai", g][:, 2 * pair : 2 * pair + 2]
             copy(eng, dst, tiles["tp", g, pair][:].rearrange("p c u r -> p c r u"))
 
@@ -253,7 +267,7 @@ def tile_weighted_hankel_subspace_s11_kernel(
 
         def h_pass(half, cs, g, tag=None):
             if g == 0:
-                tiles["h", half, cs] = psum.tile([P, len(cs), 256], F32, name=tag or "h%d" % (cs[0] // 2))
+                tiles["h", half, cs] = psum.tile([P, len(cs), 256], F32, name=tag)
             for i, c in enumerate(cs):
                 nc.tensor.matmul_mx(
                     out=tiles["h", half, cs][:, i, :],
@@ -312,6 +326,7 @@ def tile_weighted_hankel_subspace_s11_kernel(
         planes = [(f, t) for f in range(FP) for t in range(4)]
         last = GROUPS - 1
         pairs = [(c, c + 1) for c in range(0, RT, 2)]
+        z_rows = DP * P
 
         def z_part(g, lo, hi, eng):
             for d in range(DP):
@@ -335,14 +350,10 @@ def tile_weighted_hankel_subspace_s11_kernel(
             load_rows()
             load_w(3)
             load_y(1, 1)
-            for d in range(DP):
-                load_z(0, d)
-            load_pw()
-            load_pws()
             for f in range(FP):
                 load_y(2, f)
-            for gz, d in [(1, 0), (1, 1), (1, 2), (2, 0), (2, 1)]:
-                load_z(gz, d)
+            for d in range(DP):
+                load_z(0, d)
 
             for t in range(4):
                 widen(0, 0, t, "SVVV"[t])
@@ -351,6 +362,9 @@ def tile_weighted_hankel_subspace_s11_kernel(
                 widen(0, 1, t, "SSVV"[t])
             for f in range(FP):
                 load_y(3, f)
+            load_pw()
+            load_pws()
+            load_z(1, 0)
             spread_lam(0, "S")
             ilv_y(0, 1, 2, 0, 512, "V")
             for c in range(6):
@@ -362,112 +376,142 @@ def tile_weighted_hankel_subspace_s11_kernel(
                     for f in range(FP):
                         quant_y(0, f, f + 1)
                     w_quant(0)
-                    for f, t in planes[:HEAD_S]:
-                        widen(1, f, t, "S")
-            for f, t in planes[HEAD_S:HEAD_V]:
-                widen(1, f, t, "V")
+                    for t in range(4):
+                        widen(1, 0, t, "SSVV"[t])
             w_quant(1)
             widen_small()
 
             for g in range(GROUPS):
-                if g > 0:
-                    z_part(g, Z_EARLY if g == last else 0, Z_S[g], "S")
                 for c in range(RT):
+                    if c == T_AT + 1:
+                        if g + 2 < GROUPS:
+                            for f, t in planes:
+                                widen(g + 2, f, t, "S")
+                        else:
+                            z_part(0, Z0_S[g], Z0_S[g + 1], "S")
+                        if g > 0:
+                            for pair in range(4):
+                                tr_copy(g - 1, pair, "S")
                     fut(g, c)
-                    a_op(g, c)
+                    if c < AHEAD[g]:
+                        a_op(g, c)
                     if g == 0 and c == 1:
-                        for f, t in planes[HEAD_V : HEAD_V + 2]:
-                            widen(1, f, t, "S")
                         for cw in (6, 7):
                             w_transpose(cw)
                             w_copy(cw, "S")
-                        for f, t in planes[HEAD_V + 2 :]:
-                            widen(1, f, t, "S")
-                        z_part(0, P, P + Z_S[0], "S")
-                    if g == 0 and c == 1:
                         w_quant(2)
-                        ilv_z(0, 0, 0, P, "V")
-                    if g == 0 and c == W3_AT:
+                        for t in range(4):
+                            widen(1, 1, t, HEAD_W[t])
                         w_quant(3)
-                    if g > 0 and c == Q_AT:
-                        quant_past(g - 1, 0, C)
-                    if (g, c) in ((0, W3_AT), (1, Q_AT)):
-                        ilv_y(g + 1, 0, FP, 0, Y_G[g], "G")
-                for pair in range(5):
-                    if pair == (2 if g < last else H_LAST) and g > 0:
-                        for cs in pairs:
-                            h_pass(0, cs, g - 1)
-                    if pair < 4:
-                        tr(g, pair)
-                        tr_copy(g, pair, "S")
-                z_part(g, Z_S[g] + (P if g == 0 else 0), Z_LATE[g], "V")
-                if 0 < g < last:
-                    quant_z(g, 2, DP)
-                quant_z(g, 0, 2)
-                if g in (0, last):
-                    quant_z(g, 2, DP)
-                if g == last:
-                    break
+                        ilv_y(1, 0, FP, 0, Y_G[1], "G")
+                        ilv_y(1, 0, 1, Y_G[1], Y1_S, "S")
+                    if g > 0 and c == T_AT:
+                        for pair in range(4):
+                            tr(g - 1, pair)
                 if g == 0:
-                    load_z(2, 2)
-                    for d in range(2):
-                        load_z(last, d)
-                if g == 1:
-                    load_z(last, 2)
-                ilv_y(g + 1, 0, FP, Y_G[g], 512, "V")
-                first = RT if g == 1 else RT // 2
-                quant_a(g, 0, first)
-                if first == RT:
-                    quant_y(g + 1, 0, FP)
+                    for gz, d in ((1, 1), (1, 2), (2, 0), (2, 1)):
+                        load_z(gz, d)
+                if g < last:
+                    if g == 0:
+                        ilv_y(1, 1, FP, Y_G[1], 512, "V")
+                        if Y1_S < 512:
+                            ilv_y(1, 0, 1, Y1_S, 512, "V")
+                        for f in (1, 0):
+                            quant_y(1, f, f + 1)
+                    else:
+                        if g == 1:
+                            ilv_y(2, 0, FP, Y_G[2], 512, "V")
+                        else:
+                            z_part(0, Z0_S[-1], z_rows, "V")
+                        quant_y(g + 1, 0, FP)
+                        if g == 2:
+                            z_part(1, 0, Z_G, "G")
+                    if g + 2 < GROUPS:
+                        ilv_y(g + 2, 0, FP, 0, Y_G[g + 2], "G")
+                    if g == 1:
+                        ilv_y(3, 0, FP, Y_G[3], 512, "S")
                 else:
-                    for f in range(FP):
-                        quant_y(g + 1, f, f + 1)
-                    quant_a(g, first, RT)
-                z_part(g + 1, Z_LATE[g + 1], DP * P, "V")
-                later = planes if g + 2 < GROUPS else []
-                W_FIRST = W_F[g]
-                for f, t in later[:W_FIRST]:
-                    widen(g + 2, f, t, "S")
+                    if QA[1]:
+                        quant_a(1, 0, QA[1])
+                    quant_z(0, 0, 2)
+                    quant_z(0, 2, DP)
+                for c in range(AHEAD[g], RT):
+                    a_op(g, c)
+            load_z(2, 2)
+            for d in range(2):
+                load_z(last, d)
+            z_part(1, Z_G, Z_S[1], "S")
+            for cc in range(4):
+                if cc == 2:
+                    for pair in range(4):
+                        tr(last, pair)
+                        tr_copy(last, pair, "S")
+                past(0, cc, next_bank([P, 4, 128], F32))
+                past_copy(0, cc, "S")
+
+            n = len(turns)
+            b_banks = ["bank%d" % ((n + i) % 8) for i in range(2)]
+            out_banks = ["bank%d" % ((n + 2 + i) % 8) for i in range(6)]
+            open_banks = [(half, cs) for half in range(2) for cs in pairs][:6]
+
+            def b_bank(g, cc, eng):
+                past(g, cc, psum.tile([P, 4, 128], F32, name=b_banks[cc % 2]))
+                past_copy(g, cc, eng)
+
+            z_part(1, Z_S[1], z_rows, "V")
+            quant_z(1, 0, 2)
+            quant_z(1, 2, DP)
+            quant_a(0, 0, RT)
+            load_z(last, 2)
+            for g in range(1, last):
+                share = Z_S[g + 1]
+                z_part(g + 1, 2 * P, 2 * P + Z_LEAD, "V")
+                quant_past(g - 1, 0, C)
+                z_part(g + 1, 2 * P + Z_LEAD, z_rows, "V")
+                z_part(g + 1, share, 2 * P, "V")
                 for cc in range(4):
-                    past(g, cc, next_bank([P, 4, 128], F32))
-                    if g + 1 == last:
-                        z_part(last, cc * Z_EARLY // 4, (cc + 1) * Z_EARLY // 4, "S")
-                    past_copy(g, cc, "S")
-                    for f, t in later[W_FIRST + cc : W_FIRST + 1 + cc]:
-                        widen(g + 2, f, t, "S")
-                for f, t in later[W_FIRST + 4 :]:
-                    widen(g + 2, f, t, "S")
-
-            quant_a(last, 0, RT // 2)
-            quant_a(last, RT // 2, RT)
-            free = (turns[-4], turns[-3], turns[-2], turns[-1])
-
-            def last_bank(cc):
-                past(last, cc, psum.tile([P, 4, 128], F32, name=free[cc % 2]))
-                past_copy(last, cc, "SV"[cc % 2])
-                if cc % 2:
-                    quant_past(last, 128 * (cc - 1), 128 * (cc + 1))
-
-            def catch_up(cs, tag):
-                for g in range(last):
-                    h_pass(1, cs, g, tag)
+                    if g == 1 and cc < 2:
+                        z_part(2, cc * share // 2, (cc + 1) * share // 2, "S")
+                    if g == 2 and cc < 2:
+                        z_part(3, (cc + 2) * share // 4, (cc + 3) * share // 4, "S")
+                    if g == 1 and cc >= 2:
+                        z_part(3, (cc - 2) * Z_S[3] // 4, (cc - 1) * Z_S[3] // 4, "S")
+                    b_bank(g, cc, "S")
+                    if cc > 0:
+                        for i in (2 * cc - 2, 2 * cc - 1):
+                            h_pass(open_banks[i][0], open_banks[i][1], g - 1, out_banks[i])
+                quant_z(g + 1, 2, DP)
+                quant_z(g + 1, 0, 2)
+                quant_a(g, 0, RT)
 
             def finish(half, cs, eng):
                 h_pass(half, cs, last)
                 h_out(half, cs, eng)
 
-            last_bank(0)
-            last_bank(1)
-            catch_up(pairs[0], free[2])
-            for cc in (2, 3):
-                last_bank(cc)
-                finish(0, pairs[2 * cc - 4], "VS"[cc % 2])
-                finish(0, pairs[2 * cc - 3], "SV"[cc % 2])
-            catch_up(pairs[1], free[3])
+            def catch_up(cs, tag):
+                for g in range(last):
+                    h_pass(1, cs, g, tag)
+
+            quant_past(last - 1, 0, C)
+            quant_a(last, 0, RT)
+            b_bank(last, 0, "SV"[0 % 2])
+            b_bank(last, 1, "SV"[1 % 2])
+            quant_past(last, 0, 256)
+            for half, cs in open_banks[0:4]:
+                h_pass(half, cs, last - 1)
+            b_bank(last, 2, "SV"[2 % 2])
+            finish(0, pairs[0], "V")
+            finish(0, pairs[1], "S")
+            b_bank(last, 3, "SV"[3 % 2])
+            quant_past(last, 256, 512)
+            finish(0, pairs[2], "S")
+            finish(0, pairs[3], "V")
+            for half, cs in open_banks[4:6]:
+                h_pass(half, cs, last - 1)
             finish(1, pairs[0], "S")
             finish(1, pairs[1], "V")
-            catch_up(pairs[2], free[0])
+            catch_up(pairs[2], b_banks[0])
             finish(1, pairs[2], "S")
             for i, c in enumerate(pairs[3]):
-                catch_up((c,), (free[1], "h0")[i])
+                catch_up((c,), (b_banks[1], out_banks[0])[i])
                 finish(1, (c,), "VS"[i])

@@ -24,18 +24,20 @@ FP = F // 512
 DP = D // 512
 RT = R // P
 OPEN = 4
-AHEAD = (5, 4, 4, 4)
+AHEAD = (2, 4, 4, 4)
 AI = 4
 HEAD_W = "VVVV"
-Y_G = (0, 112, 320, 384)
-Z0_S = (0, 0, 0, 224, 384)
-Z_S = (0, 256, 96, 192)
+Y_G = (0, 0, 440, 352)
+Z0_S = (0, 0, 0, 256, 384)
+Z_S = (0, 224, 96, 192)
 Z_LEAD = 64
 T_AT = 3
 AT = 13
 QA = (0, 0, 0, 0)
-Z_G = 128
+Z_G = 96
 Y1_S = 256
+WI = 2
+EARLY = 2
 
 
 def tile_weighted_hankel_subspace_s11_kernel(
@@ -178,10 +180,7 @@ def tile_weighted_hankel_subspace_s11_kernel(
 
         def w_copy(c, eng):
             if c % 2 == 0:
-                if c == RT - 2:
-                    tiles["wi", c // 2] = work.tile([P, 2, FP, P, 2], F32, name="yi", bufs=1, align_bytes=64)
-                else:
-                    tiles["wi", c // 2] = work.tile([P, 2, FP, P, 2], F32, name="wi", align_bytes=64)
+                tiles["wi", c // 2] = work.tile([P, 2, FP, P, 2], F32, name="wi", bufs=WI, align_bytes=64)
             copy(eng, tiles["wi", c // 2][:, c % 2], tiles["wt", c][:].rearrange("p f u r -> p f r u"))
 
         def w_quant(pair):
@@ -380,12 +379,13 @@ def tile_weighted_hankel_subspace_s11_kernel(
                         widen(1, 0, t, "SSVV"[t])
             w_quant(1)
             widen_small()
+            ilv_y(1, 0, 1, 0, 512, "V")
 
             for g in range(GROUPS):
                 for c in range(RT):
                     if c == T_AT + 1:
                         if g + 2 < GROUPS:
-                            for f, t in planes:
+                            for f, t in planes[EARLY if g == 0 else 0 :]:
                                 widen(g + 2, f, t, "S")
                         else:
                             z_part(0, Z0_S[g], Z0_S[g + 1], "S")
@@ -396,6 +396,8 @@ def tile_weighted_hankel_subspace_s11_kernel(
                     if c < AHEAD[g]:
                         a_op(g, c)
                     if g == 0 and c == 1:
+                        for f, t in planes[:EARLY]:
+                            widen(2, f, t, "S")
                         for cw in (6, 7):
                             w_transpose(cw)
                             w_copy(cw, "S")
@@ -403,8 +405,6 @@ def tile_weighted_hankel_subspace_s11_kernel(
                         for t in range(4):
                             widen(1, 1, t, HEAD_W[t])
                         w_quant(3)
-                        ilv_y(1, 0, FP, 0, Y_G[1], "G")
-                        ilv_y(1, 0, 1, Y_G[1], Y1_S, "S")
                     if g > 0 and c == T_AT:
                         for pair in range(4):
                             tr(g - 1, pair)
@@ -413,10 +413,8 @@ def tile_weighted_hankel_subspace_s11_kernel(
                         load_z(gz, d)
                 if g < last:
                     if g == 0:
-                        ilv_y(1, 1, FP, Y_G[1], 512, "V")
-                        if Y1_S < 512:
-                            ilv_y(1, 0, 1, Y1_S, 512, "V")
-                        for f in (1, 0):
+                        ilv_y(1, 1, FP, 0, 512, "V")
+                        for f in range(FP):
                             quant_y(1, f, f + 1)
                     else:
                         if g == 1:

@@ -23,21 +23,11 @@ GROUPS = T // 512
 FP = F // 512
 DP = D // 512
 RT = R // P
-OPEN = 4
-AHEAD = (2, 4, 4, 4)
 AI = 4
-HEAD_W = "VVVV"
-Y_G = (0, 0, 440, 352)
-Z0_S = (0, 0, 0, 256, 384)
-Z_S = (0, 224, 96, 192)
-Z_LEAD = 64
-T_AT = 3
 AT = 13
-QA = (0, 0, 0, 0)
-Z_G = 96
-Y1_S = 256
 WI = 2
-EARLY = 2
+G_ROWS = 20
+Z_STEP = 48
 
 
 def tile_weighted_hankel_subspace_s11_kernel(
@@ -73,12 +63,9 @@ def tile_weighted_hankel_subspace_s11_kernel(
         out_view = out.rearrange("(p c) n -> p c n", c=RT)
 
         tiles = {}
-        turns = []
 
-        def next_bank(shape, dtype):
-            tag = "bank%d" % (len(turns) % 8)
-            turns.append(tag)
-            return psum.tile(shape, dtype, name=tag)
+        def bank_tile(bank, shape, dtype):
+            return psum.tile(shape, dtype, name="bank%d" % bank)
 
         def copy(eng, dst, src):
             if eng == "S":
@@ -113,17 +100,17 @@ def tile_weighted_hankel_subspace_s11_kernel(
             else:
                 nc.vector.tensor_scalar(out=dst, in0=src, scalar1=s, scalar2=None, op0=MULT)
 
-        def ilv_y(g, f0, f1, n0, n1, eng):
+        def ilv_y(g, n0, n1, eng):
             if ("yi", g) not in tiles:
-                tiles["yi", g] = work.tile([P, FP, 512, 4], BF16, name="yi", bufs=1, align_bytes=64)
-            dst = tiles["yi", g][:, f0:f1, n0:n1]
-            src = tiles["yw", g][:, f0:f1, :, n0:n1]
+                tiles["yi", g] = work.tile([P, FP * 512, 4], BF16, name="yi", bufs=1, align_bytes=64)
+            dst = tiles["yi", g][:, n0:n1]
+            src = tiles["yw", g][:, n0 // 512, :, n0 % 512 : (n1 - 1) % 512 + 1]
             if eng == "G":
                 nc.gpsimd.tensor_scalar(
-                    out=dst, in0=src.rearrange("p f t n -> p f n t"), scalar1=1.0, scalar2=0.0, op0=MULT, op1=ADD
+                    out=dst, in0=src.rearrange("p t n -> p n t"), scalar1=1.0, scalar2=0.0, op0=MULT, op1=ADD
                 )
             else:
-                copy(eng, dst.rearrange("p f (c i) t -> p f c t i", i=4), src.rearrange("p f t (c i) -> p f c t i", i=4))
+                copy(eng, dst.rearrange("p (c i) t -> p c t i", i=4), src.rearrange("p t (c i) -> p c t i", i=4))
 
         def quant_y(g, f0, f1):
             if ("yc", g) not in tiles:
@@ -132,19 +119,16 @@ def tile_weighted_hankel_subspace_s11_kernel(
             nc.vector.quantize_mx(
                 out=tiles["yc", g][:, f0:f1].rearrange("p f n -> p (f n)").bitcast(FP8X4),
                 scales=tiles["ys", g][:, f0:f1].rearrange("p f n -> p (f n)"),
-                in_=tiles["yi", g][:, f0:f1].rearrange("p f n t -> p (f n t)"),
+                in_=tiles["yi", g][:, 512 * f0 : 512 * f1].rearrange("p n t -> p (n t)"),
             )
 
         def ilv_z(g, d, m0, m1, eng):
-            if ("zi", g, d // 2) not in tiles:
-                if (g, d // 2) == (1, 0):
-                    zi = work.tile([P, 2, 4, 128, 4], BF16, name="yi", bufs=1, align_bytes=64)
-                elif d < 2:
-                    zi = work.tile([P, 2, 4, 128, 4], BF16, name="zi", align_bytes=64)
+            if ("zi", g, d) not in tiles:
+                if g < 2 and d == 0:
+                    tiles["zi", g, d] = work.tile([P, 4, 128, 4], BF16, name="yi", bufs=1, align_bytes=64)
                 else:
-                    zi = work.tile([P, 1, 4, 128, 4], BF16, name="zi_last", align_bytes=64)
-                tiles["zi", g, d // 2] = zi
-            dst = tiles["zi", g, d // 2][:, d % 2]
+                    tiles["zi", g, d] = work.tile([P, 4, 128, 4], BF16, name="zi", bufs=6, align_bytes=64)
+            dst = tiles["zi", g, d][:]
             src = tiles["zr", g, d][:]
             if eng == "G":
                 nc.gpsimd.tensor_scalar(
@@ -160,18 +144,18 @@ def tile_weighted_hankel_subspace_s11_kernel(
                 src = src.rearrange("p j (m e s) -> p m j e s", e=2, s=4)[:, m0 // 2 : m1 // 2]
                 copy(eng, dst, src)
 
-        def quant_z(g, d0, d1):
+        def quant_z(g, d):
             if ("zc", g) not in tiles:
                 tiles["zc", g] = work.tile([P, DP, 512], U32, name="zc", align_bytes=64)
                 tiles["zs", g] = work.tile([P, DP, 512], U8, name="zs", align_bytes=64)
             nc.vector.quantize_mx(
-                out=tiles["zc", g][:, d0:d1].rearrange("p d n -> p (d n)").bitcast(FP8X4),
-                scales=tiles["zs", g][:, d0:d1].rearrange("p d n -> p (d n)"),
-                in_=tiles["zi", g, d0 // 2][:].rearrange("p d s m j -> p (d s m j)"),
+                out=tiles["zc", g][:, d].bitcast(FP8X4),
+                scales=tiles["zs", g][:, d],
+                in_=tiles["zi", g, d][:].rearrange("p s m j -> p (s m j)"),
             )
 
-        def w_transpose(c):
-            wt = next_bank([P, FP, 2, P], F32)
+        def w_transpose(c, bank):
+            wt = bank_tile(bank, [P, FP, 2, P], F32)
             words = tiles["wf", c // 2][:, c % 2, :].bitcast(F32)
             for f in range(FP):
                 for u in range(2):
@@ -179,7 +163,7 @@ def tile_weighted_hankel_subspace_s11_kernel(
             tiles["wt", c] = wt
 
         def w_copy(c, eng):
-            if c % 2 == 0:
+            if ("wi", c // 2) not in tiles:
                 tiles["wi", c // 2] = work.tile([P, 2, FP, P, 2], F32, name="wi", bufs=WI, align_bytes=64)
             copy(eng, tiles["wi", c // 2][:, c % 2], tiles["wt", c][:].rearrange("p f u r -> p f r u"))
 
@@ -190,7 +174,8 @@ def tile_weighted_hankel_subspace_s11_kernel(
                 in_=tiles["wi", pair][:].rearrange("p c f r u -> p (c f r u)").bitcast(BF16),
             )
 
-        def past(g, cc, pp):
+        def past(g, cc, bank):
+            pp = bank_tile(bank, [P, 4, 128], F32)
             for s in range(4):
                 for d in range(DP):
                     nc.tensor.matmul_mx(
@@ -205,7 +190,7 @@ def tile_weighted_hankel_subspace_s11_kernel(
             tiles["pp", g, cc] = pp
 
         def past_copy(g, cc, eng):
-            if cc == 0:
+            if ("pi", g) not in tiles:
                 tiles["pi", g] = work.tile([P, 512, 4], BF16, name="pi", align_bytes=64)
             dst = tiles["pi", g][:, 128 * cc : 128 * cc + 128, :]
             copy(eng, dst, tiles["pp", g, cc][:].rearrange("p s n -> p n s"))
@@ -217,8 +202,8 @@ def tile_weighted_hankel_subspace_s11_kernel(
                 in_=tiles["pi", g][:, n0:n1, :].rearrange("p n s -> p (n s)"),
             )
 
-        def fut(g, c):
-            fp = next_bank([P, 512], F32)
+        def fut(g, c, bank):
+            fp = bank_tile(bank, [P, 512], F32)
             for f in range(FP):
                 nc.tensor.matmul_mx(
                     out=fp[:],
@@ -243,8 +228,8 @@ def tile_weighted_hankel_subspace_s11_kernel(
             )
             tiles["at", g, c] = at
 
-        def tr(g, pair):
-            tp = next_bank([P, 2, 2, P], F32)
+        def tr(g, pair, bank):
+            tp = bank_tile(bank, [P, 2, 2, P], F32)
             for i in range(2):
                 words = tiles["at", g, 2 * pair + i][:].bitcast(F32)
                 for u in range(2):
@@ -252,7 +237,7 @@ def tile_weighted_hankel_subspace_s11_kernel(
             tiles["tp", g, pair] = tp
 
         def tr_copy(g, pair, eng):
-            if pair == 0:
+            if ("ai", g) not in tiles:
                 tiles["ai", g] = work.tile([P, RT, P, 2], F32, name="ai", bufs=AI, align_bytes=64)
             dst = tiles["ai", g][:, 2 * pair : 2 * pair + 2]
             copy(eng, dst, tiles["tp", g, pair][:].rearrange("p c u r -> p c r u"))
@@ -264,9 +249,9 @@ def tile_weighted_hankel_subspace_s11_kernel(
                 in_=tiles["ai", g][:, c0:c1].rearrange("p c r u -> p (c r u)").bitcast(BF16),
             )
 
-        def h_pass(half, cs, g, tag=None):
+        def h_pass(half, cs, g, bank=None):
             if g == 0:
-                tiles["h", half, cs] = psum.tile([P, len(cs), 256], F32, name=tag)
+                tiles["h", half, cs] = bank_tile(bank, [P, len(cs), 256], F32)
             for i, c in enumerate(cs):
                 nc.tensor.matmul_mx(
                     out=tiles["h", half, cs][:, i, :],
@@ -288,18 +273,25 @@ def tile_weighted_hankel_subspace_s11_kernel(
                     nc.vector.tensor_scalar(
                         out=ho[:, i, :], in0=src, scalar1=rhos[:, c : c + 1], scalar2=None, op0=MULT
                     )
-            nc.sync.dma_start(out=out_view[:, cs[0] : cs[-1] + 1, 256 * half : 256 * half + 256], in_=ho[:])
+            tiles["ho", half, cs] = ho
+
+        def store(half, cs):
+            dst = out_view[:, cs[0] : cs[-1] + 1, 256 * half : 256 * half + 256]
+            nc.sync.dma_start(out=dst, in_=tiles["ho", half, cs][:])
 
         def load_lam():
             nc.sync.dma_start(out=lam_row[0:1, :], in_=lam.rearrange("(o n) -> o n", o=1))
 
-        def spread_lam(i, eng):
-            lp = next_bank([P, 2, 512], BF16)
+        def spread_lam(i, bank):
+            lp = bank_tile(bank, [P, 2, 512], BF16)
             for k in range(2):
                 g = 2 * i + k
                 row = lam_row[:, 512 * g : 512 * g + 512].rearrange("p (q u) -> p u q", u=2)
                 nc.tensor.matmul(out=lp[:, k, :], lhsT=ones[:], rhs=row, start=True, stop=True)
-            copy(eng, lam_ord[:, 1024 * i : 1024 * i + 1024], lp[:].rearrange("p k n -> p (k n)"))
+            tiles["lp", i] = lp
+
+        def lam_copy(i, eng):
+            copy(eng, lam_ord[:, 1024 * i : 1024 * i + 1024], tiles["lp", i][:].rearrange("p k n -> p (k n)"))
 
         def load_scale():
             nc.scalar.dma_start(out=y_scale[:], in_=y_f_scale.rearrange("(g p t) o -> p g (t o)", g=FP, p=P, t=4))
@@ -322,16 +314,36 @@ def tile_weighted_hankel_subspace_s11_kernel(
             nc.vector.tensor_copy(out=lev[:], in_=lev16[:])
             nc.vector.tensor_copy(out=rhos[:], in_=rho16[:])
 
-        planes = [(f, t) for f in range(FP) for t in range(4)]
         last = GROUPS - 1
         pairs = [(c, c + 1) for c in range(0, RT, 2)]
+        half_rt = RT // 2
+        y_cols = FP * 512
         z_rows = DP * P
 
-        def z_part(g, lo, hi, eng):
+        def ilv_z_rows(g, lo, hi, eng):
             for d in range(DP):
                 m0, m1 = max(lo - P * d, 0), min(hi - P * d, P)
                 if m0 < m1:
                     ilv_z(g, d, m0, m1, eng)
+
+        def ilv_z_scalar(g, lo, hi, extra):
+            if lo < extra:
+                ilv_z(g, 1, lo, min(hi, extra), "S")
+            if hi > extra:
+                ilv_z(g, 0, max(lo, extra) - extra, hi - extra, "S")
+
+        def widen_planes(g, f, engs, first=0):
+            for i, eng in enumerate(engs):
+                widen(g, f, first + i, eng)
+
+        def w_tile(c):
+            w_transpose(c, 3 + (c + 1) % 4)
+            w_copy(c, "S")
+
+        def finish(half, cs, eng):
+            h_pass(half, cs, last)
+            h_out(half, cs, eng)
+            store(half, cs)
 
         with tc.manual_schedule():
             nc.vector.memset(lam_row[:].bitcast(I32), 0)
@@ -341,175 +353,175 @@ def tile_weighted_hankel_subspace_s11_kernel(
             load_scale()
             load_y(0, 0, 2)
             load_y(0, 1)
+            load_y(1, 0)
             load_lam()
             load_w(0)
             load_w(1)
-            load_y(1, 0)
+            load_y(1, 1)
             load_w(2)
             load_rows()
             load_w(3)
-            load_y(1, 1)
             for f in range(FP):
                 load_y(2, f)
-            for d in range(DP):
-                load_z(0, d)
 
-            for t in range(4):
-                widen(0, 0, t, "SVVV"[t])
-            ilv_y(0, 0, 1, 0, 512, "V")
-            for t in range(4):
-                widen(0, 1, t, "SSVV"[t])
+            widen_planes(0, 0, "SVVV")
+            ilv_y(0, 0, 512, "V")
+            widen_planes(0, 1, "SSVV")
+            quant_y(0, 0, 1)
+            ilv_y(0, 512, y_cols, "V")
             for f in range(FP):
                 load_y(3, f)
+            for d in (2, 0, 1):
+                load_z(0, d)
             load_pw()
             load_pws()
             load_z(1, 0)
-            spread_lam(0, "S")
-            ilv_y(0, 1, 2, 0, 512, "V")
-            for c in range(6):
-                if c == 2:
-                    spread_lam(1, "S")
-                w_transpose(c)
-                w_copy(c, "S")
-                if c == 3:
-                    for f in range(FP):
-                        quant_y(0, f, f + 1)
-                    w_quant(0)
-                    for t in range(4):
-                        widen(1, 0, t, "SSVV"[t])
+            widen_planes(1, 0, "SSSS")
+            widen_planes(1, 1, "VV", 2)
+            quant_y(0, 1, 2)
+            spread_lam(0, 0)
+            lam_copy(0, "S")
+            for c in range(4):
+                w_tile(c)
+            spread_lam(1, 7)
+            w_quant(0)
+            ilv_y(1, 0, 512, "V")
+            widen_planes(1, 1, "SS")
             w_quant(1)
             widen_small()
-            ilv_y(1, 0, 1, 0, 512, "V")
+            for c in pairs[2]:
+                w_tile(c)
+            fut(0, 0, 0)
+            ilv_y(1, 512, y_cols, "V")
+            widen_planes(2, 0, "SS")
+            w_quant(2)
+            for c in pairs[3]:
+                w_tile(c)
+            quant_y(1, 0, 1)
+            w_quant(3)
+            quant_y(1, 1, 2)
+            widen_planes(2, 0, "SS", 2)
+            lam_copy(1, "S")
+            ilv_y(2, 0, 512, "G")
+            widen_planes(2, 1, "SSSS")
+            ilv_y(2, 512, y_cols, "G")
+            for c in range(RT):
+                if c > 0:
+                    fut(0, c, c)
+                a_op(0, c)
+            for g, d in ((1, 1), (1, 2), (2, 0), (2, 1)):
+                load_z(g, d)
 
-            for g in range(GROUPS):
-                for c in range(RT):
-                    if c == T_AT + 1:
-                        if g + 2 < GROUPS:
-                            for f, t in planes[EARLY if g == 0 else 0 :]:
-                                widen(g + 2, f, t, "S")
-                        else:
-                            z_part(0, Z0_S[g], Z0_S[g + 1], "S")
-                        if g > 0:
-                            for pair in range(4):
-                                tr_copy(g - 1, pair, "S")
-                    fut(g, c)
-                    if c < AHEAD[g]:
-                        a_op(g, c)
-                    if g == 0 and c == 1:
-                        for f, t in planes[:EARLY]:
-                            widen(2, f, t, "S")
-                        for cw in (6, 7):
-                            w_transpose(cw)
-                            w_copy(cw, "S")
-                        w_quant(2)
-                        for t in range(4):
-                            widen(1, 1, t, HEAD_W[t])
-                        w_quant(3)
-                    if g > 0 and c == T_AT:
-                        for pair in range(4):
-                            tr(g - 1, pair)
-                if g == 0:
-                    for gz, d in ((1, 1), (1, 2), (2, 0), (2, 1)):
-                        load_z(gz, d)
+            g_y = G_ROWS * RT * 4
+            g_z = (G_ROWS * RT, G_ROWS * half_rt)
+            for g in range(1, GROUPS):
+                fut_banks = half_rt * ((g + 1) % 2)
+                tr_banks = half_rt * (g % 2)
+                for c in range(half_rt):
+                    fut(g, c, fut_banks + c)
+                    a_op(g, c)
+                for pair in range(4):
+                    tr(g - 1, pair, tr_banks + pair)
+                if g == 1:
+                    widen_planes(3, 0, "SSSS")
+                    widen_planes(3, 1, "SS")
+                    tr_copy(0, 0, "S")
+                    widen_planes(3, 1, "SS", 2)
+                for pair in range(1 if g == 1 else 0, 4):
+                    tr_copy(g - 1, pair, "S")
+                for c in range(half_rt, RT):
+                    fut(g, c, fut_banks + c - half_rt)
+                if g == 2:
+                    ilv_y(3, (g_y + y_cols) // 2, y_cols, "V")
                 if g < last:
-                    if g == 0:
-                        ilv_y(1, 1, FP, 0, 512, "V")
-                        for f in range(FP):
-                            quant_y(1, f, f + 1)
-                    else:
-                        if g == 1:
-                            ilv_y(2, 0, FP, Y_G[2], 512, "V")
-                        else:
-                            z_part(0, Z0_S[-1], z_rows, "V")
-                        quant_y(g + 1, 0, FP)
-                        if g == 2:
-                            z_part(1, 0, Z_G, "G")
-                    if g + 2 < GROUPS:
-                        ilv_y(g + 2, 0, FP, 0, Y_G[g + 2], "G")
-                    if g == 1:
-                        ilv_y(3, 0, FP, Y_G[3], 512, "S")
+                    for f in range(FP):
+                        quant_y(g + 1, f, f + 1)
                 else:
-                    if QA[1]:
-                        quant_a(1, 0, QA[1])
-                    quant_z(0, 0, 2)
-                    quant_z(0, 2, DP)
-                for c in range(AHEAD[g], RT):
+                    for d in (2, 1, 0):
+                        quant_z(0, d)
+                if g == 1:
+                    ilv_y(3, 0, 512, "G")
+                    ilv_y(3, 512, g_y, "G")
+                    ilv_y(3, g_y, (g_y + y_cols) // 2, "S")
+                    ilv_z_rows(0, 2 * P, z_rows, "S")
+                elif g == 2:
+                    ilv_z_rows(0, g_z[0], 2 * P, "S")
+                    ilv_z_rows(0, 0, g_z[0], "G")
+                    ilv_z_rows(1, P, P + Z_STEP, "S")
+                else:
+                    ilv_z_rows(1, 0, g_z[1], "G")
+                    ilv_z_rows(1, P + Z_STEP, 2 * P, "S")
+                for c in range(half_rt, RT):
                     a_op(g, c)
             load_z(2, 2)
             for d in range(2):
                 load_z(last, d)
-            z_part(1, Z_G, Z_S[1], "S")
-            for cc in range(4):
-                if cc == 2:
-                    for pair in range(4):
-                        tr(last, pair)
-                        tr_copy(last, pair, "S")
-                past(0, cc, next_bank([P, 4, 128], F32))
+
+            b_banks = (4, 5)
+            for cc in range(2):
+                past(0, cc, b_banks[cc])
                 past_copy(0, cc, "S")
-
-            n = len(turns)
-            b_banks = ["bank%d" % ((n + i) % 8) for i in range(2)]
-            out_banks = ["bank%d" % ((n + 2 + i) % 8) for i in range(6)]
-            open_banks = [(half, cs) for half in range(2) for cs in pairs][:6]
-
-            def b_bank(g, cc, eng):
-                past(g, cc, psum.tile([P, 4, 128], F32, name=b_banks[cc % 2]))
-                past_copy(g, cc, eng)
-
-            z_part(1, Z_S[1], z_rows, "V")
-            quant_z(1, 0, 2)
-            quant_z(1, 2, DP)
-            quant_a(0, 0, RT)
+            for pair in range(4):
+                tr(last, pair, pair)
+                tr_copy(last, pair, "S")
+            for cc in range(2, 4):
+                past(0, cc, 4 + cc)
+                past_copy(0, cc, "S")
+            ilv_z_rows(1, 2 * P, z_rows, "V")
+            ilv_z_rows(1, g_z[1], P, "V")
+            for d in (1, 2, 0):
+                quant_z(1, d)
             load_z(last, 2)
+
+            open_sums = [(0, cs) for cs in pairs] + [(1, cs) for cs in pairs[:2]]
+            out_banks = (0, 1, 2, 3, 6, 7)
+            slots = [(2, i) for i in range(3)] + [(3, i) for i in range(4)]
+            z_scalar = {2: 3 * Z_STEP, 3: 4 * Z_STEP}
             for g in range(1, last):
-                share = Z_S[g + 1]
-                z_part(g + 1, 2 * P, 2 * P + Z_LEAD, "V")
+                quant_a(g - 1, 0, RT)
                 quant_past(g - 1, 0, C)
-                z_part(g + 1, 2 * P + Z_LEAD, z_rows, "V")
-                z_part(g + 1, share, 2 * P, "V")
+                ilv_z_rows(g + 1, 2 * P, z_rows, "V")
                 for cc in range(4):
-                    if g == 1 and cc < 2:
-                        z_part(2, cc * share // 2, (cc + 1) * share // 2, "S")
-                    if g == 2 and cc < 2:
-                        z_part(3, (cc + 2) * share // 4, (cc + 3) * share // 4, "S")
-                    if g == 1 and cc >= 2:
-                        z_part(3, (cc - 2) * Z_S[3] // 4, (cc - 1) * Z_S[3] // 4, "S")
-                    b_bank(g, cc, "S")
+                    step = 4 * (g - 1) + cc
+                    if step < len(slots):
+                        gz, i = slots[step]
+                        ilv_z_scalar(gz, Z_STEP * i, Z_STEP * (i + 1), z_scalar[gz] - P)
+                    past(g, cc, b_banks[cc % 2])
+                    past_copy(g, cc, "S")
                     if cc > 0:
                         for i in (2 * cc - 2, 2 * cc - 1):
-                            h_pass(open_banks[i][0], open_banks[i][1], g - 1, out_banks[i])
-                quant_z(g + 1, 2, DP)
-                quant_z(g + 1, 0, 2)
-                quant_a(g, 0, RT)
+                            h_pass(open_sums[i][0], open_sums[i][1], g - 1, out_banks[i])
+                ilv_z_rows(g + 1, z_scalar[g + 1], 2 * P, "V")
+                for d in (2, 1, 0):
+                    quant_z(g + 1, d)
 
-            def finish(half, cs, eng):
-                h_pass(half, cs, last)
-                h_out(half, cs, eng)
-
-            def catch_up(cs, tag):
-                for g in range(last):
-                    h_pass(1, cs, g, tag)
-
+            quant_a(last - 1, 0, RT)
             quant_past(last - 1, 0, C)
             quant_a(last, 0, RT)
-            b_bank(last, 0, "SV"[0 % 2])
-            b_bank(last, 1, "SV"[1 % 2])
+            for cc in range(2):
+                past(last, cc, b_banks[cc])
+                past_copy(last, cc, "S")
             quant_past(last, 0, 256)
-            for half, cs in open_banks[0:4]:
-                h_pass(half, cs, last - 1)
-            b_bank(last, 2, "SV"[2 % 2])
-            finish(0, pairs[0], "V")
-            finish(0, pairs[1], "S")
-            b_bank(last, 3, "SV"[3 % 2])
-            quant_past(last, 256, 512)
-            finish(0, pairs[2], "S")
-            finish(0, pairs[3], "V")
-            for half, cs in open_banks[4:6]:
-                h_pass(half, cs, last - 1)
-            finish(1, pairs[0], "S")
-            finish(1, pairs[1], "V")
-            catch_up(pairs[2], b_banks[0])
-            finish(1, pairs[2], "S")
+            for cs in pairs:
+                h_pass(0, cs, last - 1)
+            past(last, 2, b_banks[0])
+            past_copy(last, 2, "S")
+            for cs in pairs[:2]:
+                finish(0, cs, "V")
+            past(last, 3, b_banks[1])
+            past_copy(last, 3, "S")
+            finish(0, pairs[2], "V")
+            finish(0, pairs[3], "S")
+            quant_past(last, 256, C)
+            for cs in pairs[:2]:
+                h_pass(1, cs, last - 1)
+            for g in range(2):
+                h_pass(1, pairs[2], g, b_banks[0])
+            finish(1, pairs[0], "V")
+            finish(1, pairs[1], "S")
+            h_pass(1, pairs[2], last - 1)
+            finish(1, pairs[2], "V")
             for i, c in enumerate(pairs[3]):
-                catch_up((c,), (b_banks[1], out_banks[0])[i])
-                finish(1, (c,), "VS"[i])
+                for g in range(last):
+                    h_pass(1, (c,), g, i)
+                finish(1, (c,), "SV"[i])

@@ -26,8 +26,9 @@ RT = R // P
 AI = 4
 AT = 13
 WI = 2
-G_ROWS = 20
-Z_STEP = 48
+G_Y = 736
+Z_STEP = 44
+Z1_S = 96
 
 
 def tile_weighted_hankel_subspace_s11_kernel(
@@ -57,12 +58,15 @@ def tile_weighted_hankel_subspace_s11_kernel(
         bcode = keep.tile([P, GROUPS, C], U32, name="bcode", align_bytes=64)
         bscale = keep.tile([P, GROUPS, C], U8, name="bscale", align_bytes=64)
 
+        shared = keep.tile([P, FP * 512 * 4], BF16, name="shared", align_bytes=64)
+
         y_view = y_f_bytes.rearrange("(g p t) n -> g p t n", g=FP, p=P, t=4)
         z_view = z_p.rearrange("(g p t) n -> g p t n", g=DP, p=P, t=4)
         w_view = w_f.rearrange("(p c) f -> p c f", c=RT)
         out_view = out.rearrange("(p c) n -> p c n", c=RT)
 
         tiles = {}
+        last = GROUPS - 1
 
         def bank_tile(bank, shape, dtype):
             return psum.tile(shape, dtype, name="bank%d" % bank)
@@ -89,11 +93,16 @@ def tile_weighted_hankel_subspace_s11_kernel(
             nc.sync.dma_start(out=wf[:], in_=w_view[:, 2 * pair : 2 * pair + 2, :])
             tiles["wf", pair] = wf
 
-        def widen(g, f, t, eng):
+        def widened(g):
             if ("yw", g) not in tiles:
-                tiles["yw", g] = work.tile([P, FP, 4, 512], BF16, name="yw", align_bytes=64)
+                tiles["yw", g] = work.tile([P, FP * 4 * 512], BF16, name="yw", align_bytes=64)
+            if g == last:
+                return tiles["yw", g][:].rearrange("p (t f n) -> p f t n", t=4, f=FP)
+            return tiles["yw", g][:].rearrange("p (f t n) -> p f t n", t=4, f=FP)
+
+        def widen(g, f, t, eng):
             src = tiles["yb", g, f][:, t, :].bitcast(FP8)
-            dst = tiles["yw", g][:, f, t, :]
+            dst = widened(g)[:, f, t, :]
             s = y_scale[:, f, t : t + 1]
             if eng == "S":
                 nc.scalar.activation(out=dst, in_=src, func=COPY, scale=s)
@@ -101,10 +110,11 @@ def tile_weighted_hankel_subspace_s11_kernel(
                 nc.vector.tensor_scalar(out=dst, in0=src, scalar1=s, scalar2=None, op0=MULT)
 
         def ilv_y(g, n0, n1, eng):
-            if ("yi", g) not in tiles:
-                tiles["yi", g] = work.tile([P, FP * 512, 4], BF16, name="yi", bufs=1, align_bytes=64)
-            dst = tiles["yi", g][:, n0:n1]
-            src = tiles["yw", g][:, n0 // 512, :, n0 % 512 : (n1 - 1) % 512 + 1]
+            dst = shared[:, 4 * n0 : 4 * n1].rearrange("p (n t) -> p n t", t=4)
+            if g == last:
+                src = tiles["yw", g][:].rearrange("p (t n) -> p t n", t=4)[:, :, n0:n1]
+            else:
+                src = widened(g)[:, n0 // 512, :, n0 % 512 : (n1 - 1) % 512 + 1]
             if eng == "G":
                 nc.gpsimd.tensor_scalar(
                     out=dst, in0=src.rearrange("p t n -> p n t"), scalar1=1.0, scalar2=0.0, op0=MULT, op1=ADD
@@ -112,28 +122,29 @@ def tile_weighted_hankel_subspace_s11_kernel(
             else:
                 copy(eng, dst.rearrange("p (c i) t -> p c t i", i=4), src.rearrange("p t (c i) -> p c t i", i=4))
 
-        def quant_y(g, f0, f1):
+        def quant_y(g, n0, n1):
             if ("yc", g) not in tiles:
-                tiles["yc", g] = work.tile([P, FP, 512], U32, name="yc", align_bytes=64)
-                tiles["ys", g] = work.tile([P, FP, 512], U8, name="ys", align_bytes=64)
+                tiles["yc", g] = work.tile([P, FP * 512], U32, name="yc", align_bytes=64)
+                tiles["ys", g] = work.tile([P, FP * 512], U8, name="ys", align_bytes=64)
             nc.vector.quantize_mx(
-                out=tiles["yc", g][:, f0:f1].rearrange("p f n -> p (f n)").bitcast(FP8X4),
-                scales=tiles["ys", g][:, f0:f1].rearrange("p f n -> p (f n)"),
-                in_=tiles["yi", g][:, 512 * f0 : 512 * f1].rearrange("p n t -> p (n t)"),
+                out=tiles["yc", g][:, n0:n1].bitcast(FP8X4),
+                scales=tiles["ys", g][:, n0:n1],
+                in_=shared[:, 4 * n0 : 4 * n1],
             )
 
         def ilv_z(g, d, m0, m1, eng):
             if ("zi", g, d) not in tiles:
-                if g < 2 and d == 0:
-                    tiles["zi", g, d] = work.tile([P, 4, 128, 4], BF16, name="yi", bufs=1, align_bytes=64)
+                if eng == "G":
+                    tiles["zi", g, d] = shared[:, 0:2048]
                 else:
-                    tiles["zi", g, d] = work.tile([P, 4, 128, 4], BF16, name="zi", bufs=6, align_bytes=64)
-            dst = tiles["zi", g, d][:]
+                    zi = work.tile([P, 2048], BF16, name="zi", bufs=6, align_bytes=64)
+                    tiles["zi", g, d] = zi[:]
+            dst = tiles["zi", g, d].rearrange("p (s m j) -> p s m j", s=4, j=4)
             src = tiles["zr", g, d][:]
             if eng == "G":
                 nc.gpsimd.tensor_scalar(
-                    out=dst[:, :, m0:m1],
-                    in0=src.rearrange("p j (m s) -> p s m j", s=4)[:, :, m0:m1],
+                    out=dst.rearrange("p s m j -> p m s j")[:, m0:m1],
+                    in0=src.rearrange("p j (m s) -> p m s j", s=4)[:, m0:m1],
                     scalar1=1.0,
                     scalar2=0.0,
                     op0=MULT,
@@ -151,7 +162,7 @@ def tile_weighted_hankel_subspace_s11_kernel(
             nc.vector.quantize_mx(
                 out=tiles["zc", g][:, d].bitcast(FP8X4),
                 scales=tiles["zs", g][:, d],
-                in_=tiles["zi", g, d][:].rearrange("p s m j -> p (s m j)"),
+                in_=tiles["zi", g, d],
             )
 
         def w_transpose(c, bank):
@@ -209,8 +220,8 @@ def tile_weighted_hankel_subspace_s11_kernel(
                     out=fp[:],
                     lhsT=wcode[:, c, f, :].bitcast(FP8X4),
                     lhsT_scale=wscale[:, c, f, :],
-                    rhs=tiles["yc", g][:, f, :].bitcast(FP8X4),
-                    rhs_scale=tiles["ys", g][:, f, :],
+                    rhs=tiles["yc", g][:, 512 * f : 512 * f + 512].bitcast(FP8X4),
+                    rhs_scale=tiles["ys", g][:, 512 * f : 512 * f + 512],
                     start=(f == 0),
                     stop=(f == FP - 1),
                 )
@@ -314,7 +325,6 @@ def tile_weighted_hankel_subspace_s11_kernel(
             nc.vector.tensor_copy(out=lev[:], in_=lev16[:])
             nc.vector.tensor_copy(out=rhos[:], in_=rho16[:])
 
-        last = GROUPS - 1
         pairs = [(c, c + 1) for c in range(0, RT, 2)]
         half_rt = RT // 2
         y_cols = FP * 512
@@ -367,7 +377,7 @@ def tile_weighted_hankel_subspace_s11_kernel(
             widen_planes(0, 0, "SVVV")
             ilv_y(0, 0, 512, "V")
             widen_planes(0, 1, "SSVV")
-            quant_y(0, 0, 1)
+            quant_y(0, 0, 512)
             ilv_y(0, 512, y_cols, "V")
             for f in range(FP):
                 load_y(3, f)
@@ -378,7 +388,7 @@ def tile_weighted_hankel_subspace_s11_kernel(
             load_z(1, 0)
             widen_planes(1, 0, "SSSS")
             widen_planes(1, 1, "VV", 2)
-            quant_y(0, 1, 2)
+            quant_y(0, 512, y_cols)
             spread_lam(0, 0)
             lam_copy(0, "S")
             for c in range(4):
@@ -397,9 +407,9 @@ def tile_weighted_hankel_subspace_s11_kernel(
             w_quant(2)
             for c in pairs[3]:
                 w_tile(c)
-            quant_y(1, 0, 1)
+            quant_y(1, 0, 512)
             w_quant(3)
-            quant_y(1, 1, 2)
+            quant_y(1, 512, y_cols)
             widen_planes(2, 0, "SS", 2)
             lam_copy(1, "S")
             ilv_y(2, 0, 512, "G")
@@ -412,14 +422,14 @@ def tile_weighted_hankel_subspace_s11_kernel(
             for g, d in ((1, 1), (1, 2), (2, 0), (2, 1)):
                 load_z(g, d)
 
-            g_y = G_ROWS * RT * 4
-            g_z = (G_ROWS * RT, G_ROWS * half_rt)
             for g in range(1, GROUPS):
                 fut_banks = half_rt * ((g + 1) % 2)
                 tr_banks = half_rt * (g % 2)
+                ahead = half_rt if g < last else 2
                 for c in range(half_rt):
                     fut(g, c, fut_banks + c)
-                    a_op(g, c)
+                    if c < ahead:
+                        a_op(g, c)
                 for pair in range(4):
                     tr(g - 1, pair, tr_banks + pair)
                 if g == 1:
@@ -430,62 +440,62 @@ def tile_weighted_hankel_subspace_s11_kernel(
                 for pair in range(1 if g == 1 else 0, 4):
                     tr_copy(g - 1, pair, "S")
                 for c in range(half_rt, RT):
-                    fut(g, c, fut_banks + c - half_rt)
-                if g == 2:
-                    ilv_y(3, (g_y + y_cols) // 2, y_cols, "V")
-                if g < last:
-                    for f in range(FP):
-                        quant_y(g + 1, f, f + 1)
+                    fut(g, c, fut_banks + c - half_rt if c - half_rt < ahead else tr_banks + c - half_rt - ahead)
+                if g == 1:
+                    for n0, n1 in ((0, 512), (512, 768), (768, y_cols)):
+                        quant_y(2, n0, n1)
+                elif g == 2:
+                    for n0 in (0, 512):
+                        quant_y(3, n0, n0 + 512)
                 else:
-                    for d in (2, 1, 0):
+                    for d in (2, 0, 1):
                         quant_z(0, d)
                 if g == 1:
-                    ilv_y(3, 0, 512, "G")
-                    ilv_y(3, 512, g_y, "G")
-                    ilv_y(3, g_y, (g_y + y_cols) // 2, "S")
-                    ilv_z_rows(0, 2 * P, z_rows, "S")
+                    ilv_y(3, 0, G_Y, "G")
+                    ilv_y(3, G_Y, y_cols, "S")
+                    ilv_z(0, 2, 0, P, "S")
                 elif g == 2:
-                    ilv_z_rows(0, g_z[0], 2 * P, "S")
-                    ilv_z_rows(0, 0, g_z[0], "G")
-                    ilv_z_rows(1, P, P + Z_STEP, "S")
+                    ilv_z(0, 0, 0, P, "G")
+                    ilv_z(0, 1, 0, P, "S")
                 else:
-                    ilv_z_rows(1, 0, g_z[1], "G")
-                    ilv_z_rows(1, P + Z_STEP, 2 * P, "S")
-                for c in range(half_rt, RT):
+                    ilv_z(1, 0, 0, P, "G")
+                    ilv_z(1, 1, 0, Z1_S, "S")
+                for c in range(ahead, RT):
                     a_op(g, c)
             load_z(2, 2)
             for d in range(2):
                 load_z(last, d)
 
-            b_banks = (4, 5)
-            for cc in range(2):
-                past(0, cc, b_banks[cc])
+            b_banks = (6, 7)
+            for cc, bank in enumerate((6, 7, 2)):
+                past(0, cc, bank)
                 past_copy(0, cc, "S")
-            for pair in range(4):
-                tr(last, pair, pair)
+                if cc < 2:
+                    ilv_z(1, 1, Z1_S + (P - Z1_S) // 2 * cc, Z1_S + (P - Z1_S) // 2 * (cc + 1), "S")
+            for pair, bank in enumerate((3, 0, 1, 4)):
+                tr(last, pair, bank)
                 tr_copy(last, pair, "S")
-            for cc in range(2, 4):
-                past(0, cc, 4 + cc)
-                past_copy(0, cc, "S")
-            ilv_z_rows(1, 2 * P, z_rows, "V")
-            ilv_z_rows(1, g_z[1], P, "V")
-            for d in (1, 2, 0):
+            past(0, 3, 5)
+            past_copy(0, 3, "S")
+            ilv_z(1, 2, 0, P, "V")
+            for d in (0, 1, 2):
                 quant_z(1, d)
             load_z(last, 2)
 
             open_sums = [(0, cs) for cs in pairs] + [(1, cs) for cs in pairs[:2]]
-            out_banks = (0, 1, 2, 3, 6, 7)
+            out_banks = (2, 3, 0, 1, 4, 5)
             slots = [(2, i) for i in range(3)] + [(3, i) for i in range(4)]
-            z_scalar = {2: 3 * Z_STEP, 3: 4 * Z_STEP}
+            z_scalar = {2: P, 3: 4 * Z_STEP}
             for g in range(1, last):
                 quant_a(g - 1, 0, RT)
-                quant_past(g - 1, 0, C)
-                ilv_z_rows(g + 1, 2 * P, z_rows, "V")
+                quant_past(g - 1, 0, 256)
+                ilv_z(g + 1, 2, 0, P, "V")
+                quant_past(g - 1, 256, C)
                 for cc in range(4):
                     step = 4 * (g - 1) + cc
                     if step < len(slots):
                         gz, i = slots[step]
-                        ilv_z_scalar(gz, Z_STEP * i, Z_STEP * (i + 1), z_scalar[gz] - P)
+                        ilv_z_scalar(gz, Z_STEP * i, min(Z_STEP * (i + 1), z_scalar[gz]), z_scalar[gz] - P)
                     past(g, cc, b_banks[cc % 2])
                     past_copy(g, cc, "S")
                     if cc > 0:
@@ -523,5 +533,5 @@ def tile_weighted_hankel_subspace_s11_kernel(
             finish(1, pairs[2], "V")
             for i, c in enumerate(pairs[3]):
                 for g in range(last):
-                    h_pass(1, (c,), g, i)
+                    h_pass(1, (c,), g, out_banks[i])
                 finish(1, (c,), "SV"[i])

@@ -26,8 +26,8 @@ RT = R // P
 AI = 4
 AT = 13
 WI = 2
-G_Y = 736
-Z_STEP = 44
+G_Y = 704
+Z_STEP = 48
 Z1_S = 96
 
 
@@ -46,9 +46,6 @@ def tile_weighted_hankel_subspace_s11_kernel(
         rho16 = keep.tile([P, RT], BF16, name="rho16")
         lev = keep.tile([P, RT], F32, name="lev")
         rhos = keep.tile([P, RT], F32, name="rhos")
-        lam_row = keep.tile([P, T], BF16, name="lam_row")
-        ones = keep.tile([P, P], BF16, name="ones")
-        lam_ord = keep.tile([P, T], BF16, name="lam_ord")
         wcode = keep.tile([P, RT, FP, P], U32, name="wcode", align_bytes=64)
         wscale = keep.tile([P, RT, FP, P], U8, name="wscale", align_bytes=64)
         pw = keep.tile([P, DP, 2 * C], U8, name="pw", align_bytes=64)
@@ -233,7 +230,7 @@ def tile_weighted_hankel_subspace_s11_kernel(
                 out=at[:].rearrange("p (u q) -> p u q", u=2),
                 in0=tiles["fp", g, c][:].rearrange("p (q u) -> p u q", u=2),
                 scalar=lev[:, c : c + 1],
-                in1=lam_ord[:, 512 * g : 512 * g + 512].rearrange("p (u q) -> p u q", u=2),
+                in1=tiles["lam", g][:].rearrange("p (q u) -> p u q", u=2),
                 op0=ADD,
                 op1=MULT,
             )
@@ -274,35 +271,25 @@ def tile_weighted_hankel_subspace_s11_kernel(
                     stop=(g == GROUPS - 1 and i == len(cs) - 1),
                 )
 
-        def h_out(half, cs, eng):
-            ho = work.tile([P, len(cs), 256], F32, name="zr", bufs=8, align_bytes=64)
-            for i, c in enumerate(cs):
-                src = tiles["h", half, cs][:, i, :]
-                if eng == "S":
-                    nc.scalar.activation(out=ho[:, i, :], in_=src, func=COPY, scale=rhos[:, c : c + 1])
-                else:
-                    nc.vector.tensor_scalar(
-                        out=ho[:, i, :], in0=src, scalar1=rhos[:, c : c + 1], scalar2=None, op0=MULT
-                    )
-            tiles["ho", half, cs] = ho
+        def h_out(half, cs, eng, step):
+            for i0 in range(0, len(cs), step):
+                ho = work.tile([P, step, 256], F32, name="zr", bufs=8, align_bytes=64)
+                for i in range(step):
+                    c = cs[i0 + i]
+                    src = tiles["h", half, cs][:, i0 + i, :]
+                    if eng == "S":
+                        nc.scalar.activation(out=ho[:, i, :], in_=src, func=COPY, scale=rhos[:, c : c + 1])
+                    else:
+                        nc.vector.tensor_scalar(
+                            out=ho[:, i, :], in0=src, scalar1=rhos[:, c : c + 1], scalar2=None, op0=MULT
+                        )
+                c0 = cs[i0]
+                nc.sync.dma_start(out=out_view[:, c0 : c0 + step, 256 * half : 256 * half + 256], in_=ho[:])
 
-        def store(half, cs):
-            dst = out_view[:, cs[0] : cs[-1] + 1, 256 * half : 256 * half + 256]
-            nc.sync.dma_start(out=dst, in_=tiles["ho", half, cs][:])
-
-        def load_lam():
-            nc.sync.dma_start(out=lam_row[0:1, :], in_=lam.rearrange("(o n) -> o n", o=1))
-
-        def spread_lam(i, bank):
-            lp = bank_tile(bank, [P, 2, 512], BF16)
-            for k in range(2):
-                g = 2 * i + k
-                row = lam_row[:, 512 * g : 512 * g + 512].rearrange("p (q u) -> p u q", u=2)
-                nc.tensor.matmul(out=lp[:, k, :], lhsT=ones[:], rhs=row, start=True, stop=True)
-            tiles["lp", i] = lp
-
-        def lam_copy(i, eng):
-            copy(eng, lam_ord[:, 1024 * i : 1024 * i + 1024], tiles["lp", i][:].rearrange("p k n -> p (k n)"))
+        def load_lam(g):
+            lam_all = keep.tile([P, 512], BF16, name="lam%d" % g)
+            nc.sync.dma_start(out=lam_all[:], in_=lam[512 * g : 512 * g + 512].partition_broadcast(P))
+            tiles["lam", g] = lam_all
 
         def load_scale():
             nc.scalar.dma_start(out=y_scale[:], in_=y_f_scale.rearrange("(g p t) o -> p g (t o)", g=FP, p=P, t=4))
@@ -346,77 +333,78 @@ def tile_weighted_hankel_subspace_s11_kernel(
             for i, eng in enumerate(engs):
                 widen(g, f, first + i, eng)
 
-        def w_tile(c):
-            w_transpose(c, 3 + (c + 1) % 4)
-            w_copy(c, "S")
+        def w_turn(pair):
+            for c in pairs[pair]:
+                w_transpose(c, half_rt + c % half_rt)
+
+        def w_copies(pair):
+            for c in pairs[pair]:
+                w_copy(c, "S")
 
         def finish(half, cs, eng):
             h_pass(half, cs, last)
-            h_out(half, cs, eng)
-            store(half, cs)
+            h_out(half, cs, eng, 1 if half else len(cs))
 
         with tc.manual_schedule():
-            nc.vector.memset(lam_row[:].bitcast(I32), 0)
             make_identity(nc, ident[:])
-            nc.vector.memset(ones[:], 1.0)
             nc.vector.memset(pws[:].rearrange("p d n -> p (d n)").bitcast(I32), 0)
             load_scale()
             load_y(0, 0, 2)
             load_y(0, 1)
-            load_y(1, 0)
-            load_lam()
             load_w(0)
+            load_y(1, 0)
             load_w(1)
-            load_y(1, 1)
             load_w(2)
-            load_rows()
+            load_y(1, 1)
             load_w(3)
-            for f in range(FP):
-                load_y(2, f)
+            load_rows()
+            load_y(2, 0)
+            load_lam(0)
+            load_y(2, 1)
 
             widen_planes(0, 0, "SVVV")
             ilv_y(0, 0, 512, "V")
-            widen_planes(0, 1, "SSVV")
+            widen_planes(0, 1, "SSSV")
             quant_y(0, 0, 512)
             ilv_y(0, 512, y_cols, "V")
             for f in range(FP):
                 load_y(3, f)
+            for g in range(1, GROUPS):
+                load_lam(g)
             for d in (2, 0, 1):
                 load_z(0, d)
             load_pw()
             load_pws()
             load_z(1, 0)
-            widen_planes(1, 0, "SSSS")
-            widen_planes(1, 1, "VV", 2)
-            quant_y(0, 512, y_cols)
-            spread_lam(0, 0)
-            lam_copy(0, "S")
-            for c in range(4):
-                w_tile(c)
-            spread_lam(1, 7)
+            w_turn(0)
+            w_copies(0)
             w_quant(0)
+            quant_y(0, 512, y_cols)
+            widen_planes(1, 0, "SSSV")
+            w_turn(1)
+            w_copies(1)
+            widen_planes(1, 1, "SSVV")
             ilv_y(1, 0, 512, "V")
-            widen_planes(1, 1, "SS")
             w_quant(1)
             widen_small()
-            for c in pairs[2]:
-                w_tile(c)
-            fut(0, 0, 0)
+            w_turn(2)
+            w_copies(2)
+            for c in pairs[0]:
+                fut(0, c, c)
+            w_turn(3)
             ilv_y(1, 512, y_cols, "V")
-            widen_planes(2, 0, "SS")
             w_quant(2)
-            for c in pairs[3]:
-                w_tile(c)
+            widen_planes(2, 0, "S")
+            w_copies(3)
             quant_y(1, 0, 512)
             w_quant(3)
             quant_y(1, 512, y_cols)
-            widen_planes(2, 0, "SS", 2)
-            lam_copy(1, "S")
+            widen_planes(2, 0, "SSS", 1)
             ilv_y(2, 0, 512, "G")
             widen_planes(2, 1, "SSSS")
             ilv_y(2, 512, y_cols, "G")
             for c in range(RT):
-                if c > 0:
+                if c > 1:
                     fut(0, c, c)
                 a_op(0, c)
             for g, d in ((1, 1), (1, 2), (2, 0), (2, 1)):

@@ -389,8 +389,7 @@ def tile_weighted_hankel_subspace_s11_kernel(
             widen_small()
             w_turn(2)
             w_copies(2)
-            for c in pairs[0]:
-                fut(0, c, c)
+            fut(0, 0, 0)
             w_turn(3)
             ilv_y(1, 512, y_cols, "V")
             w_quant(2)
@@ -404,7 +403,7 @@ def tile_weighted_hankel_subspace_s11_kernel(
             widen_planes(2, 1, "SSSS")
             ilv_y(2, 512, y_cols, "G")
             for c in range(RT):
-                if c > 1:
+                if c > 0:
                     fut(0, c, c)
                 a_op(0, c)
             for g, d in ((1, 1), (1, 2), (2, 0), (2, 1)):
@@ -418,8 +417,15 @@ def tile_weighted_hankel_subspace_s11_kernel(
                     fut(g, c, fut_banks + c)
                     if c < ahead:
                         a_op(g, c)
-                for pair in range(4):
-                    tr(g - 1, pair, tr_banks + pair)
+                if g == 1:
+                    for pair in range(4):
+                        tr(0, pair, (half_rt + pair + 2 * (pair // 2)) % RT)
+                        if pair == 1:
+                            for c in (4, 5):
+                                fut(1, c, c + 2)
+                else:
+                    for pair in range(4):
+                        tr(g - 1, pair, tr_banks + pair)
                 if g == 1:
                     widen_planes(3, 0, "SSSS")
                     widen_planes(3, 1, "SS")
@@ -427,7 +433,7 @@ def tile_weighted_hankel_subspace_s11_kernel(
                     widen_planes(3, 1, "SS", 2)
                 for pair in range(1 if g == 1 else 0, 4):
                     tr_copy(g - 1, pair, "S")
-                for c in range(half_rt, RT):
+                for c in range(6 if g == 1 else half_rt, RT):
                     fut(g, c, fut_banks + c - half_rt if c - half_rt < ahead else tr_banks + c - half_rt - ahead)
                 if g == 1:
                     for n0, n1 in ((0, 512), (512, 768), (768, y_cols)):

@@ -19,16 +19,21 @@ MULT = mybir.AluOpType.mult
 COPY = mybir.ActivationFunctionType.Copy
 
 P = 128
-GROUPS = T // 512
-FP = F // 512
-DP = D // 512
+N = 512
+HALF = C // 2
+GROUPS = T // N
+FP = F // N
+DP = D // N
 RT = R // P
-AI = 4
-AT = 13
-WI = 2
-G_Y = 704
+
+FEW, MANY, EVEN = "SVVV", "SSSV", "SSVV"
+Y_POOL = 704
 Z_STEP = 48
-Z1_S = 96
+
+Y_BUFS = 6
+LOAD_BUFS = 8
+Z_BUFS = 6
+AT_BUFS = RT + RT // 2 + 1
 
 
 def tile_weighted_hankel_subspace_s11_kernel(
@@ -54,19 +59,19 @@ def tile_weighted_hankel_subspace_s11_kernel(
         ascale = keep.tile([P, GROUPS, R], U8, name="ascale", align_bytes=64)
         bcode = keep.tile([P, GROUPS, C], U32, name="bcode", align_bytes=64)
         bscale = keep.tile([P, GROUPS, C], U8, name="bscale", align_bytes=64)
+        shared = keep.tile([P, FP * N * 4], BF16, name="shared", align_bytes=64)
 
-        shared = keep.tile([P, FP * 512 * 4], BF16, name="shared", align_bytes=64)
-
-        y_view = y_f_bytes.rearrange("(g p t) n -> g p t n", g=FP, p=P, t=4)
-        z_view = z_p.rearrange("(g p t) n -> g p t n", g=DP, p=P, t=4)
+        y_view = y_f_bytes.rearrange("(f p t) n -> f p t n", f=FP, p=P, t=4)
+        z_view = z_p.rearrange("(d p t) n -> d p t n", d=DP, p=P, t=4)
         w_view = w_f.rearrange("(p c) f -> p c f", c=RT)
         out_view = out.rearrange("(p c) n -> p c n", c=RT)
 
         tiles = {}
         last = GROUPS - 1
+        pairs = [(c, c + 1) for c in range(0, RT, 2)]
 
-        def bank_tile(bank, shape, dtype):
-            return psum.tile(shape, dtype, name="bank%d" % bank)
+        def bank_tile(bank, shape):
+            return psum.tile(shape, F32, name="bank%d" % bank)
 
         def copy(eng, dst, src):
             if eng == "S":
@@ -74,106 +79,110 @@ def tile_weighted_hankel_subspace_s11_kernel(
             else:
                 nc.vector.tensor_copy(out=dst, in_=src)
 
+        def pool_copy(dst, src):
+            nc.gpsimd.tensor_scalar(out=dst, in0=src, scalar1=1.0, scalar2=0.0, op0=MULT, op1=ADD)
+
         def load_y(g, f, step=4):
-            yb = work.tile([P, 4, 512], U8, name="yb", bufs=6, align_bytes=64)
+            yb = work.tile([P, 4, N], U8, name="yb", bufs=Y_BUFS, align_bytes=64)
             for t in range(0, 4, step):
-                nc.sync.dma_start(out=yb[:, t : t + step], in_=y_view[f][:, t : t + step, 512 * g : 512 * g + 512])
+                nc.sync.dma_start(out=yb[:, t : t + step], in_=y_view[f][:, t : t + step, N * g : N * g + N])
             tiles["yb", g, f] = yb
 
         def load_z(g, d):
-            zr = work.tile([P, 4, 512], BF16, name="zr", bufs=8, align_bytes=64)
-            nc.sync.dma_start(out=zr[:], in_=z_view[d][:, :, 512 * g : 512 * g + 512])
+            zr = work.tile([P, 4, N], BF16, name="zr", bufs=LOAD_BUFS, align_bytes=64)
+            nc.sync.dma_start(out=zr[:], in_=z_view[d][:, :, N * g : N * g + N])
             tiles["zr", g, d] = zr
 
         def load_w(pair):
-            wf = work.tile([P, 2, F], BF16, name="zr", bufs=8, align_bytes=64)
+            wf = work.tile([P, 2, F], BF16, name="zr", bufs=LOAD_BUFS, align_bytes=64)
             nc.sync.dma_start(out=wf[:], in_=w_view[:, 2 * pair : 2 * pair + 2, :])
             tiles["wf", pair] = wf
 
-        def widened(g):
+        def load_lam(g):
+            lam_all = keep.tile([P, N], BF16, name="lam%d" % g)
+            nc.sync.dma_start(out=lam_all[:], in_=lam[N * g : N * g + N].partition_broadcast(P))
+            tiles["lam", g] = lam_all
+
+        def load_wp():
+            nc.sync.dma_start(out=pw[:], in_=w_p_words.rearrange("d p n -> p d n"))
+            for q in range(4):
+                nc.sync.dma_start(
+                    out=pws[32 * q : 32 * q + 4, :, :].bitcast(I32),
+                    in_=w_p_scales[:, 4 * q : 4 * q + 4, :].rearrange("d q n -> q d n").bitcast(I32),
+                )
+
+        def widen(g, f, engs, first=0):
             if ("yw", g) not in tiles:
-                tiles["yw", g] = work.tile([P, FP * 4 * 512], BF16, name="yw", align_bytes=64)
-            if g == last:
-                return tiles["yw", g][:].rearrange("p (t f n) -> p f t n", t=4, f=FP)
-            return tiles["yw", g][:].rearrange("p (f t n) -> p f t n", t=4, f=FP)
+                tiles["yw", g] = work.tile([P, FP * 4 * N], BF16, name="yw", align_bytes=64)
+            order = "p (t f n) -> p f t n" if g == last else "p (f t n) -> p f t n"
+            planes = tiles["yw", g][:].rearrange(order, t=4, f=FP)
+            for i, eng in enumerate(engs):
+                t = first + i
+                src = tiles["yb", g, f][:, t, :].bitcast(FP8)
+                s = y_scale[:, f, t : t + 1]
+                if eng == "S":
+                    nc.scalar.activation(out=planes[:, f, t, :], in_=src, func=COPY, scale=s)
+                else:
+                    nc.vector.tensor_scalar(out=planes[:, f, t, :], in0=src, scalar1=s, scalar2=None, op0=MULT)
 
-        def widen(g, f, t, eng):
-            src = tiles["yb", g, f][:, t, :].bitcast(FP8)
-            dst = widened(g)[:, f, t, :]
-            s = y_scale[:, f, t : t + 1]
-            if eng == "S":
-                nc.scalar.activation(out=dst, in_=src, func=COPY, scale=s)
-            else:
-                nc.vector.tensor_scalar(out=dst, in0=src, scalar1=s, scalar2=None, op0=MULT)
-
-        def ilv_y(g, n0, n1, eng):
+        def weave_y(g, n0, n1, eng):
             dst = shared[:, 4 * n0 : 4 * n1].rearrange("p (n t) -> p n t", t=4)
             if g == last:
                 src = tiles["yw", g][:].rearrange("p (t n) -> p t n", t=4)[:, :, n0:n1]
             else:
-                src = widened(g)[:, n0 // 512, :, n0 % 512 : (n1 - 1) % 512 + 1]
+                src = tiles["yw", g][:, 4 * n0 : 4 * n1].rearrange("p (t n) -> p t n", t=4)
             if eng == "G":
-                nc.gpsimd.tensor_scalar(
-                    out=dst, in0=src.rearrange("p t n -> p n t"), scalar1=1.0, scalar2=0.0, op0=MULT, op1=ADD
-                )
+                pool_copy(dst, src.rearrange("p t n -> p n t"))
             else:
                 copy(eng, dst.rearrange("p (c i) t -> p c t i", i=4), src.rearrange("p t (c i) -> p c t i", i=4))
 
         def quant_y(g, n0, n1):
             if ("yc", g) not in tiles:
-                tiles["yc", g] = work.tile([P, FP * 512], U32, name="yc", align_bytes=64)
-                tiles["ys", g] = work.tile([P, FP * 512], U8, name="ys", align_bytes=64)
+                tiles["yc", g] = work.tile([P, FP * N], U32, name="yc", align_bytes=64)
+                tiles["ys", g] = work.tile([P, FP * N], U8, name="ys", align_bytes=64)
             nc.vector.quantize_mx(
                 out=tiles["yc", g][:, n0:n1].bitcast(FP8X4),
                 scales=tiles["ys", g][:, n0:n1],
                 in_=shared[:, 4 * n0 : 4 * n1],
             )
 
-        def ilv_z(g, d, m0, m1, eng):
+        def weave_z(g, d, m0, m1, eng):
             if ("zi", g, d) not in tiles:
                 if eng == "G":
-                    tiles["zi", g, d] = shared[:, 0:2048]
+                    tiles["zi", g, d] = shared[:, 0 : 4 * N]
                 else:
-                    zi = work.tile([P, 2048], BF16, name="zi", bufs=6, align_bytes=64)
-                    tiles["zi", g, d] = zi[:]
+                    tiles["zi", g, d] = work.tile([P, 4 * N], BF16, name="zi", bufs=Z_BUFS, align_bytes=64)[:]
             dst = tiles["zi", g, d].rearrange("p (s m j) -> p s m j", s=4, j=4)
             src = tiles["zr", g, d][:]
             if eng == "G":
-                nc.gpsimd.tensor_scalar(
-                    out=dst.rearrange("p s m j -> p m s j")[:, m0:m1],
-                    in0=src.rearrange("p j (m s) -> p m s j", s=4)[:, m0:m1],
-                    scalar1=1.0,
-                    scalar2=0.0,
-                    op0=MULT,
-                    op1=ADD,
-                )
+                src = src.rearrange("p j (m s) -> p m s j", s=4)
+                pool_copy(dst.rearrange("p s m j -> p m s j")[:, m0:m1], src[:, m0:m1])
             else:
-                dst = dst.rearrange("p s (m e) j -> p m j e s", e=2)[:, m0 // 2 : m1 // 2]
-                src = src.rearrange("p j (m e s) -> p m j e s", e=2, s=4)[:, m0 // 2 : m1 // 2]
+                dst = dst.rearrange("p s m (h e) -> p m h s e", e=2)[:, m0:m1]
+                src = src.rearrange("p (h e) (m s) -> p m h s e", e=2, s=4)[:, m0:m1]
                 copy(eng, dst, src)
 
-        def quant_z(g, d):
-            if ("zc", g) not in tiles:
-                tiles["zc", g] = work.tile([P, DP, 512], U32, name="zc", align_bytes=64)
-                tiles["zs", g] = work.tile([P, DP, 512], U8, name="zs", align_bytes=64)
-            nc.vector.quantize_mx(
-                out=tiles["zc", g][:, d].bitcast(FP8X4),
-                scales=tiles["zs", g][:, d],
-                in_=tiles["zi", g, d],
-            )
+        def quant_z(g, order):
+            tiles["zc", g] = work.tile([P, DP, N], U32, name="zc", align_bytes=64)
+            tiles["zs", g] = work.tile([P, DP, N], U8, name="zs", align_bytes=64)
+            for d in order:
+                nc.vector.quantize_mx(
+                    out=tiles["zc", g][:, d].bitcast(FP8X4), scales=tiles["zs", g][:, d], in_=tiles["zi", g, d]
+                )
 
-        def w_transpose(c, bank):
-            wt = bank_tile(bank, [P, FP, 2, P], F32)
-            words = tiles["wf", c // 2][:, c % 2, :].bitcast(F32)
-            for f in range(FP):
-                for u in range(2):
-                    nc.tensor.transpose(wt[:, f, u, :], words[:, 256 * f + u : 256 * (f + 1) : 2], ident[:])
-            tiles["wt", c] = wt
+        def w_turn(pair):
+            for c in pairs[pair]:
+                wt = bank_tile(4 + c % 4, [P, FP, 2, P])
+                words = tiles["wf", pair][:, c % 2, :].bitcast(F32)
+                for f in range(FP):
+                    for u in range(2):
+                        nc.tensor.transpose(wt[:, f, u, :], words[:, 256 * f + u : 256 * (f + 1) : 2], ident[:])
+                tiles["wt", c] = wt
 
-        def w_copy(c, eng):
-            if ("wi", c // 2) not in tiles:
-                tiles["wi", c // 2] = work.tile([P, 2, FP, P, 2], F32, name="wi", bufs=WI, align_bytes=64)
-            copy(eng, tiles["wi", c // 2][:, c % 2], tiles["wt", c][:].rearrange("p f u r -> p f r u"))
+        def w_copy(pair):
+            tiles["wi", pair] = work.tile([P, 2, FP, P, 2], F32, name="wi", align_bytes=64)
+            for c in pairs[pair]:
+                copy("S", tiles["wi", pair][:, c % 2], tiles["wt", c][:].rearrange("p f u r -> p f r u"))
 
         def w_quant(pair):
             nc.vector.quantize_mx(
@@ -182,50 +191,21 @@ def tile_weighted_hankel_subspace_s11_kernel(
                 in_=tiles["wi", pair][:].rearrange("p c f r u -> p (c f r u)").bitcast(BF16),
             )
 
-        def past(g, cc, bank):
-            pp = bank_tile(bank, [P, 4, 128], F32)
-            for s in range(4):
-                for d in range(DP):
-                    nc.tensor.matmul_mx(
-                        out=pp[:, 2 * (s % 2) + s // 2, :],
-                        lhsT=tiles["zc", g][:, d, 128 * s : 128 * s + 128].bitcast(FP8X4),
-                        lhsT_scale=tiles["zs", g][:, d, 128 * s : 128 * s + 128],
-                        rhs=pw[:, d, 256 * cc : 256 * cc + 256].bitcast(FP4X4),
-                        rhs_scale=pws[:, d, 128 * cc : 128 * cc + 128],
-                        start=(d == 0),
-                        stop=(d == DP - 1),
-                    )
-            tiles["pp", g, cc] = pp
-
-        def past_copy(g, cc, eng):
-            if ("pi", g) not in tiles:
-                tiles["pi", g] = work.tile([P, 512, 4], BF16, name="pi", align_bytes=64)
-            dst = tiles["pi", g][:, 128 * cc : 128 * cc + 128, :]
-            copy(eng, dst, tiles["pp", g, cc][:].rearrange("p s n -> p n s"))
-
-        def quant_past(g, n0, n1):
-            nc.vector.quantize_mx(
-                out=bcode[:, g, n0:n1].bitcast(FP8X4),
-                scales=bscale[:, g, n0:n1],
-                in_=tiles["pi", g][:, n0:n1, :].rearrange("p n s -> p (n s)"),
-            )
-
-        def fut(g, c, bank):
-            fp = bank_tile(bank, [P, 512], F32)
+        def future(g, c, bank):
+            tiles["fp", g, c] = bank_tile(bank, [P, N])
             for f in range(FP):
                 nc.tensor.matmul_mx(
-                    out=fp[:],
+                    out=tiles["fp", g, c][:],
                     lhsT=wcode[:, c, f, :].bitcast(FP8X4),
                     lhsT_scale=wscale[:, c, f, :],
-                    rhs=tiles["yc", g][:, 512 * f : 512 * f + 512].bitcast(FP8X4),
-                    rhs_scale=tiles["ys", g][:, 512 * f : 512 * f + 512],
+                    rhs=tiles["yc", g][:, N * f : N * f + N].bitcast(FP8X4),
+                    rhs_scale=tiles["ys", g][:, N * f : N * f + N],
                     start=(f == 0),
                     stop=(f == FP - 1),
                 )
-            tiles["fp", g, c] = fp
 
-        def a_op(g, c):
-            at = work.tile([P, 512], BF16, name="at", bufs=AT, align_bytes=64)
+        def epilogue(g, c):
+            at = work.tile([P, N], BF16, name="at", bufs=AT_BUFS, align_bytes=64)
             nc.vector.scalar_tensor_tensor(
                 out=at[:].rearrange("p (u q) -> p u q", u=2),
                 in0=tiles["fp", g, c][:].rearrange("p (q u) -> p u q", u=2),
@@ -236,119 +216,85 @@ def tile_weighted_hankel_subspace_s11_kernel(
             )
             tiles["at", g, c] = at
 
-        def tr(g, pair, bank):
-            tp = bank_tile(bank, [P, 2, 2, P], F32)
+        def a_turn(g, pair, bank):
+            tp = bank_tile(bank, [P, 2, 2, P])
             for i in range(2):
                 words = tiles["at", g, 2 * pair + i][:].bitcast(F32)
                 for u in range(2):
                     nc.tensor.transpose(tp[:, i, u, :], words[:, P * u : P * u + P], ident[:])
             tiles["tp", g, pair] = tp
 
-        def tr_copy(g, pair, eng):
-            if ("ai", g) not in tiles:
-                tiles["ai", g] = work.tile([P, RT, P, 2], F32, name="ai", bufs=AI, align_bytes=64)
+        def a_copy(g, pair):
+            if pair == 0:
+                tiles["ai", g] = work.tile([P, RT, P, 2], F32, name="ai", bufs=GROUPS, align_bytes=64)
             dst = tiles["ai", g][:, 2 * pair : 2 * pair + 2]
-            copy(eng, dst, tiles["tp", g, pair][:].rearrange("p c u r -> p c r u"))
+            copy("S", dst, tiles["tp", g, pair][:].rearrange("p c u r -> p c r u"))
 
-        def quant_a(g, c0, c1):
+        def quant_a(g):
             nc.vector.quantize_mx(
-                out=acode[:, g, P * c0 : P * c1].bitcast(FP8X4),
-                scales=ascale[:, g, P * c0 : P * c1],
-                in_=tiles["ai", g][:, c0:c1].rearrange("p c r u -> p (c r u)").bitcast(BF16),
+                out=acode[:, g].bitcast(FP8X4),
+                scales=ascale[:, g],
+                in_=tiles["ai", g][:].rearrange("p c r u -> p (c r u)").bitcast(BF16),
             )
 
-        def h_pass(half, cs, g, bank=None):
+        def past(g, cc, bank):
+            pp = bank_tile(bank, [P, 4, P])
+            for s in range(4):
+                for d in range(DP):
+                    nc.tensor.matmul_mx(
+                        out=pp[:, 2 * (s % 2) + s // 2, :],
+                        lhsT=tiles["zc", g][:, d, P * s : P * s + P].bitcast(FP8X4),
+                        lhsT_scale=tiles["zs", g][:, d, P * s : P * s + P],
+                        rhs=pw[:, d, 2 * P * cc : 2 * P * (cc + 1)].bitcast(FP4X4),
+                        rhs_scale=pws[:, d, P * cc : P * cc + P],
+                        start=(d == 0),
+                        stop=(d == DP - 1),
+                    )
+            if cc == 0:
+                tiles["pi", g] = work.tile([P, C, 4], BF16, name="pi", align_bytes=64)
+            copy("S", tiles["pi", g][:, P * cc : P * cc + P, :], pp[:].rearrange("p s n -> p n s"))
+
+        def quant_b(g, n0, n1):
+            nc.vector.quantize_mx(
+                out=bcode[:, g, n0:n1].bitcast(FP8X4),
+                scales=bscale[:, g, n0:n1],
+                in_=tiles["pi", g][:, n0:n1, :].rearrange("p n s -> p (n s)"),
+            )
+
+        def sum_pass(half, cs, g, bank=None):
             if g == 0:
-                tiles["h", half, cs] = bank_tile(bank, [P, len(cs), 256], F32)
+                tiles["h", half, cs] = bank_tile(bank, [P, len(cs), HALF])
             for i, c in enumerate(cs):
                 nc.tensor.matmul_mx(
                     out=tiles["h", half, cs][:, i, :],
                     lhsT=acode[:, g, P * c : P * c + P].bitcast(FP8X4),
                     lhsT_scale=ascale[:, g, P * c : P * c + P],
-                    rhs=bcode[:, g, 256 * half : 256 * half + 256].bitcast(FP8X4),
-                    rhs_scale=bscale[:, g, 256 * half : 256 * half + 256],
+                    rhs=bcode[:, g, HALF * half : HALF * half + HALF].bitcast(FP8X4),
+                    rhs_scale=bscale[:, g, HALF * half : HALF * half + HALF],
                     start=(g == 0 and i == 0),
-                    stop=(g == GROUPS - 1 and i == len(cs) - 1),
+                    stop=(g == last and i == len(cs) - 1),
                 )
-
-        def h_out(half, cs, eng, step):
-            for i0 in range(0, len(cs), step):
-                ho = work.tile([P, step, 256], F32, name="zr", bufs=8, align_bytes=64)
-                for i in range(step):
-                    c = cs[i0 + i]
-                    src = tiles["h", half, cs][:, i0 + i, :]
-                    if eng == "S":
-                        nc.scalar.activation(out=ho[:, i, :], in_=src, func=COPY, scale=rhos[:, c : c + 1])
-                    else:
-                        nc.vector.tensor_scalar(
-                            out=ho[:, i, :], in0=src, scalar1=rhos[:, c : c + 1], scalar2=None, op0=MULT
-                        )
-                c0 = cs[i0]
-                nc.sync.dma_start(out=out_view[:, c0 : c0 + step, 256 * half : 256 * half + 256], in_=ho[:])
-
-        def load_lam(g):
-            lam_all = keep.tile([P, 512], BF16, name="lam%d" % g)
-            nc.sync.dma_start(out=lam_all[:], in_=lam[512 * g : 512 * g + 512].partition_broadcast(P))
-            tiles["lam", g] = lam_all
-
-        def load_scale():
-            nc.scalar.dma_start(out=y_scale[:], in_=y_f_scale.rearrange("(g p t) o -> p g (t o)", g=FP, p=P, t=4))
-
-        def load_rows():
-            nc.sync.dma_start(out=lev16[:], in_=level.rearrange("(p c) -> p c", c=RT))
-            nc.sync.dma_start(out=rho16[:], in_=rho.rearrange("(p c) -> p c", c=RT))
-
-        def load_pw():
-            nc.sync.dma_start(out=pw[:], in_=w_p_words.rearrange("d p n -> p d n"))
-
-        def load_pws():
-            for q in range(4):
-                nc.sync.dma_start(
-                    out=pws[32 * q : 32 * q + 4, :, :].bitcast(I32),
-                    in_=w_p_scales[:, 4 * q : 4 * q + 4, :].rearrange("d q n -> q d n").bitcast(I32),
-                )
-
-        def widen_small():
-            nc.vector.tensor_copy(out=lev[:], in_=lev16[:])
-            nc.vector.tensor_copy(out=rhos[:], in_=rho16[:])
-
-        pairs = [(c, c + 1) for c in range(0, RT, 2)]
-        half_rt = RT // 2
-        y_cols = FP * 512
-        z_rows = DP * P
-
-        def ilv_z_rows(g, lo, hi, eng):
-            for d in range(DP):
-                m0, m1 = max(lo - P * d, 0), min(hi - P * d, P)
-                if m0 < m1:
-                    ilv_z(g, d, m0, m1, eng)
-
-        def ilv_z_scalar(g, lo, hi, extra):
-            if lo < extra:
-                ilv_z(g, 1, lo, min(hi, extra), "S")
-            if hi > extra:
-                ilv_z(g, 0, max(lo, extra) - extra, hi - extra, "S")
-
-        def widen_planes(g, f, engs, first=0):
-            for i, eng in enumerate(engs):
-                widen(g, f, first + i, eng)
-
-        def w_turn(pair):
-            for c in pairs[pair]:
-                w_transpose(c, half_rt + c % half_rt)
-
-        def w_copies(pair):
-            for c in pairs[pair]:
-                w_copy(c, "S")
 
         def finish(half, cs, eng):
-            h_pass(half, cs, last)
-            h_out(half, cs, eng, 1 if half else len(cs))
+            sum_pass(half, cs, last)
+            step = 1 if half else len(cs)
+            for i0 in range(0, len(cs), step):
+                ho = work.tile([P, step, HALF], F32, name="zr", bufs=LOAD_BUFS, align_bytes=64)
+                for i in range(step):
+                    src = tiles["h", half, cs][:, i0 + i, :]
+                    s = rhos[:, cs[i0 + i] : cs[i0 + i] + 1]
+                    if eng == "S":
+                        nc.scalar.activation(out=ho[:, i, :], in_=src, func=COPY, scale=s)
+                    else:
+                        nc.vector.tensor_scalar(out=ho[:, i, :], in0=src, scalar1=s, scalar2=None, op0=MULT)
+                rows = out_view[:, cs[i0] : cs[i0] + step, HALF * half : HALF * half + HALF]
+                nc.sync.dma_start(out=rows, in_=ho[:])
 
         with tc.manual_schedule():
             make_identity(nc, ident[:])
             nc.vector.memset(pws[:].rearrange("p d n -> p (d n)").bitcast(I32), 0)
-            load_scale()
+
+            nc.scalar.dma_start(out=y_scale[:], in_=y_f_scale.rearrange("(f p t) o -> p f (t o)", f=FP, p=P, t=4))
             load_y(0, 0, 2)
             load_y(0, 1)
             load_w(0)
@@ -357,175 +303,178 @@ def tile_weighted_hankel_subspace_s11_kernel(
             load_w(2)
             load_y(1, 1)
             load_w(3)
-            load_rows()
+            nc.sync.dma_start(out=lev16[:], in_=level.rearrange("(p c) -> p c", c=RT))
+            nc.sync.dma_start(out=rho16[:], in_=rho.rearrange("(p c) -> p c", c=RT))
             load_y(2, 0)
             load_lam(0)
             load_y(2, 1)
 
-            widen_planes(0, 0, "SVVV")
-            ilv_y(0, 0, 512, "V")
-            widen_planes(0, 1, "SSSV")
-            quant_y(0, 0, 512)
-            ilv_y(0, 512, y_cols, "V")
+            widen(0, 0, FEW)
+            weave_y(0, 0, N, "V")
+            widen(0, 1, MANY)
+            quant_y(0, 0, N)
+            weave_y(0, N, 2 * N, "V")
             for f in range(FP):
-                load_y(3, f)
+                load_y(last, f)
             for g in range(1, GROUPS):
                 load_lam(g)
             for d in (2, 0, 1):
                 load_z(0, d)
-            load_pw()
-            load_pws()
+            load_wp()
             load_z(1, 0)
             w_turn(0)
-            w_copies(0)
+            w_copy(0)
             w_quant(0)
-            quant_y(0, 512, y_cols)
-            widen_planes(1, 0, "SSSV")
+            quant_y(0, N, 2 * N)
+            widen(1, 0, MANY)
             w_turn(1)
-            w_copies(1)
-            widen_planes(1, 1, "SSVV")
-            ilv_y(1, 0, 512, "V")
+            w_copy(1)
+            widen(1, 1, EVEN)
+            weave_y(1, 0, N, "V")
             w_quant(1)
-            widen_small()
+            nc.vector.tensor_copy(out=lev[:], in_=lev16[:])
+            nc.vector.tensor_copy(out=rhos[:], in_=rho16[:])
             w_turn(2)
-            w_copies(2)
-            fut(0, 0, 0)
+            w_copy(2)
+            future(0, 0, 0)
             w_turn(3)
-            ilv_y(1, 512, y_cols, "V")
+            weave_y(1, N, 2 * N, "V")
             w_quant(2)
-            widen_planes(2, 0, "S")
-            w_copies(3)
-            quant_y(1, 0, 512)
+            widen(2, 0, "S")
+            w_copy(3)
+            quant_y(1, 0, N)
             w_quant(3)
-            quant_y(1, 512, y_cols)
-            widen_planes(2, 0, "SSS", 1)
-            ilv_y(2, 0, 512, "G")
-            widen_planes(2, 1, "SSSS")
-            ilv_y(2, 512, y_cols, "G")
+            quant_y(1, N, 2 * N)
+
+            widen(2, 0, "SSS", 1)
+            weave_y(2, 0, N, "G")
+            widen(2, 1, "SSSS")
+            weave_y(2, N, 2 * N, "G")
             for c in range(RT):
                 if c > 0:
-                    fut(0, c, c)
-                a_op(0, c)
+                    future(0, c, c)
+                epilogue(0, c)
             for g, d in ((1, 1), (1, 2), (2, 0), (2, 1)):
                 load_z(g, d)
+            for c in range(4):
+                future(1, c, c)
+                epilogue(1, c)
+            for pair, bank in enumerate((4, 5, 0, 1)):
+                a_turn(0, pair, bank)
+                if pair == 1:
+                    for c in pairs[2]:
+                        future(1, c, c + 2)
+            widen(last, 0, "SSSS")
+            widen(last, 1, "SS")
+            a_copy(0, 0)
+            widen(last, 1, "SS", 2)
+            for pair in range(1, 4):
+                a_copy(0, pair)
+            for c in pairs[3]:
+                future(1, c, c - 4)
+            for n0, n1 in ((0, N), (N, N + N // 2), (N + N // 2, 2 * N)):
+                quant_y(2, n0, n1)
 
-            for g in range(1, GROUPS):
-                fut_banks = half_rt * ((g + 1) % 2)
-                tr_banks = half_rt * (g % 2)
-                ahead = half_rt if g < last else 2
-                for c in range(half_rt):
-                    fut(g, c, fut_banks + c)
-                    if c < ahead:
-                        a_op(g, c)
-                if g == 1:
-                    for pair in range(4):
-                        tr(0, pair, (half_rt + pair + 2 * (pair // 2)) % RT)
-                        if pair == 1:
-                            for c in (4, 5):
-                                fut(1, c, c + 2)
-                else:
-                    for pair in range(4):
-                        tr(g - 1, pair, tr_banks + pair)
-                if g == 1:
-                    widen_planes(3, 0, "SSSS")
-                    widen_planes(3, 1, "SS")
-                    tr_copy(0, 0, "S")
-                    widen_planes(3, 1, "SS", 2)
-                for pair in range(1 if g == 1 else 0, 4):
-                    tr_copy(g - 1, pair, "S")
-                for c in range(6 if g == 1 else half_rt, RT):
-                    fut(g, c, fut_banks + c - half_rt if c - half_rt < ahead else tr_banks + c - half_rt - ahead)
-                if g == 1:
-                    for n0, n1 in ((0, 512), (512, 768), (768, y_cols)):
-                        quant_y(2, n0, n1)
-                elif g == 2:
-                    for n0 in (0, 512):
-                        quant_y(3, n0, n0 + 512)
-                else:
-                    for d in (2, 0, 1):
-                        quant_z(0, d)
-                if g == 1:
-                    ilv_y(3, 0, G_Y, "G")
-                    ilv_y(3, G_Y, y_cols, "S")
-                    ilv_z(0, 2, 0, P, "S")
-                elif g == 2:
-                    ilv_z(0, 0, 0, P, "G")
-                    ilv_z(0, 1, 0, P, "S")
-                else:
-                    ilv_z(1, 0, 0, P, "G")
-                    ilv_z(1, 1, 0, Z1_S, "S")
-                for c in range(ahead, RT):
-                    a_op(g, c)
+            weave_y(last, 0, Y_POOL, "G")
+            weave_y(last, Y_POOL, 2 * N, "S")
+            weave_z(0, 2, 0, P, "S")
+            for c in range(4, RT):
+                epilogue(1, c)
+            for c in range(4):
+                future(2, c, 4 + c)
+                epilogue(2, c)
+            for pair in range(4):
+                a_turn(1, pair, pair)
+            for pair in range(4):
+                a_copy(1, pair)
+            for c in range(4, RT):
+                future(2, c, c)
+            for f in range(FP):
+                quant_y(last, N * f, N * f + N)
+
+            weave_z(0, 0, 0, P, "G")
+            weave_z(0, 1, 0, P, "S")
+            for c in range(4, RT):
+                epilogue(2, c)
+            for c in range(4):
+                future(last, c, c)
+                if c < 2:
+                    epilogue(last, c)
+            for pair in range(4):
+                a_turn(2, pair, 4 + pair)
+            for pair in range(4):
+                a_copy(2, pair)
+            for c, bank in zip(range(4, RT), (0, 1, 4, 5)):
+                future(last, c, bank)
+            quant_z(0, (2, 0, 1))
+            weave_z(1, 0, 0, P, "G")
+            weave_z(1, 1, 0, 2 * Z_STEP, "S")
+            for c in range(2, RT):
+                epilogue(last, c)
             load_z(2, 2)
             for d in range(2):
                 load_z(last, d)
 
-            b_banks = (6, 7)
+            rest = (P - 2 * Z_STEP) // 2
             for cc, bank in enumerate((6, 7, 2)):
                 past(0, cc, bank)
-                past_copy(0, cc, "S")
                 if cc < 2:
-                    ilv_z(1, 1, Z1_S + (P - Z1_S) // 2 * cc, Z1_S + (P - Z1_S) // 2 * (cc + 1), "S")
+                    weave_z(1, 1, 2 * Z_STEP + rest * cc, 2 * Z_STEP + rest * (cc + 1), "S")
             for pair, bank in enumerate((3, 0, 1, 4)):
-                tr(last, pair, bank)
-                tr_copy(last, pair, "S")
+                a_turn(last, pair, bank)
+                a_copy(last, pair)
             past(0, 3, 5)
-            past_copy(0, 3, "S")
-            ilv_z(1, 2, 0, P, "V")
-            for d in (0, 1, 2):
-                quant_z(1, d)
+            weave_z(1, 2, 0, P, "V")
+            quant_z(1, range(DP))
             load_z(last, 2)
 
-            open_sums = [(0, cs) for cs in pairs] + [(1, cs) for cs in pairs[:2]]
-            out_banks = (2, 3, 0, 1, 4, 5)
-            slots = [(2, i) for i in range(3)] + [(3, i) for i in range(4)]
-            z_scalar = {2: P, 3: 4 * Z_STEP}
+            b_banks = (6, 7)
+            sums = [(0, cs) for cs in pairs] + [(1, cs) for cs in pairs[:2]]
+            sum_banks = (2, 3, 0, 1, 4, 5)
+            over = {2: 0, last: 4 * Z_STEP - P}
+            steps = [(2, Z_STEP * i) for i in range(3)] + [(last, Z_STEP * i) for i in range(4)]
             for g in range(1, last):
-                quant_a(g - 1, 0, RT)
-                quant_past(g - 1, 0, 256)
-                ilv_z(g + 1, 2, 0, P, "V")
-                quant_past(g - 1, 256, C)
+                quant_a(g - 1)
+                quant_b(g - 1, 0, HALF)
+                weave_z(g + 1, 2, 0, P, "V")
+                quant_b(g - 1, HALF, C)
                 for cc in range(4):
-                    step = 4 * (g - 1) + cc
-                    if step < len(slots):
-                        gz, i = slots[step]
-                        ilv_z_scalar(gz, Z_STEP * i, min(Z_STEP * (i + 1), z_scalar[gz]), z_scalar[gz] - P)
+                    for gz, lo in steps[4 * (g - 1) + cc : 4 * (g - 1) + cc + 1]:
+                        hi, cut = lo + Z_STEP, over[gz]
+                        if lo < cut:
+                            weave_z(gz, 1, lo, min(hi, cut), "S")
+                        if hi > cut:
+                            weave_z(gz, 0, max(lo, cut) - cut, min(hi - cut, P), "S")
                     past(g, cc, b_banks[cc % 2])
-                    past_copy(g, cc, "S")
-                    if cc > 0:
-                        for i in (2 * cc - 2, 2 * cc - 1):
-                            h_pass(open_sums[i][0], open_sums[i][1], g - 1, out_banks[i])
-                ilv_z_rows(g + 1, z_scalar[g + 1], 2 * P, "V")
-                for d in (2, 1, 0):
-                    quant_z(g + 1, d)
+                    for i in range(max(2 * cc - 2, 0), 2 * cc):
+                        sum_pass(sums[i][0], sums[i][1], g - 1, sum_banks[i])
+                weave_z(g + 1, 1, over[g + 1], P, "V")
+                quant_z(g + 1, (2, 1, 0))
 
-            quant_a(last - 1, 0, RT)
-            quant_past(last - 1, 0, C)
-            quant_a(last, 0, RT)
+            quant_a(last - 1)
+            quant_b(last - 1, 0, C)
+            quant_a(last)
             for cc in range(2):
                 past(last, cc, b_banks[cc])
-                past_copy(last, cc, "S")
-            quant_past(last, 0, 256)
+            quant_b(last, 0, HALF)
             for cs in pairs:
-                h_pass(0, cs, last - 1)
+                sum_pass(0, cs, last - 1)
             past(last, 2, b_banks[0])
-            past_copy(last, 2, "S")
             for cs in pairs[:2]:
                 finish(0, cs, "V")
             past(last, 3, b_banks[1])
-            past_copy(last, 3, "S")
             finish(0, pairs[2], "V")
             finish(0, pairs[3], "S")
-            quant_past(last, 256, C)
+            quant_b(last, HALF, C)
             for cs in pairs[:2]:
-                h_pass(1, cs, last - 1)
+                sum_pass(1, cs, last - 1)
             for g in range(2):
-                h_pass(1, pairs[2], g, b_banks[0])
+                sum_pass(1, pairs[2], g, b_banks[0])
             finish(1, pairs[0], "V")
             finish(1, pairs[1], "S")
-            h_pass(1, pairs[2], last - 1)
+            sum_pass(1, pairs[2], last - 1)
             finish(1, pairs[2], "V")
             for i, c in enumerate(pairs[3]):
                 for g in range(last):
-                    h_pass(1, (c,), g, out_banks[i])
+                    sum_pass(1, (c,), g, sum_banks[i])
                 finish(1, (c,), "SV"[i])

@@ -26,14 +26,12 @@ FP = F // N
 DP = D // N
 RT = R // P
 
-FEW, MANY, EVEN = "SVVV", "SSSV", "SSVV"
+Y_GROUPS = 3
+SLOTS = 8
+W_BUFS = 2
+AT_BUFS = RT + RT // 2 + 1
 Y_POOL = 704
 Z_STEP = 48
-
-Y_BUFS = 6
-LOAD_BUFS = 8
-Z_BUFS = 6
-AT_BUFS = RT + RT // 2 + 1
 
 
 def tile_weighted_hankel_subspace_s11_kernel(
@@ -42,14 +40,12 @@ def tile_weighted_hankel_subspace_s11_kernel(
     nc = tc.nc
     with ExitStack() as ctx:
         keep = ctx.enter_context(tc.tile_pool(name="keep", bufs=1))
-        work = ctx.enter_context(tc.tile_pool(name="work", bufs=2))
         psum = ctx.enter_context(tc.psum_pool(name="psum", bufs=1))
 
         ident = keep.tile([P, P], F32, name="ident")
         y_scale = keep.tile([P, FP, 4], F32, name="y_scale")
         lev16 = keep.tile([P, RT], BF16, name="lev16")
         rho16 = keep.tile([P, RT], BF16, name="rho16")
-        lev = keep.tile([P, RT], F32, name="lev")
         rhos = keep.tile([P, RT], F32, name="rhos")
         wcode = keep.tile([P, RT, FP, P], U32, name="wcode", align_bytes=64)
         wscale = keep.tile([P, RT, FP, P], U8, name="wscale", align_bytes=64)
@@ -70,8 +66,8 @@ def tile_weighted_hankel_subspace_s11_kernel(
         last = GROUPS - 1
         pairs = [(c, c + 1) for c in range(0, RT, 2)]
 
-        def bank_tile(bank, shape):
-            return psum.tile(shape, F32, name="bank%d" % bank)
+        def bank_tile(bank, shape, dtype=F32):
+            return psum.tile(shape, dtype, name="bank%d" % bank)
 
         def copy(eng, dst, src):
             if eng == "S":
@@ -82,26 +78,38 @@ def tile_weighted_hankel_subspace_s11_kernel(
         def pool_copy(dst, src):
             nc.gpsimd.tensor_scalar(out=dst, in0=src, scalar1=1.0, scalar2=0.0, op0=MULT, op1=ADD)
 
-        def load_y(g, f, step=4):
-            yb = work.tile([P, 4, N], U8, name="yb", bufs=Y_BUFS, align_bytes=64)
-            for t in range(0, 4, step):
-                nc.sync.dma_start(out=yb[:, t : t + step], in_=y_view[f][:, t : t + step, N * g : N * g + N])
-            tiles["yb", g, f] = yb
+        def slot_tile(slot, shape, dtype):
+            return keep.tile(shape, dtype, name="slot%d" % slot, align_bytes=64)
 
-        def load_z(g, d):
-            zr = work.tile([P, 4, N], BF16, name="zr", bufs=LOAD_BUFS, align_bytes=64)
-            nc.sync.dma_start(out=zr[:], in_=z_view[d][:, :, N * g : N * g + N])
-            tiles["zr", g, d] = zr
+        def load_scale():
+            nc.scalar.dma_start(out=y_scale[:], in_=y_f_scale.rearrange("(f p t) o -> p f (t o)", f=FP, p=P, t=4))
 
-        def load_w(pair):
-            wf = work.tile([P, 2, F], BF16, name="zr", bufs=LOAD_BUFS, align_bytes=64)
-            nc.sync.dma_start(out=wf[:], in_=w_view[:, 2 * pair : 2 * pair + 2, :])
-            tiles["wf", pair] = wf
+        def load_y(g, f, t0, t1):
+            if t0 == 0:
+                tiles["yb", g, f] = keep.tile([P, 4, N], U8, name="yb%d%d" % (g % Y_GROUPS, f), align_bytes=64)
+            nc.sync.dma_start(out=tiles["yb", g, f][:, t0:t1], in_=y_view[f][:, t0:t1, N * g : N * g + N])
+
+        def load_z(g, d, slot):
+            tiles["zr", g, d] = slot_tile(slot, [P, 4, N], BF16)
+            nc.sync.dma_start(out=tiles["zr", g, d][:], in_=z_view[d][:, :, N * g : N * g + N])
+
+        def load_w(c0, c1, slot):
+            if c0 % 2 == 0:
+                tiles["wf", c0 // 2] = slot_tile(slot, [P, 2, F], BF16)
+            nc.sync.dma_start(out=tiles["wf", c0 // 2][:, c0 % 2 : c0 % 2 + c1 - c0], in_=w_view[:, c0:c1, :])
+
+        def load_level():
+            nc.sync.dma_start(out=lev16[:], in_=level.rearrange("(p c) -> p c", c=RT))
+
+        def load_rho():
+            nc.sync.dma_start(out=rho16[:], in_=rho.rearrange("(p c) -> p c", c=RT))
 
         def load_lam(g):
-            lam_all = keep.tile([P, N], BF16, name="lam%d" % g)
-            nc.sync.dma_start(out=lam_all[:], in_=lam[N * g : N * g + N].partition_broadcast(P))
-            tiles["lam", g] = lam_all
+            tiles["lam", g] = keep.tile([P, N], BF16, name="lam%d" % g)
+            nc.sync.dma_start(out=tiles["lam", g][:], in_=lam[N * g : N * g + N].partition_broadcast(P))
+
+        def zero_scales():
+            nc.vector.memset(pws[:].rearrange("p d n -> p (d n)").bitcast(I32), 0)
 
         def load_wp():
             nc.sync.dma_start(out=pw[:], in_=w_p_words.rearrange("d p n -> p d n"))
@@ -111,26 +119,29 @@ def tile_weighted_hankel_subspace_s11_kernel(
                     in_=w_p_scales[:, 4 * q : 4 * q + 4, :].rearrange("d q n -> q d n").bitcast(I32),
                 )
 
-        def widen(g, f, engs, first=0):
-            if ("yw", g) not in tiles:
-                tiles["yw", g] = work.tile([P, FP * 4 * N], BF16, name="yw", align_bytes=64)
-            order = "p (t f n) -> p f t n" if g == last else "p (f t n) -> p f t n"
-            planes = tiles["yw", g][:].rearrange(order, t=4, f=FP)
-            for i, eng in enumerate(engs):
-                t = first + i
-                src = tiles["yb", g, f][:, t, :].bitcast(FP8)
-                s = y_scale[:, f, t : t + 1]
-                if eng == "S":
-                    nc.scalar.activation(out=planes[:, f, t, :], in_=src, func=COPY, scale=s)
-                else:
-                    nc.vector.tensor_scalar(out=planes[:, f, t, :], in0=src, scalar1=s, scalar2=None, op0=MULT)
+        def cast_rho():
+            nc.vector.tensor_copy(out=rhos[:], in_=rho16[:])
 
-        def weave_y(g, n0, n1, eng):
+        def widen(eng, g, f, t):
+            if ("yw", g) not in tiles:
+                tiles["yw", g] = keep.tile([P, FP * 4 * N], BF16, name="yw%d" % (g % 2), align_bytes=64)
+            order = "p (t f n) -> p f t n" if g == last else "p (f t n) -> p f t n"
+            plane = tiles["yw", g][:].rearrange(order, t=4, f=FP)[:, f, t, :]
+            src = tiles["yb", g, f][:, t, :].bitcast(FP8)
+            s = y_scale[:, f, t : t + 1]
+            if eng == "S":
+                nc.scalar.activation(out=plane, in_=src, func=COPY, scale=s)
+            else:
+                nc.vector.tensor_scalar(out=plane, in0=src, scalar1=s, scalar2=None, op0=MULT)
+
+        def weave_y(eng, g, n0, n1):
             dst = shared[:, 4 * n0 : 4 * n1].rearrange("p (n t) -> p n t", t=4)
             if g == last:
                 src = tiles["yw", g][:].rearrange("p (t n) -> p t n", t=4)[:, :, n0:n1]
             else:
-                src = tiles["yw", g][:, 4 * n0 : 4 * n1].rearrange("p (t n) -> p t n", t=4)
+                f = n0 // N
+                src = tiles["yw", g][:, 4 * N * f : 4 * N * (f + 1)].rearrange("p (t n) -> p t n", t=4)
+                src = src[:, :, n0 - N * f : n1 - N * f]
             if eng == "G":
                 pool_copy(dst, src.rearrange("p t n -> p n t"))
             else:
@@ -138,20 +149,20 @@ def tile_weighted_hankel_subspace_s11_kernel(
 
         def quant_y(g, n0, n1):
             if ("yc", g) not in tiles:
-                tiles["yc", g] = work.tile([P, FP * N], U32, name="yc", align_bytes=64)
-                tiles["ys", g] = work.tile([P, FP * N], U8, name="ys", align_bytes=64)
+                tiles["yc", g] = keep.tile([P, FP * N], U32, name="yc%d" % (g % 2), align_bytes=64)
+                tiles["ys", g] = keep.tile([P, FP * N], U8, name="ys%d" % (g % 2), align_bytes=64)
             nc.vector.quantize_mx(
                 out=tiles["yc", g][:, n0:n1].bitcast(FP8X4),
                 scales=tiles["ys", g][:, n0:n1],
                 in_=shared[:, 4 * n0 : 4 * n1],
             )
 
-        def weave_z(g, d, m0, m1, eng):
+        def weave_z(eng, g, d, m0, m1):
             if ("zi", g, d) not in tiles:
                 if eng == "G":
                     tiles["zi", g, d] = shared[:, 0 : 4 * N]
                 else:
-                    tiles["zi", g, d] = work.tile([P, 4 * N], BF16, name="zi", bufs=Z_BUFS, align_bytes=64)[:]
+                    tiles["zi", g, d] = keep.tile([P, 4 * N], BF16, name="zi%d%d" % (g % 2, d), align_bytes=64)[:]
             dst = tiles["zi", g, d].rearrange("p (s m j) -> p s m j", s=4, j=4)
             src = tiles["zr", g, d][:]
             if eng == "G":
@@ -162,27 +173,27 @@ def tile_weighted_hankel_subspace_s11_kernel(
                 src = src.rearrange("p (h e) (m s) -> p m h s e", e=2, s=4)[:, m0:m1]
                 copy(eng, dst, src)
 
-        def quant_z(g, order):
-            tiles["zc", g] = work.tile([P, DP, N], U32, name="zc", align_bytes=64)
-            tiles["zs", g] = work.tile([P, DP, N], U8, name="zs", align_bytes=64)
-            for d in order:
-                nc.vector.quantize_mx(
-                    out=tiles["zc", g][:, d].bitcast(FP8X4), scales=tiles["zs", g][:, d], in_=tiles["zi", g, d]
-                )
+        def quant_z(g, d):
+            if ("zc", g) not in tiles:
+                tiles["zc", g] = keep.tile([P, DP, N], U32, name="zc%d" % (g % 2), align_bytes=64)
+                tiles["zs", g] = keep.tile([P, DP, N], U8, name="zs%d" % (g % 2), align_bytes=64)
+            nc.vector.quantize_mx(
+                out=tiles["zc", g][:, d].bitcast(FP8X4), scales=tiles["zs", g][:, d], in_=tiles["zi", g, d]
+            )
 
-        def w_turn(pair):
-            for c in pairs[pair]:
-                wt = bank_tile(4 + c % 4, [P, FP, 2, P])
-                words = tiles["wf", pair][:, c % 2, :].bitcast(F32)
-                for f in range(FP):
-                    for u in range(2):
-                        nc.tensor.transpose(wt[:, f, u, :], words[:, 256 * f + u : 256 * (f + 1) : 2], ident[:])
-                tiles["wt", c] = wt
+        def w_turn(c, bank):
+            wt = bank_tile(bank, [P, FP, 2, P])
+            words = tiles["wf", c // 2][:, c % 2, :].bitcast(F32)
+            for f in range(FP):
+                for u in range(2):
+                    nc.tensor.transpose(wt[:, f, u, :], words[:, 256 * f + u : 256 * (f + 1) : 2], ident[:])
+            tiles["wt", c] = wt
 
-        def w_copy(pair):
-            tiles["wi", pair] = work.tile([P, 2, FP, P, 2], F32, name="wi", align_bytes=64)
-            for c in pairs[pair]:
-                copy("S", tiles["wi", pair][:, c % 2], tiles["wt", c][:].rearrange("p f u r -> p f r u"))
+        def w_copy(eng, c):
+            if c % 2 == 0:
+                name = "wi%d" % (c // 2 % W_BUFS)
+                tiles["wi", c // 2] = keep.tile([P, 2, FP, P, 2], F32, name=name, align_bytes=64)
+            copy(eng, tiles["wi", c // 2][:, c % 2], tiles["wt", c][:].rearrange("p f u r -> p f r u"))
 
         def w_quant(pair):
             nc.vector.quantize_mx(
@@ -205,11 +216,11 @@ def tile_weighted_hankel_subspace_s11_kernel(
                 )
 
         def epilogue(g, c):
-            at = work.tile([P, N], BF16, name="at", bufs=AT_BUFS, align_bytes=64)
+            at = keep.tile([P, N], BF16, name="at%d" % ((RT * g + c) % AT_BUFS), align_bytes=64)
             nc.vector.scalar_tensor_tensor(
                 out=at[:].rearrange("p (u q) -> p u q", u=2),
                 in0=tiles["fp", g, c][:].rearrange("p (q u) -> p u q", u=2),
-                scalar=lev[:, c : c + 1],
+                scalar=lev16[:, c : c + 1],
                 in1=tiles["lam", g][:].rearrange("p (q u) -> p u q", u=2),
                 op0=ADD,
                 op1=MULT,
@@ -224,17 +235,17 @@ def tile_weighted_hankel_subspace_s11_kernel(
                     nc.tensor.transpose(tp[:, i, u, :], words[:, P * u : P * u + P], ident[:])
             tiles["tp", g, pair] = tp
 
-        def a_copy(g, pair):
-            if pair == 0:
-                tiles["ai", g] = work.tile([P, RT, P, 2], F32, name="ai", bufs=GROUPS, align_bytes=64)
+        def a_copy(eng, g, pair):
+            if ("ai", g) not in tiles:
+                tiles["ai", g] = keep.tile([P, RT, P, 2], F32, name="ai%d" % g, align_bytes=64)
             dst = tiles["ai", g][:, 2 * pair : 2 * pair + 2]
-            copy("S", dst, tiles["tp", g, pair][:].rearrange("p c u r -> p c r u"))
+            copy(eng, dst, tiles["tp", g, pair][:].rearrange("p c u r -> p c r u"))
 
-        def quant_a(g):
+        def quant_a(g, p0, p1):
             nc.vector.quantize_mx(
-                out=acode[:, g].bitcast(FP8X4),
-                scales=ascale[:, g],
-                in_=tiles["ai", g][:].rearrange("p c r u -> p (c r u)").bitcast(BF16),
+                out=acode[:, g, 2 * P * p0 : 2 * P * p1].bitcast(FP8X4),
+                scales=ascale[:, g, 2 * P * p0 : 2 * P * p1],
+                in_=tiles["ai", g][:, 2 * p0 : 2 * p1].rearrange("p c r u -> p (c r u)").bitcast(BF16),
             )
 
         def past(g, cc, bank):
@@ -250,9 +261,12 @@ def tile_weighted_hankel_subspace_s11_kernel(
                         start=(d == 0),
                         stop=(d == DP - 1),
                     )
-            if cc == 0:
-                tiles["pi", g] = work.tile([P, C, 4], BF16, name="pi", align_bytes=64)
-            copy("S", tiles["pi", g][:, P * cc : P * cc + P, :], pp[:].rearrange("p s n -> p n s"))
+            tiles["pp", g, cc] = pp
+
+        def b_copy(eng, g, cc):
+            if ("pi", g) not in tiles:
+                tiles["pi", g] = keep.tile([P, C, 4], BF16, name="pi%d" % (g % 2), align_bytes=64)
+            copy(eng, tiles["pi", g][:, P * cc : P * cc + P, :], tiles["pp", g, cc][:].rearrange("p s n -> p n s"))
 
         def quant_b(g, n0, n1):
             nc.vector.quantize_mx(
@@ -261,7 +275,7 @@ def tile_weighted_hankel_subspace_s11_kernel(
                 in_=tiles["pi", g][:, n0:n1, :].rearrange("p n s -> p (n s)"),
             )
 
-        def sum_pass(half, cs, g, bank=None):
+        def sum_pass(half, cs, g, bank):
             if g == 0:
                 tiles["h", half, cs] = bank_tile(bank, [P, len(cs), HALF])
             for i, c in enumerate(cs):
@@ -275,206 +289,215 @@ def tile_weighted_hankel_subspace_s11_kernel(
                     stop=(g == last and i == len(cs) - 1),
                 )
 
-        def finish(half, cs, eng):
-            sum_pass(half, cs, last)
-            step = 1 if half else len(cs)
-            for i0 in range(0, len(cs), step):
-                ho = work.tile([P, step, HALF], F32, name="zr", bufs=LOAD_BUFS, align_bytes=64)
-                for i in range(step):
-                    src = tiles["h", half, cs][:, i0 + i, :]
-                    s = rhos[:, cs[i0 + i] : cs[i0 + i] + 1]
-                    if eng == "S":
-                        nc.scalar.activation(out=ho[:, i, :], in_=src, func=COPY, scale=s)
-                    else:
-                        nc.vector.tensor_scalar(out=ho[:, i, :], in0=src, scalar1=s, scalar2=None, op0=MULT)
-                rows = out_view[:, cs[i0] : cs[i0] + step, HALF * half : HALF * half + HALF]
-                nc.sync.dma_start(out=rows, in_=ho[:])
+        def scale_out(eng, half, cs, i, slot):
+            if ("ho", slot) not in tiles:
+                tiles["ho", slot] = slot_tile(slot % SLOTS, [P, 2, HALF], F32)
+            src = tiles["h", half, cs][:, i, :]
+            dst = tiles["ho", slot][:, i, :]
+            s = rhos[:, cs[i] : cs[i] + 1]
+            if eng == "S":
+                nc.scalar.activation(out=dst, in_=src, func=COPY, scale=s)
+            else:
+                nc.vector.tensor_scalar(out=dst, in0=src, scalar1=s, scalar2=None, op0=MULT)
+
+        def store(half, cs, i0, i1, slot):
+            rows = out_view[:, cs[i0] : cs[i1 - 1] + 1, HALF * half : HALF * half + HALF]
+            nc.sync.dma_start(out=rows, in_=tiles["ho", slot][:, i0:i1])
+
+        def planes(eng, g, f, ts):
+            return [(widen, eng, g, f, t) for t in ts]
+
+        def epilogues(first, count):
+            return [(epilogue, i // RT, i % RT) for i in range(first, first + count)]
+
+        def futures(first, banks):
+            return [(future, (first + i) // RT, (first + i) % RT, b) for i, b in enumerate(banks)]
+
+        def finish(eng, half, cs, slot, step):
+            return [(scale_out, eng, half, cs, i, slot) for i in range(len(cs))]
+
+        def w_turns(pair, bank):
+            return [(w_turn, c, bank + c % 2) for c in pairs[pair]]
+
+        def w_copies(pair):
+            return [(w_copy, "S", c) for c in pairs[pair]]
+
+        def a_turns(g, ps, banks):
+            return [(a_turn, g, p, b) for p, b in zip(ps, banks)]
+
+        def a_copies(g, ps):
+            return [(a_copy, "S", g, p) for p in ps]
+
+        def quants_z(g, order):
+            return [(quant_z, g, d) for d in order]
+
+        sync = [(load_y, 0, 0, 0, 2), (load_y, 0, 0, 2, 4), (load_y, 0, 1, 0, 4), (load_w, 0, 1, 0), (load_w, 1, 2, 0), (load_y, 1, 0, 0, 4)]
+        sync += [(load_w, 2, 4, 1), (load_w, 4, 6, 2), (load_y, 1, 1, 0, 4), (load_w, 6, 8, 3)]
+        sync += [(load_y, 2, 0, 0, 4), (load_level,), (load_lam, 0), (load_y, 2, 1, 0, 4), (load_y, 3, 0, 0, 4), (load_y, 3, 1, 0, 4)]
+        sync += [(load_lam, g) for g in range(1, GROUPS)]
+        zs = [(0, 2), (0, 0), (0, 1)] + [(g, d) for g in (1, 2) for d in range(DP)] + [(last, d) for d in range(DP)]
+        zl = [(load_z, g, d, (4 + i) % SLOTS) for i, (g, d) in enumerate(zs)]
+        sync += zl[:3] + [(load_wp,), (load_rho,)] + zl[3:]
+
+        b_banks = (6, 7, 5)
+        sums = [(0, cs) for cs in pairs] + [(1, pairs[0])]
+        sum_banks = (2, 3, 0, 1, 4)
+        ends = [("V", 0, pairs[0]), ("S", 0, pairs[1]), ("V", 0, pairs[2]), ("S", 0, pairs[3])]
+        ends += [("V", 1, pairs[0]), ("S", 1, pairs[1]), ("V", 1, pairs[2]), ("S", 1, (6,)), ("V", 1, (7,))]
+        outs = [[(scale_out, e, h, cs, i, k) for i in range(len(cs))] for k, (e, h, cs) in enumerate(ends)]
+        for k, (e, h, cs) in enumerate(ends):
+            sync += [(store, h, cs, i, i + 1, k) for i in range(len(cs))] if k > 5 else [(store, h, cs, 0, 2, k)]
+
+        vector = [(zero_scales,)] + planes("V", 0, 0, (1, 2, 3)) + [(weave_y, "V", 0, 0, N)] + planes("V", 0, 1, (3,))
+        vector += [(quant_y, 0, 0, N), (weave_y, "V", 0, N, 2 * N), (w_quant, 0), (quant_y, 0, N, 2 * N)]
+        vector += planes("V", 1, 0, (3,)) + planes("V", 1, 1, (2, 3)) + [(weave_y, "V", 1, 0, N), (w_quant, 1)]
+        vector += [(weave_y, "V", 1, N, 2 * N), (w_quant, 2), (quant_y, 1, 0, N), (w_quant, 3), (quant_y, 1, N, 2 * N)]
+        vector += epilogues(0, 12) + [(quant_y, 2, 0, N), (quant_y, 2, N, N + N // 2), (quant_y, 2, N + N // 2, 2 * N)]
+        vector += epilogues(12, 8) + [(quant_y, 3, 0, N), (quant_y, 3, N, 2 * N)]
+        vector += epilogues(20, 6) + quants_z(0, (2, 0, 1))
+        vector += epilogues(26, 6) + [(weave_z, "V", 1, 2, 0, P)] + quants_z(1, (0, 1, 2))
+        over = {2: 0, last: 4 * Z_STEP - P}
+        for g in (1, 2):
+            vector += [(quant_a, g - 1, 0, 4), (quant_b, g - 1, 0, HALF), (weave_z, "V", g + 1, 2, 0, P), (quant_b, g - 1, HALF, C)]
+            vector += [(weave_z, "V", g + 1, 1, over[g + 1], P)] + quants_z(g + 1, (2, 1, 0))
+        vector += [(quant_a, 2, 0, 4), (quant_b, 2, 0, C), (quant_a, 3, 0, 4), (cast_rho,), (quant_b, 3, 0, HALF)]
+        vector += outs[0] + [(quant_b, 3, HALF, C)] + outs[2] + outs[4] + outs[6] + outs[8]
+
+        scalar = [(load_scale,)] + planes("S", 0, 0, (0,)) + planes("S", 0, 1, (0, 1, 2)) + w_copies(0)
+        scalar += planes("S", 1, 0, (0, 1, 2)) + w_copies(1) + planes("S", 1, 1, (0, 1)) + w_copies(2)
+        scalar += planes("S", 2, 0, (0,)) + w_copies(3) + planes("S", 2, 0, (1, 2, 3)) + planes("S", 2, 1, range(4))
+        scalar += planes("S", 3, 0, range(4)) + planes("S", 3, 1, (0, 1)) + a_copies(0, (0,)) + planes("S", 3, 1, (2, 3))
+        scalar += a_copies(0, (1, 2, 3)) + [(weave_y, "S", 3, Y_POOL, 2 * N), (weave_z, "S", 0, 2, 0, P)] + a_copies(1, range(4))
+        scalar += [(weave_z, "S", 0, 1, 0, P)] + a_copies(2, range(4))
+        scalar += [(weave_z, "S", 1, 1, 0, P)] + [(b_copy, "S", 0, cc) for cc in range(3)] + a_copies(3, range(4))
+        scalar += [(b_copy, "S", 0, 3), (weave_z, "S", 2, 0, 0, 80), (b_copy, "S", 1, 0), (weave_z, "S", 2, 0, 80, P)]
+        scalar += [(b_copy, "S", 1, 1), (b_copy, "S", 1, 2), (weave_z, "S", 3, 1, 0, 64), (b_copy, "S", 1, 3)]
+        scalar += [(weave_z, "S", 3, 0, 0, 80), (b_copy, "S", 2, 0), (weave_z, "S", 3, 0, 80, P)]
+        scalar += [(b_copy, "S", 2, cc) for cc in (1, 2, 3)]
+        scalar += [(b_copy, "S", 3, cc) for cc in range(4)] + outs[1] + outs[3] + outs[5] + outs[7]
+
+        gpsimd = [(weave_y, "G", 2, 0, N), (weave_y, "G", 2, N, 2 * N), (weave_y, "G", 3, 0, Y_POOL)]
+        gpsimd += [(weave_z, "G", 0, 0, 0, P), (weave_z, "G", 1, 0, 0, P)]
+
+        tensor = w_turns(0, 4) + w_turns(1, 6) + w_turns(2, 4) + futures(0, (0,)) + w_turns(3, 6)
+        tensor += futures(1, range(1, 8)) + futures(8, range(4)) + a_turns(0, (0, 1), (4, 5)) + futures(12, (6, 7))
+        tensor += a_turns(0, (2, 3), (0, 1)) + futures(14, (2, 3)) + futures(16, (4, 5, 6, 7)) + a_turns(1, range(4), range(4))
+        tensor += futures(20, (4, 5, 6, 7)) + futures(24, range(4)) + a_turns(2, range(4), (4, 5, 6, 7)) + futures(28, (0, 1, 4, 5))
+        tensor += [(past, 0, 0, 6), (past, 0, 1, 7), (past, 0, 2, 2)] + a_turns(3, range(4), (3, 0, 1, 4)) + [(past, 0, 3, 5)]
+        def summed(i, g):
+            return (sum_pass,) + sums[i] + (g, sum_banks[i])
+        for g in (1, 2):
+            for cc in range(4):
+                tensor += [(past, g, cc, b_banks[(4 * g + cc - 4) % 3])]
+                tensor += [summed(i, g - 1) for i in ((), (0,), (1, 2), (3, 4))[cc]]
+        tensor += [(past, 3, 0, 5), (past, 3, 1, 6), (past, 3, 2, 7), summed(0, 2), (past, 3, 3, 5), summed(0, 3)]
+        for i in range(1, 5):
+            tensor += [summed(i, 2), summed(i, 3)]
+        for cs, bank in ((pairs[1], 6), (pairs[2], 7), ((6,), 5), ((7,), 2)):
+            tensor += [(sum_pass, 1, cs, g, bank) for g in range(GROUPS)]
+
+        steps = sync + vector + scalar + gpsimd + tensor
+
+        def every(fn, test):
+            return [s for s in steps if s[0] == fn and test(*s[1:])]
+
+        def before(step, same):
+            order = sync + tensor
+            ahead = [s for s in order[: order.index(step)] if same(s)]
+            return ahead[-1:]
+
+        def bank_users(step):
+            fn = step[0]
+            if fn == w_turn:
+                return every(w_copy, lambda e, c: c == step[1])
+            if fn == future:
+                return [(epilogue,) + step[1:3]]
+            if fn == a_turn:
+                return every(a_copy, lambda e, g, p: (g, p) == step[1:3])
+            if fn == past:
+                return every(b_copy, lambda e, g, cc: (g, cc) == step[1:3])
+            return every(scale_out, lambda e, h, cs, i, sl: (h, cs) == step[1:3])
+
+        def slot_users(step):
+            if step[0] == load_w:
+                return every(w_turn, lambda c, b: c // 2 == step[1] // 2)
+            return every(weave_z, lambda e, g, d, m0, m1: (g, d) == step[1:3])
+
+        def shared_readers(step, n0, n1):
+            g = step[2] + (GROUPS if step[0] == weave_z else 0)
+            ys = every(quant_y, lambda h, a, b: h < g and a < n1 and n0 < b)
+            zs = [(quant_z, s[2], s[3]) for s in gpsimd if s[0] == weave_z and s[2] + GROUPS < g]
+            return ys + zs
+
+        def needs(step):
+            fn, a = step[0], step[1:]
+            got = []
+            if step in tensor and (fn != sum_pass or a[2] == 0):
+                for s in before(step, lambda s: s in tensor and s[-1] == a[-1]):
+                    got = got + bank_users(s)
+            if fn == load_z:
+                for s in before(step, lambda s: s[0] in (load_w, load_z) and s[-1] == a[-1]):
+                    got = got + slot_users(s)
+            if fn == load_y:
+                got = got + every(widen, lambda e, g, f, t: (g, f) == (a[0] - Y_GROUPS, a[1]))
+            if fn == load_wp:
+                got = got + [(zero_scales,)]
+            if fn == cast_rho:
+                got = got + [(load_rho,)]
+            if fn == widen:
+                got = got + [(load_scale,)] + every(load_y, lambda g, f, t0, t1: (g, f) == a[1:3] and t0 <= a[3])
+                got = got + every(weave_y, lambda e, g, n0, n1: g == a[1] - 2)
+            if fn == weave_y:
+                got = got + every(widen, lambda e, g, f, t: g == a[1] and a[2] < N * f + N and N * f < a[3])
+                got = got + shared_readers(step, a[2], a[3])
+            if fn == quant_y:
+                got = got + every(weave_y, lambda e, g, n0, n1: g == a[0] and n0 < a[2] and a[1] < n1)
+                got = got + every(future, lambda g, c, b: g == a[0] - 2)
+            if fn == weave_z:
+                got = got + every(load_z, lambda g, d, sl: (g, d) == a[1:3])
+                got = got + (shared_readers(step, 0, N) if a[0] == "G" else every(quant_z, lambda g, d: (g, d) == (a[1] - 2, a[2])))
+            if fn == quant_z:
+                got = got + every(weave_z, lambda e, g, d, m0, m1: (g, d) == a) + every(past, lambda g, cc, b: g == a[0] - 2)
+            if fn == w_turn:
+                got = got + every(load_w, lambda c0, c1, sl: c0 <= a[0] < c1)
+            if fn == w_copy:
+                got = got + every(w_turn, lambda c, b: c == a[1]) + every(w_quant, lambda p: p == a[1] // 2 - W_BUFS)
+            if fn == w_quant:
+                got = got + every(w_copy, lambda e, c: c // 2 == a[0])
+            if fn == future:
+                got = got + [(w_quant, a[1] // 2)] + every(quant_y, lambda g, n0, n1: g == a[0])
+            if fn == epilogue:
+                got = got + every(future, lambda g, c, b: (g, c) == a) + [(load_level,), (load_lam, a[0])]
+                got = got + every(a_turn, lambda g, p, b: (RT * g + 2 * p) // 2 == (RT * a[0] + a[1] - AT_BUFS) // 2)
+            if fn == a_turn:
+                got = got + [(epilogue, a[0], c) for c in pairs[a[1]]]
+            if fn == a_copy:
+                got = got + every(a_turn, lambda g, p, b: (g, p) == a[1:3])
+            if fn == quant_a:
+                got = got + every(a_copy, lambda e, g, p: g == a[0] and a[1] <= p < a[2])
+            if fn == past:
+                got = got + [(load_wp,)] + every(quant_z, lambda g, d: g == a[0])
+            if fn == b_copy:
+                got = got + every(past, lambda g, cc, b: (g, cc) == a[1:3]) + every(quant_b, lambda g, n0, n1: g == a[1] - 2)
+            if fn == quant_b:
+                got = got + every(b_copy, lambda e, g, cc: g == a[0] and a[1] <= P * cc < a[2])
+            if fn == sum_pass:
+                got = got + every(quant_a, lambda g, p0, p1: g == a[2] and p0 <= a[1][0] // 2 < p1)
+                got = got + every(quant_b, lambda g, n0, n1: g == a[2] and n0 <= HALF * a[0] < n1)
+            if fn == scale_out:
+                got = got + [(cast_rho,)] + every(sum_pass, lambda h, cs, g, b: (h, cs) == a[1:3])
+                got = got + [s for z in every(load_z, lambda g, d, sl: sl == a[4] % SLOTS) for s in slot_users(z)]
+                got = got + every(store, lambda h, cs, i0, i1, sl: sl == a[4] - SLOTS)
+            if fn == store:
+                got = got + every(scale_out, lambda e, h, cs, i, sl: (h, cs) == a[0:2] and a[2] <= i < a[3])
+            return got
 
         with tc.manual_schedule():
             make_identity(nc, ident[:])
-            nc.vector.memset(pws[:].rearrange("p d n -> p (d n)").bitcast(I32), 0)
-
-            nc.scalar.dma_start(out=y_scale[:], in_=y_f_scale.rearrange("(f p t) o -> p f (t o)", f=FP, p=P, t=4))
-            load_y(0, 0, 2)
-            load_y(0, 1)
-            load_w(0)
-            load_y(1, 0)
-            load_w(1)
-            load_w(2)
-            load_y(1, 1)
-            load_w(3)
-            nc.sync.dma_start(out=lev16[:], in_=level.rearrange("(p c) -> p c", c=RT))
-            nc.sync.dma_start(out=rho16[:], in_=rho.rearrange("(p c) -> p c", c=RT))
-            load_y(2, 0)
-            load_lam(0)
-            load_y(2, 1)
-
-            widen(0, 0, FEW)
-            weave_y(0, 0, N, "V")
-            widen(0, 1, MANY)
-            quant_y(0, 0, N)
-            weave_y(0, N, 2 * N, "V")
-            for f in range(FP):
-                load_y(last, f)
-            for g in range(1, GROUPS):
-                load_lam(g)
-            for d in (2, 0, 1):
-                load_z(0, d)
-            load_wp()
-            load_z(1, 0)
-            w_turn(0)
-            w_copy(0)
-            w_quant(0)
-            quant_y(0, N, 2 * N)
-            widen(1, 0, MANY)
-            w_turn(1)
-            w_copy(1)
-            widen(1, 1, EVEN)
-            weave_y(1, 0, N, "V")
-            w_quant(1)
-            nc.vector.tensor_copy(out=lev[:], in_=lev16[:])
-            nc.vector.tensor_copy(out=rhos[:], in_=rho16[:])
-            w_turn(2)
-            w_copy(2)
-            future(0, 0, 0)
-            w_turn(3)
-            weave_y(1, N, 2 * N, "V")
-            w_quant(2)
-            widen(2, 0, "S")
-            w_copy(3)
-            quant_y(1, 0, N)
-            w_quant(3)
-            quant_y(1, N, 2 * N)
-
-            widen(2, 0, "SSS", 1)
-            weave_y(2, 0, N, "G")
-            widen(2, 1, "SSSS")
-            weave_y(2, N, 2 * N, "G")
-            for c in range(RT):
-                if c > 0:
-                    future(0, c, c)
-                epilogue(0, c)
-            for g, d in ((1, 1), (1, 2), (2, 0), (2, 1)):
-                load_z(g, d)
-            for c in range(4):
-                future(1, c, c)
-                epilogue(1, c)
-            for pair, bank in enumerate((4, 5, 0, 1)):
-                a_turn(0, pair, bank)
-                if pair == 1:
-                    for c in pairs[2]:
-                        future(1, c, c + 2)
-            widen(last, 0, "SSSS")
-            widen(last, 1, "SS")
-            a_copy(0, 0)
-            widen(last, 1, "SS", 2)
-            for pair in range(1, 4):
-                a_copy(0, pair)
-            for c in pairs[3]:
-                future(1, c, c - 4)
-            for n0, n1 in ((0, N), (N, N + N // 2), (N + N // 2, 2 * N)):
-                quant_y(2, n0, n1)
-
-            weave_y(last, 0, Y_POOL, "G")
-            weave_y(last, Y_POOL, 2 * N, "S")
-            weave_z(0, 2, 0, P, "S")
-            for c in range(4, RT):
-                epilogue(1, c)
-            for c in range(4):
-                future(2, c, 4 + c)
-                epilogue(2, c)
-            for pair in range(4):
-                a_turn(1, pair, pair)
-            for pair in range(4):
-                a_copy(1, pair)
-            for c in range(4, RT):
-                future(2, c, c)
-            for f in range(FP):
-                quant_y(last, N * f, N * f + N)
-
-            weave_z(0, 0, 0, P, "G")
-            weave_z(0, 1, 0, P, "S")
-            for c in range(4, RT):
-                epilogue(2, c)
-            for c in range(4):
-                future(last, c, c)
-                if c < 2:
-                    epilogue(last, c)
-            for pair in range(4):
-                a_turn(2, pair, 4 + pair)
-            for pair in range(4):
-                a_copy(2, pair)
-            for c, bank in zip(range(4, RT), (0, 1, 4, 5)):
-                future(last, c, bank)
-            quant_z(0, (2, 0, 1))
-            weave_z(1, 0, 0, P, "G")
-            weave_z(1, 1, 0, 2 * Z_STEP, "S")
-            for c in range(2, RT):
-                epilogue(last, c)
-            load_z(2, 2)
-            for d in range(2):
-                load_z(last, d)
-
-            rest = (P - 2 * Z_STEP) // 2
-            for cc, bank in enumerate((6, 7, 2)):
-                past(0, cc, bank)
-                if cc < 2:
-                    weave_z(1, 1, 2 * Z_STEP + rest * cc, 2 * Z_STEP + rest * (cc + 1), "S")
-            for pair, bank in enumerate((3, 0, 1, 4)):
-                a_turn(last, pair, bank)
-                a_copy(last, pair)
-            past(0, 3, 5)
-            weave_z(1, 2, 0, P, "V")
-            quant_z(1, range(DP))
-            load_z(last, 2)
-
-            b_banks = (6, 7)
-            sums = [(0, cs) for cs in pairs] + [(1, cs) for cs in pairs[:2]]
-            sum_banks = (2, 3, 0, 1, 4, 5)
-            over = {2: 0, last: 4 * Z_STEP - P}
-            steps = [(2, Z_STEP * i) for i in range(3)] + [(last, Z_STEP * i) for i in range(4)]
-            for g in range(1, last):
-                quant_a(g - 1)
-                quant_b(g - 1, 0, HALF)
-                weave_z(g + 1, 2, 0, P, "V")
-                quant_b(g - 1, HALF, C)
-                for cc in range(4):
-                    for gz, lo in steps[4 * (g - 1) + cc : 4 * (g - 1) + cc + 1]:
-                        hi, cut = lo + Z_STEP, over[gz]
-                        if lo < cut:
-                            weave_z(gz, 1, lo, min(hi, cut), "S")
-                        if hi > cut:
-                            weave_z(gz, 0, max(lo, cut) - cut, min(hi - cut, P), "S")
-                    past(g, cc, b_banks[cc % 2])
-                    for i in range(max(2 * cc - 2, 0), 2 * cc):
-                        sum_pass(sums[i][0], sums[i][1], g - 1, sum_banks[i])
-                weave_z(g + 1, 1, over[g + 1], P, "V")
-                quant_z(g + 1, (2, 1, 0))
-
-            quant_a(last - 1)
-            quant_b(last - 1, 0, C)
-            quant_a(last)
-            for cc in range(2):
-                past(last, cc, b_banks[cc])
-            quant_b(last, 0, HALF)
-            for cs in pairs:
-                sum_pass(0, cs, last - 1)
-            past(last, 2, b_banks[0])
-            for cs in pairs[:2]:
-                finish(0, cs, "V")
-            past(last, 3, b_banks[1])
-            finish(0, pairs[2], "V")
-            finish(0, pairs[3], "S")
-            quant_b(last, HALF, C)
-            for cs in pairs[:2]:
-                sum_pass(1, cs, last - 1)
-            for g in range(2):
-                sum_pass(1, pairs[2], g, b_banks[0])
-            finish(1, pairs[0], "V")
-            finish(1, pairs[1], "S")
-            sum_pass(1, pairs[2], last - 1)
-            finish(1, pairs[2], "V")
-            for i, c in enumerate(pairs[3]):
-                for g in range(last):
-                    sum_pass(1, (c,), g, sum_banks[i])
-                finish(1, (c,), "SV"[i])
+            queues = [list(q) for q in (sync, vector, scalar, gpsimd, tensor)]
+            done = []
+            while any(queues):
+                ready = [q for q in queues if q and all(s in done for s in needs(q[0]))]
+                step = ready[0].pop(0)
+                step[0](*step[1:])
+                done.append(step)

@@ -356,7 +356,7 @@ def tile_weighted_hankel_subspace_s11_kernel(
         vector += epilogues(12, 8) + [(quant_y, 3, 0, N), (quant_y, 3, N, 2 * N)]
         vector += epilogues(20, 6) + quants_z(0, (2, 0, 1))
         vector += epilogues(26, 6) + [(weave_z, "V", 1, 2, 0, P)] + quants_z(1, (0, 1, 2))
-        over = {2: 0, last: 4 * Z_STEP - P}
+        over = {2: 32, last: 80}
         for g in (1, 2):
             vector += [(quant_a, g - 1, 0, 4), (quant_b, g - 1, 0, HALF), (weave_z, "V", g + 1, 2, 0, P), (quant_b, g - 1, HALF, C)]
             vector += [(weave_z, "V", g + 1, 1, over[g + 1], P)] + quants_z(g + 1, (2, 1, 0))
@@ -369,10 +369,10 @@ def tile_weighted_hankel_subspace_s11_kernel(
         scalar += planes("S", 3, 0, range(4)) + planes("S", 3, 1, (0, 1)) + a_copies(0, (0,)) + planes("S", 3, 1, (2, 3))
         scalar += a_copies(0, (1, 2, 3)) + [(weave_y, "S", 3, Y_POOL, 2 * N), (weave_z, "S", 0, 2, 0, P)] + a_copies(1, range(4))
         scalar += [(weave_z, "S", 0, 1, 0, P)] + a_copies(2, range(4))
-        scalar += [(weave_z, "S", 1, 1, 0, P)] + [(b_copy, "S", 0, cc) for cc in range(3)] + a_copies(3, range(4))
-        scalar += [(b_copy, "S", 0, 3), (weave_z, "S", 2, 0, 0, 80), (b_copy, "S", 1, 0), (weave_z, "S", 2, 0, 80, P)]
-        scalar += [(b_copy, "S", 1, 1), (b_copy, "S", 1, 2), (weave_z, "S", 3, 1, 0, 64), (b_copy, "S", 1, 3)]
-        scalar += [(weave_z, "S", 3, 0, 0, 80), (b_copy, "S", 2, 0), (weave_z, "S", 3, 0, 80, P)]
+        scalar += [(weave_z, "S", 1, 1, 0, P), (b_copy, "S", 0, 0), (weave_z, "S", 2, 0, 0, 32), (b_copy, "S", 0, 1), (b_copy, "S", 0, 2)] + a_copies(3, range(4))
+        scalar += [(b_copy, "S", 0, 3), (weave_z, "S", 2, 0, 32, 112), (b_copy, "S", 1, 0), (weave_z, "S", 2, 0, 112, P), (weave_z, "S", 2, 1, 0, 32)]
+        scalar += [(b_copy, "S", 1, 1), (b_copy, "S", 1, 2), (weave_z, "S", 3, 1, 0, 80), (b_copy, "S", 1, 3)]
+        scalar += [(weave_z, "S", 3, 0, 0, 64), (b_copy, "S", 2, 0), (weave_z, "S", 3, 0, 64, P)]
         scalar += [(b_copy, "S", 2, cc) for cc in (1, 2, 3)]
         scalar += [(b_copy, "S", 3, cc) for cc in range(4)] + outs[1] + outs[3] + outs[5] + outs[7]
 

@@ -65,6 +65,7 @@ def tile_weighted_hankel_subspace_s11_kernel(
         tiles = {}
         last = GROUPS - 1
         pairs = [(c, c + 1) for c in range(0, RT, 2)]
+        z_order = [(2, 0, 1), (0, 1, 2), (2, 1, 0), (2, 1, 0)]
 
         def bank_tile(bank, shape, dtype=F32):
             return psum.tile(shape, dtype, name="bank%d" % bank)
@@ -248,20 +249,22 @@ def tile_weighted_hankel_subspace_s11_kernel(
                 in_=tiles["ai", g][:, 2 * p0 : 2 * p1].rearrange("p c r u -> p (c r u)").bitcast(BF16),
             )
 
-        def past(g, cc, bank):
-            pp = bank_tile(bank, [P, 4, P])
-            for s in range(4):
-                for d in range(DP):
+        def past(g, cc, i0, i1, bank):
+            if i0 == 0:
+                tiles["pp", g, cc] = bank_tile(bank, [P, 4, P])
+            pp = tiles["pp", g, cc]
+            for i in range(i0, i1):
+                d = z_order[g][i]
+                for s in range(4):
                     nc.tensor.matmul_mx(
                         out=pp[:, 2 * (s % 2) + s // 2, :],
                         lhsT=tiles["zc", g][:, d, P * s : P * s + P].bitcast(FP8X4),
                         lhsT_scale=tiles["zs", g][:, d, P * s : P * s + P],
                         rhs=pw[:, d, 2 * P * cc : 2 * P * (cc + 1)].bitcast(FP4X4),
                         rhs_scale=pws[:, d, P * cc : P * cc + P],
-                        start=(d == 0),
-                        stop=(d == DP - 1),
+                        start=(i == 0 and s == 0),
+                        stop=(i == DP - 1 and s == 3),
                     )
-            tiles["pp", g, cc] = pp
 
         def b_copy(eng, g, cc):
             if ("pi", g) not in tiles:
@@ -360,7 +363,7 @@ def tile_weighted_hankel_subspace_s11_kernel(
         for g in (1, 2):
             vector += [(quant_a, g - 1, 0, 4), (quant_b, g - 1, 0, HALF), (weave_z, "V", g + 1, 2, 0, P), (quant_b, g - 1, HALF, C)]
             vector += [(weave_z, "V", g + 1, 1, over[g + 1], P)] + quants_z(g + 1, (2, 1, 0))
-        vector += [(quant_a, 2, 0, 4), (quant_b, 2, 0, C), (quant_a, 3, 0, 4), (cast_rho,), (quant_b, 3, 0, HALF)]
+        vector += [(quant_a, 2, 0, 4), (quant_b, 2, 0, HALF), (quant_a, 3, 0, 4), (quant_b, 3, 0, HALF), (cast_rho,), (quant_b, 2, HALF, C)]
         vector += outs[0] + [(quant_b, 3, HALF, C)] + outs[2] + outs[4] + outs[6] + outs[8]
 
         scalar = [(load_scale,)] + planes("S", 0, 0, (0,)) + planes("S", 0, 1, (0, 1, 2)) + w_copies(0)
@@ -372,8 +375,8 @@ def tile_weighted_hankel_subspace_s11_kernel(
         scalar += [(weave_z, "S", 1, 1, 0, P), (b_copy, "S", 0, 0), (weave_z, "S", 2, 0, 0, 32), (b_copy, "S", 0, 1), (b_copy, "S", 0, 2)] + a_copies(3, range(4))
         scalar += [(b_copy, "S", 0, 3), (weave_z, "S", 2, 0, 32, 112), (b_copy, "S", 1, 0), (weave_z, "S", 2, 0, 112, P), (weave_z, "S", 2, 1, 0, 32)]
         scalar += [(b_copy, "S", 1, 1), (b_copy, "S", 1, 2), (weave_z, "S", 3, 1, 0, 80), (b_copy, "S", 1, 3)]
-        scalar += [(weave_z, "S", 3, 0, 0, 64), (b_copy, "S", 2, 0), (weave_z, "S", 3, 0, 64, P)]
-        scalar += [(b_copy, "S", 2, cc) for cc in (1, 2, 3)]
+        scalar += [(weave_z, "S", 3, 0, 0, 64), (b_copy, "S", 2, 0), (b_copy, "S", 2, 1), (weave_z, "S", 3, 0, 64, P)]
+        scalar += [(b_copy, "S", 2, cc) for cc in (2, 3)]
         scalar += [(b_copy, "S", 3, cc) for cc in range(4)] + outs[1] + outs[3] + outs[5] + outs[7]
 
         gpsimd = [(weave_y, "G", 2, 0, N), (weave_y, "G", 2, N, 2 * N), (weave_y, "G", 3, 0, Y_POOL)]
@@ -383,15 +386,19 @@ def tile_weighted_hankel_subspace_s11_kernel(
         tensor += futures(1, range(1, 8)) + futures(8, range(4)) + a_turns(0, (0, 1), (4, 5)) + futures(12, (6, 7))
         tensor += a_turns(0, (2, 3), (0, 1)) + futures(14, (2, 3)) + futures(16, (4, 5, 6, 7)) + a_turns(1, range(4), range(4))
         tensor += futures(20, (4, 5, 6, 7)) + futures(24, range(4)) + a_turns(2, range(4), (4, 5, 6, 7)) + futures(28, (0, 1, 4, 5))
-        tensor += [(past, 0, 0, 6), (past, 0, 1, 7), (past, 0, 2, 2)] + a_turns(3, range(4), (3, 0, 1, 4)) + [(past, 0, 3, 5)]
+        tensor += [(past, 0, 0, 0, 3, 6), (past, 0, 1, 0, 3, 7), (past, 0, 2, 0, 3, 2)] + a_turns(3, range(4), (3, 0, 1, 4)) + [(past, 0, 3, 0, 3, 5)]
         def summed(i, g):
             return (sum_pass,) + sums[i] + (g, sum_banks[i])
-        for g in (1, 2):
-            for cc in range(4):
-                tensor += [(past, g, cc, b_banks[(4 * g + cc - 4) % 3])]
-                tensor += [summed(i, g - 1) for i in ((), (0,), (1, 2), (3, 4))[cc]]
-        tensor += [(past, 3, 0, 5), (past, 3, 1, 6), (past, 3, 2, 7), summed(0, 2), (past, 3, 3, 5), summed(0, 3)]
-        for i in range(1, 5):
+        def bb(g, cc):
+            return b_banks[(4 * g + cc - 4) % 3]
+        tensor += [(past, 1, 0, 0, 3, bb(1, 0)), (past, 1, 1, 0, 3, bb(1, 1)), summed(0, 0), (past, 1, 2, 0, 3, bb(1, 2)), summed(1, 0), summed(2, 0), (past, 1, 3, 0, 3, bb(1, 3)), summed(3, 0), summed(4, 0)]
+        for g in (2, 3):
+            for i in range(3):
+                tensor += [(past, g, 0, i, i + 1, bb(g, 0)), (past, g, 1, i, i + 1, bb(g, 1))]
+            if g == 2:
+                tensor += [(past, g, 2, 0, 3, bb(g, 2)), summed(0, 1), summed(1, 1), summed(2, 1), (past, g, 3, 0, 3, bb(g, 3)), summed(3, 1), summed(4, 1)]
+        tensor += [(past, 3, 2, 0, 3, 7), (past, 3, 3, 0, 3, 5)]
+        for i in range(5):
             tensor += [summed(i, 2), summed(i, 3)]
         for cs, bank in ((pairs[1], 6), (pairs[2], 7), ((6,), 5), ((7,), 2)):
             tensor += [(sum_pass, 1, cs, g, bank) for g in range(GROUPS)]
@@ -432,7 +439,7 @@ def tile_weighted_hankel_subspace_s11_kernel(
         def needs(step):
             fn, a = step[0], step[1:]
             got = []
-            if step in tensor and (fn != sum_pass or a[2] == 0):
+            if step in tensor and (fn != sum_pass or a[2] == 0) and (fn != past or a[2] == 0):
                 for s in before(step, lambda s: s in tensor and s[-1] == a[-1]):
                     got = got + bank_users(s)
             if fn == load_z:
@@ -457,7 +464,7 @@ def tile_weighted_hankel_subspace_s11_kernel(
                 got = got + every(load_z, lambda g, d, sl: (g, d) == a[1:3])
                 got = got + (shared_readers(step, 0, N) if a[0] == "G" else every(quant_z, lambda g, d: (g, d) == (a[1] - 2, a[2])))
             if fn == quant_z:
-                got = got + every(weave_z, lambda e, g, d, m0, m1: (g, d) == a) + every(past, lambda g, cc, b: g == a[0] - 2)
+                got = got + every(weave_z, lambda e, g, d, m0, m1: (g, d) == a) + every(past, lambda g, cc, i0, i1, b: g == a[0] - 2)
             if fn == w_turn:
                 got = got + every(load_w, lambda c0, c1, sl: c0 <= a[0] < c1)
             if fn == w_copy:
@@ -476,9 +483,9 @@ def tile_weighted_hankel_subspace_s11_kernel(
             if fn == quant_a:
                 got = got + every(a_copy, lambda e, g, p: g == a[0] and a[1] <= p < a[2])
             if fn == past:
-                got = got + [(load_wp,)] + every(quant_z, lambda g, d: g == a[0])
+                got = got + [(load_wp,)] + [(quant_z, a[0], d) for d in z_order[a[0]][a[2] : a[3]]]
             if fn == b_copy:
-                got = got + every(past, lambda g, cc, b: (g, cc) == a[1:3]) + every(quant_b, lambda g, n0, n1: g == a[1] - 2)
+                got = got + every(past, lambda g, cc, i0, i1, b: (g, cc) == a[1:3]) + every(quant_b, lambda g, n0, n1: g == a[1] - 2)
             if fn == quant_b:
                 got = got + every(b_copy, lambda e, g, cc: g == a[0] and a[1] <= P * cc < a[2])
             if fn == sum_pass:

@@ -30,7 +30,8 @@ Y_GROUPS = 3
 SLOTS = 8
 W_BUFS = 2
 AT_BUFS = RT + RT // 2 + 1
-Y_POOL = 704
+Y_POOL = 928
+SHIFT = 0
 Z_STEP = 48
 
 
@@ -55,7 +56,7 @@ def tile_weighted_hankel_subspace_s11_kernel(
         ascale = keep.tile([P, GROUPS, R], U8, name="ascale", align_bytes=64)
         bcode = keep.tile([P, GROUPS, C], U32, name="bcode", align_bytes=64)
         bscale = keep.tile([P, GROUPS, C], U8, name="bscale", align_bytes=64)
-        shared = keep.tile([P, FP * N * 4], BF16, name="shared", align_bytes=64)
+        shared = keep.tile([P, (FP * N + SHIFT) * 4], BF16, name="shared", align_bytes=64)
 
         y_view = y_f_bytes.rearrange("(f p t) n -> f p t n", f=FP, p=P, t=4)
         z_view = z_p.rearrange("(d p t) n -> d p t n", d=DP, p=P, t=4)
@@ -65,7 +66,9 @@ def tile_weighted_hankel_subspace_s11_kernel(
         tiles = {}
         last = GROUPS - 1
         pairs = [(c, c + 1) for c in range(0, RT, 2)]
-        z_order = [(2, 0, 1), (0, 1, 2), (2, 1, 0), (2, 1, 0)]
+        f_order = [(0, 1)] * GROUPS
+        shifts = (0, 0, 0, 0)
+        z_order = [(2, 0, 1), (0, 1, 2), (2, 0, 1), (2, 1, 0)]
 
         def bank_tile(bank, shape, dtype=F32):
             return psum.tile(shape, dtype, name="bank%d" % bank)
@@ -126,7 +129,7 @@ def tile_weighted_hankel_subspace_s11_kernel(
         def widen(eng, g, f, t):
             if ("yw", g) not in tiles:
                 tiles["yw", g] = keep.tile([P, FP * 4 * N], BF16, name="yw%d" % (g % 2), align_bytes=64)
-            order = "p (t f n) -> p f t n" if g == last else "p (f t n) -> p f t n"
+            order = "p (f t n) -> p f t n"
             plane = tiles["yw", g][:].rearrange(order, t=4, f=FP)[:, f, t, :]
             src = tiles["yb", g, f][:, t, :].bitcast(FP8)
             s = y_scale[:, f, t : t + 1]
@@ -135,14 +138,15 @@ def tile_weighted_hankel_subspace_s11_kernel(
             else:
                 nc.vector.tensor_scalar(out=plane, in0=src, scalar1=s, scalar2=None, op0=MULT)
 
+        def woven(g, n0, n1):
+            shift = shifts[g]
+            return shared[:, 4 * (shift + n0) : 4 * (shift + n1)]
+
         def weave_y(eng, g, n0, n1):
-            dst = shared[:, 4 * n0 : 4 * n1].rearrange("p (n t) -> p n t", t=4)
-            if g == last:
-                src = tiles["yw", g][:].rearrange("p (t n) -> p t n", t=4)[:, :, n0:n1]
-            else:
-                f = n0 // N
-                src = tiles["yw", g][:, 4 * N * f : 4 * N * (f + 1)].rearrange("p (t n) -> p t n", t=4)
-                src = src[:, :, n0 - N * f : n1 - N * f]
+            dst = woven(g, n0, n1).rearrange("p (n t) -> p n t", t=4)
+            f = n0 // N
+            src = tiles["yw", g][:, 4 * N * f : 4 * N * (f + 1)].rearrange("p (t n) -> p t n", t=4)
+            src = src[:, :, n0 - N * f : n1 - N * f]
             if eng == "G":
                 pool_copy(dst, src.rearrange("p t n -> p n t"))
             else:
@@ -155,13 +159,13 @@ def tile_weighted_hankel_subspace_s11_kernel(
             nc.vector.quantize_mx(
                 out=tiles["yc", g][:, n0:n1].bitcast(FP8X4),
                 scales=tiles["ys", g][:, n0:n1],
-                in_=shared[:, 4 * n0 : 4 * n1],
+                in_=woven(g, n0, n1),
             )
 
         def weave_z(eng, g, d, m0, m1):
             if ("zi", g, d) not in tiles:
                 if eng == "G":
-                    tiles["zi", g, d] = shared[:, 0 : 4 * N]
+                    tiles["zi", g, d] = woven(last, 0, N)
                 else:
                     tiles["zi", g, d] = keep.tile([P, 4 * N], BF16, name="zi%d%d" % (g % 2, d), align_bytes=64)[:]
             dst = tiles["zi", g, d].rearrange("p (s m j) -> p s m j", s=4, j=4)
@@ -203,17 +207,19 @@ def tile_weighted_hankel_subspace_s11_kernel(
                 in_=tiles["wi", pair][:].rearrange("p c f r u -> p (c f r u)").bitcast(BF16),
             )
 
-        def future(g, c, bank):
-            tiles["fp", g, c] = bank_tile(bank, [P, N])
-            for f in range(FP):
+        def future(g, c, i0, i1, bank):
+            if i0 == 0:
+                tiles["fp", g, c] = bank_tile(bank, [P, N])
+            for i in range(i0, i1):
+                f = f_order[g][i]
                 nc.tensor.matmul_mx(
                     out=tiles["fp", g, c][:],
                     lhsT=wcode[:, c, f, :].bitcast(FP8X4),
                     lhsT_scale=wscale[:, c, f, :],
                     rhs=tiles["yc", g][:, N * f : N * f + N].bitcast(FP8X4),
                     rhs_scale=tiles["ys", g][:, N * f : N * f + N],
-                    start=(f == 0),
-                    stop=(f == FP - 1),
+                    start=(i == 0),
+                    stop=(i == FP - 1),
                 )
 
         def epilogue(g, c):
@@ -313,8 +319,8 @@ def tile_weighted_hankel_subspace_s11_kernel(
         def epilogues(first, count):
             return [(epilogue, i // RT, i % RT) for i in range(first, first + count)]
 
-        def futures(first, banks):
-            return [(future, (first + i) // RT, (first + i) % RT, b) for i, b in enumerate(banks)]
+        def futures(first, banks, i0=0, i1=FP):
+            return [(future, (first + i) // RT, (first + i) % RT, i0, i1, b) for i, b in enumerate(banks)]
 
         def finish(eng, half, cs, slot, step):
             return [(scale_out, eng, half, cs, i, slot) for i in range(len(cs))]
@@ -342,65 +348,76 @@ def tile_weighted_hankel_subspace_s11_kernel(
         zl = [(load_z, g, d, (4 + i) % SLOTS) for i, (g, d) in enumerate(zs)]
         sync += zl[:3] + [(load_wp,), (load_rho,)] + zl[3:]
 
-        b_banks = (6, 7, 5)
+        b_banks = (1, 2, 3)
         sums = [(0, cs) for cs in pairs] + [(1, pairs[0])]
-        sum_banks = (2, 3, 0, 1, 4)
+        sum_banks = (5, 4, 7, 0, 6)
         ends = [("V", 0, pairs[0]), ("S", 0, pairs[1]), ("V", 0, pairs[2]), ("S", 0, pairs[3])]
         ends += [("V", 1, pairs[0]), ("S", 1, pairs[1]), ("V", 1, pairs[2]), ("S", 1, (6,)), ("V", 1, (7,))]
         outs = [[(scale_out, e, h, cs, i, k) for i in range(len(cs))] for k, (e, h, cs) in enumerate(ends)]
         for k, (e, h, cs) in enumerate(ends):
             sync += [(store, h, cs, i, i + 1, k) for i in range(len(cs))] if k > 5 else [(store, h, cs, 0, 2, k)]
 
-        vector = [(zero_scales,)] + planes("V", 0, 0, (1, 2, 3)) + [(weave_y, "V", 0, 0, N)] + planes("V", 0, 1, (3,))
+        vector = [(zero_scales,)] + planes("V", 0, 0, (1, 2, 3)) + planes("V", 0, 1, (3,)) + [(weave_y, "V", 0, 0, 384)] + planes("V", 0, 1, (2,))
         vector += [(quant_y, 0, 0, N), (weave_y, "V", 0, N, 2 * N), (w_quant, 0), (quant_y, 0, N, 2 * N)]
         vector += planes("V", 1, 0, (3,)) + planes("V", 1, 1, (2, 3)) + [(weave_y, "V", 1, 0, N), (w_quant, 1)]
-        vector += [(weave_y, "V", 1, N, 2 * N), (w_quant, 2), (quant_y, 1, 0, N), (w_quant, 3), (quant_y, 1, N, 2 * N)]
-        vector += epilogues(0, 12) + [(quant_y, 2, 0, N), (quant_y, 2, N, N + N // 2), (quant_y, 2, N + N // 2, 2 * N)]
-        vector += epilogues(12, 8) + [(quant_y, 3, 0, N), (quant_y, 3, N, 2 * N)]
-        vector += epilogues(20, 6) + quants_z(0, (2, 0, 1))
-        vector += epilogues(26, 6) + [(weave_z, "V", 1, 2, 0, P)] + quants_z(1, (0, 1, 2))
+        vector += [(weave_y, "V", 1, N, 2 * N), (w_quant, 2), (w_quant, 3), (quant_y, 1, 0, N), (quant_y, 1, N, 2 * N)]
+        vector += epilogues(0, 11) + [(quant_y, 2, 0, N), (quant_y, 2, N, 2 * N)]
+        vector += epilogues(11, 10) + [(quant_y, 3, 0, N), (quant_y, 3, N, 2 * N)]
+        vector += epilogues(21, 6) + quants_z(0, (2, 0, 1))
+        vector += epilogues(27, 5) + [(weave_z, "V", 1, 2, 0, P)] + quants_z(1, (0, 1, 2))
         over = {2: 32, last: 80}
         for g in (1, 2):
             vector += [(quant_a, g - 1, 0, 4), (quant_b, g - 1, 0, HALF), (weave_z, "V", g + 1, 2, 0, P), (quant_b, g - 1, HALF, C)]
-            vector += [(weave_z, "V", g + 1, 1, over[g + 1], P)] + quants_z(g + 1, (2, 1, 0))
+            vector += [(weave_z, "V", g + 1, 1, over[g + 1], P)] + quants_z(g + 1, z_order[g + 1])
         vector += [(quant_a, 2, 0, 4), (quant_b, 2, 0, HALF), (quant_a, 3, 0, 4), (quant_b, 3, 0, HALF), (cast_rho,), (quant_b, 2, HALF, C)]
         vector += outs[0] + [(quant_b, 3, HALF, C)] + outs[2] + outs[4] + outs[6] + outs[8]
 
-        scalar = [(load_scale,)] + planes("S", 0, 0, (0,)) + planes("S", 0, 1, (0, 1, 2)) + w_copies(0)
+        scalar = [(load_scale,)] + planes("S", 0, 0, (0,)) + planes("S", 0, 1, (0,)) + [(weave_y, "S", 0, 384, N)] + planes("S", 0, 1, (1,)) + w_copies(0)
         scalar += planes("S", 1, 0, (0, 1, 2)) + w_copies(1) + planes("S", 1, 1, (0, 1)) + w_copies(2)
         scalar += planes("S", 2, 0, (0,)) + w_copies(3) + planes("S", 2, 0, (1, 2, 3)) + planes("S", 2, 1, range(4))
-        scalar += planes("S", 3, 0, range(4)) + planes("S", 3, 1, (0, 1)) + a_copies(0, (0,)) + planes("S", 3, 1, (2, 3))
-        scalar += a_copies(0, (1, 2, 3)) + [(weave_y, "S", 3, Y_POOL, 2 * N), (weave_z, "S", 0, 2, 0, P)] + a_copies(1, range(4))
-        scalar += [(weave_z, "S", 0, 1, 0, P)] + a_copies(2, range(4))
-        scalar += [(weave_z, "S", 1, 1, 0, P), (b_copy, "S", 0, 0), (weave_z, "S", 2, 0, 0, 32), (b_copy, "S", 0, 1), (b_copy, "S", 0, 2)] + a_copies(3, range(4))
-        scalar += [(b_copy, "S", 0, 3), (weave_z, "S", 2, 0, 32, 112), (b_copy, "S", 1, 0), (weave_z, "S", 2, 0, 112, P), (weave_z, "S", 2, 1, 0, 32)]
-        scalar += [(b_copy, "S", 1, 1), (b_copy, "S", 1, 2), (weave_z, "S", 3, 1, 0, 80), (b_copy, "S", 1, 3)]
-        scalar += [(weave_z, "S", 3, 0, 0, 64), (b_copy, "S", 2, 0), (b_copy, "S", 2, 1), (weave_z, "S", 3, 0, 64, P)]
-        scalar += [(b_copy, "S", 2, cc) for cc in (2, 3)]
+        scalar += planes("S", 3, 0, range(4)) + planes("S", 3, 1, (0,)) + a_copies(0, (0, 1)) + planes("S", 3, 1, (1, 2)) + a_copies(0, (2, 3)) + planes("S", 3, 1, (3,))
+        shares = [(0, 2, P), (0, 1, P), (1, 1, P), (2, 0, P), (2, 1, over[2]), (3, 1, over[3]), (3, 0, P)]
+        rows = [(g, d, m) for g, d, n in shares for m in range(n)]
+        taken = [0]
+
+        def z_rows(n):
+            part = rows[taken[-1] : taken[-1] + n]
+            taken.append(taken[-1] + n)
+            return [(weave_z, "S", g, d, min(m for h, e, m in part if (h, e) == (g, d)), max(m for h, e, m in part if (h, e) == (g, d)) + 1) for g, d, n in shares if any(r[:2] == (g, d) for r in part)]
+
+        def b_copies(g, ccs):
+            return [(b_copy, "S", g, cc) for cc in ccs]
+
+        scalar += z_rows(48) + [(weave_y, "S", 3, Y_POOL, 2 * N)] + z_rows(80) + a_copies(1, range(4)) + z_rows(192) + a_copies(2, range(4))
+        scalar += z_rows(144) + b_copies(0, (0, 1, 2)) + a_copies(3, range(4)) + b_copies(0, (3,))
+        for g in (1, 2):
+            scalar += z_rows(48) + b_copies(g, (0, 1)) + z_rows(48) + b_copies(g, (2,)) + z_rows(48) + b_copies(g, (3,))
+        assert taken[-1] == len(rows)
         scalar += [(b_copy, "S", 3, cc) for cc in range(4)] + outs[1] + outs[3] + outs[5] + outs[7]
 
-        gpsimd = [(weave_y, "G", 2, 0, N), (weave_y, "G", 2, N, 2 * N), (weave_y, "G", 3, 0, Y_POOL)]
+        gpsimd = [(weave_y, "G", 2, 0, N), (weave_y, "G", 2, N, 2 * N), (weave_y, "G", 3, 0, N), (weave_y, "G", 3, N, Y_POOL)]
         gpsimd += [(weave_z, "G", 0, 0, 0, P), (weave_z, "G", 1, 0, 0, P)]
 
         tensor = w_turns(0, 4) + w_turns(1, 6) + w_turns(2, 4) + futures(0, (0,)) + w_turns(3, 6)
-        tensor += futures(1, range(1, 8)) + futures(8, range(4)) + a_turns(0, (0, 1), (4, 5)) + futures(12, (6, 7))
-        tensor += a_turns(0, (2, 3), (0, 1)) + futures(14, (2, 3)) + futures(16, (4, 5, 6, 7)) + a_turns(1, range(4), range(4))
-        tensor += futures(20, (4, 5, 6, 7)) + futures(24, range(4)) + a_turns(2, range(4), (4, 5, 6, 7)) + futures(28, (0, 1, 4, 5))
-        tensor += [(past, 0, 0, 0, 3, 6), (past, 0, 1, 0, 3, 7), (past, 0, 2, 0, 3, 2)] + a_turns(3, range(4), (3, 0, 1, 4)) + [(past, 0, 3, 0, 3, 5)]
+        tensor += futures(1, range(1, 8)) + futures(8, range(5)) + a_turns(0, (0, 1), (5, 6)) + futures(13, (7, 0))
+        tensor += a_turns(0, (2, 3), (1, 2)) + futures(15, (5, 6, 1, 2, 3)) + a_turns(1, range(4), (4, 7, 0, 5)) + futures(20, (6, 1, 2, 3))
+        tensor += futures(24, (4, 7, 0), 0, 1) + futures(24, (4, 7, 0), 1, 2) + futures(27, (5,)) + a_turns(2, range(4), (6, 1, 2, 3))
+        tensor += futures(28, (4, 7, 0, 6))
+        tensor += [(past, 0, cc, i, i + 1, b) for i in range(3) for cc, b in ((0, 1), (1, 2))] + [(past, 0, 2, 0, 3, 3)] + a_turns(3, range(4), (5, 4, 7, 0)) + [(past, 0, 3, 0, 3, 6)]
         def summed(i, g):
             return (sum_pass,) + sums[i] + (g, sum_banks[i])
         def bb(g, cc):
             return b_banks[(4 * g + cc - 4) % 3]
-        tensor += [(past, 1, 0, 0, 3, bb(1, 0)), (past, 1, 1, 0, 3, bb(1, 1)), summed(0, 0), (past, 1, 2, 0, 3, bb(1, 2)), summed(1, 0), summed(2, 0), (past, 1, 3, 0, 3, bb(1, 3)), summed(3, 0), summed(4, 0)]
-        for g in (2, 3):
+        for g in (1, 2, 3):
             for i in range(3):
                 tensor += [(past, g, 0, i, i + 1, bb(g, 0)), (past, g, 1, i, i + 1, bb(g, 1))]
-            if g == 2:
-                tensor += [(past, g, 2, 0, 3, bb(g, 2)), summed(0, 1), summed(1, 1), summed(2, 1), (past, g, 3, 0, 3, bb(g, 3)), summed(3, 1), summed(4, 1)]
-        tensor += [(past, 3, 2, 0, 3, 7), (past, 3, 3, 0, 3, 5)]
+            if g < last:
+                tensor += [(past, g, 2, 0, 3, bb(g, 2)), summed(0, g - 1), summed(1, g - 1), summed(2, g - 1), (past, g, 3, 0, 3, bb(g, 3)), summed(3, g - 1), summed(4, g - 1)]
+        tensor += [(past, 3, 2, 0, 3, bb(3, 2)), (past, 3, 3, 0, 3, bb(3, 3))]
+        tensor += [summed(0, 2)]
         for i in range(5):
-            tensor += [summed(i, 2), summed(i, 3)]
-        for cs, bank in ((pairs[1], 6), (pairs[2], 7), ((6,), 5), ((7,), 2)):
+            tensor += [summed(i + 1, 2), summed(i, 3)] if i < 4 else [summed(i, 3)]
+        for cs, bank in ((pairs[1], bb(3, 1)), (pairs[2], bb(3, 2)), ((6,), bb(3, 3)), ((7,), sum_banks[0])):
             tensor += [(sum_pass, 1, cs, g, bank) for g in range(GROUPS)]
 
         steps = sync + vector + scalar + gpsimd + tensor
@@ -432,14 +449,15 @@ def tile_weighted_hankel_subspace_s11_kernel(
 
         def shared_readers(step, n0, n1):
             g = step[2] + (GROUPS if step[0] == weave_z else 0)
-            ys = every(quant_y, lambda h, a, b: h < g and a < n1 and n0 < b)
+            shift = shifts[min(g, last)]
+            ys = every(quant_y, lambda h, a, b: h < g and a + shifts[h] < n1 + shift and n0 + shift < b + shifts[h])
             zs = [(quant_z, s[2], s[3]) for s in gpsimd if s[0] == weave_z and s[2] + GROUPS < g]
             return ys + zs
 
         def needs(step):
             fn, a = step[0], step[1:]
             got = []
-            if step in tensor and (fn != sum_pass or a[2] == 0) and (fn != past or a[2] == 0):
+            if step in tensor and (fn != sum_pass or a[2] == 0) and (fn not in (past, future) or a[2] == 0):
                 for s in before(step, lambda s: s in tensor and s[-1] == a[-1]):
                     got = got + bank_users(s)
             if fn == load_z:
@@ -459,7 +477,7 @@ def tile_weighted_hankel_subspace_s11_kernel(
                 got = got + shared_readers(step, a[2], a[3])
             if fn == quant_y:
                 got = got + every(weave_y, lambda e, g, n0, n1: g == a[0] and n0 < a[2] and a[1] < n1)
-                got = got + every(future, lambda g, c, b: g == a[0] - 2)
+                got = got + every(future, lambda g, c, i0, i1, b: g == a[0] - 2)
             if fn == weave_z:
                 got = got + every(load_z, lambda g, d, sl: (g, d) == a[1:3])
                 got = got + (shared_readers(step, 0, N) if a[0] == "G" else every(quant_z, lambda g, d: (g, d) == (a[1] - 2, a[2])))
@@ -472,9 +490,9 @@ def tile_weighted_hankel_subspace_s11_kernel(
             if fn == w_quant:
                 got = got + every(w_copy, lambda e, c: c // 2 == a[0])
             if fn == future:
-                got = got + [(w_quant, a[1] // 2)] + every(quant_y, lambda g, n0, n1: g == a[0])
+                got = got + [(w_quant, a[1] // 2)] + every(quant_y, lambda g, n0, n1: g == a[0] and n0 // N in f_order[g][a[2] : a[3]])
             if fn == epilogue:
-                got = got + every(future, lambda g, c, b: (g, c) == a) + [(load_level,), (load_lam, a[0])]
+                got = got + every(future, lambda g, c, i0, i1, b: (g, c) == a) + [(load_level,), (load_lam, a[0])]
                 got = got + every(a_turn, lambda g, p, b: (RT * g + 2 * p) // 2 == (RT * a[0] + a[1] - AT_BUFS) // 2)
             if fn == a_turn:
                 got = got + [(epilogue, a[0], c) for c in pairs[a[1]]]

@@ -148,7 +148,7 @@ def tile_weighted_hankel_subspace_s11_kernel(
             src = tiles["yw", g][:, 4 * N * f : 4 * N * (f + 1)].rearrange("p (t n) -> p t n", t=4)
             src = src[:, :, n0 - N * f : n1 - N * f]
             if eng == "G":
-                pool_copy(dst, src.rearrange("p t n -> p n t"))
+                pool_copy(dst.rearrange("p (c i) t -> p c t i", i=4), src.rearrange("p t (c i) -> p c t i", i=4))
             else:
                 copy(eng, dst.rearrange("p (c i) t -> p c t i", i=4), src.rearrange("p t (c i) -> p c t i", i=4))
 
@@ -171,8 +171,8 @@ def tile_weighted_hankel_subspace_s11_kernel(
             dst = tiles["zi", g, d].rearrange("p (s m j) -> p s m j", s=4, j=4)
             src = tiles["zr", g, d][:]
             if eng == "G":
-                src = src.rearrange("p j (m s) -> p m s j", s=4)
-                pool_copy(dst.rearrange("p s m j -> p m s j")[:, m0:m1], src[:, m0:m1])
+                src = src.rearrange("p j (m s) -> p m j s", s=4)
+                pool_copy(dst.rearrange("p s m j -> p m j s")[:, m0:m1], src[:, m0:m1])
             else:
                 dst = dst.rearrange("p s m (h e) -> p m h s e", e=2)[:, m0:m1]
                 src = src.rearrange("p (h e) (m s) -> p m h s e", e=2, s=4)[:, m0:m1]
@@ -360,7 +360,7 @@ def tile_weighted_hankel_subspace_s11_kernel(
         vector = [(zero_scales,)] + planes("V", 0, 0, (1, 2, 3)) + planes("V", 0, 1, (3,)) + [(weave_y, "V", 0, 0, 384)] + planes("V", 0, 1, (2,))
         vector += [(quant_y, 0, 0, N), (weave_y, "V", 0, N, 2 * N), (w_quant, 0), (quant_y, 0, N, 2 * N)]
         vector += planes("V", 1, 0, (3,)) + planes("V", 1, 1, (2, 3)) + [(weave_y, "V", 1, 0, N), (w_quant, 1)]
-        vector += [(weave_y, "V", 1, N, 2 * N), (w_quant, 2), (w_quant, 3), (quant_y, 1, 0, N), (quant_y, 1, N, 2 * N)]
+        vector += [(weave_y, "V", 1, N, 2 * N), (w_quant, 2), (quant_y, 1, 0, N), (w_quant, 3), (quant_y, 1, N, 2 * N)]
         vector += epilogues(0, 11) + [(quant_y, 2, 0, N), (quant_y, 2, N, 2 * N)]
         vector += epilogues(11, 10) + [(quant_y, 3, 0, N), (quant_y, 3, N, 2 * N)]
         vector += epilogues(21, 6) + quants_z(0, (2, 0, 1))

@@ -30,8 +30,11 @@ Y_GROUPS = 3
 SLOTS = 8
 W_BUFS = 2
 AT_BUFS = RT + RT // 2 + 1
+
+RUNS = (11, 10, 6, 5)
 Y_POOL = 928
-SHIFT = 0
+Y_HEAD = 448
+Z_POOL = 120
 Z_STEP = 48
 
 
@@ -56,7 +59,7 @@ def tile_weighted_hankel_subspace_s11_kernel(
         ascale = keep.tile([P, GROUPS, R], U8, name="ascale", align_bytes=64)
         bcode = keep.tile([P, GROUPS, C], U32, name="bcode", align_bytes=64)
         bscale = keep.tile([P, GROUPS, C], U8, name="bscale", align_bytes=64)
-        shared = keep.tile([P, (FP * N + SHIFT) * 4], BF16, name="shared", align_bytes=64)
+        shared = keep.tile([P, FP * N * 4], BF16, name="shared", align_bytes=64)
 
         y_view = y_f_bytes.rearrange("(f p t) n -> f p t n", f=FP, p=P, t=4)
         z_view = z_p.rearrange("(d p t) n -> d p t n", d=DP, p=P, t=4)
@@ -66,8 +69,6 @@ def tile_weighted_hankel_subspace_s11_kernel(
         tiles = {}
         last = GROUPS - 1
         pairs = [(c, c + 1) for c in range(0, RT, 2)]
-        f_order = [(0, 1)] * GROUPS
-        shifts = (0, 0, 0, 0)
         z_order = [(2, 0, 1), (0, 1, 2), (2, 0, 1), (2, 1, 0)]
 
         def bank_tile(bank, shape, dtype=F32):
@@ -76,11 +77,10 @@ def tile_weighted_hankel_subspace_s11_kernel(
         def copy(eng, dst, src):
             if eng == "S":
                 nc.scalar.copy(out=dst, in_=src)
-            else:
+            elif eng == "V":
                 nc.vector.tensor_copy(out=dst, in_=src)
-
-        def pool_copy(dst, src):
-            nc.gpsimd.tensor_scalar(out=dst, in0=src, scalar1=1.0, scalar2=0.0, op0=MULT, op1=ADD)
+            else:
+                nc.gpsimd.tensor_scalar(out=dst, in0=src, scalar1=1.0, scalar2=0.0, op0=MULT, op1=ADD)
 
         def slot_tile(slot, shape, dtype):
             return keep.tile(shape, dtype, name="slot%d" % slot, align_bytes=64)
@@ -129,8 +129,7 @@ def tile_weighted_hankel_subspace_s11_kernel(
         def widen(eng, g, f, t):
             if ("yw", g) not in tiles:
                 tiles["yw", g] = keep.tile([P, FP * 4 * N], BF16, name="yw%d" % (g % 2), align_bytes=64)
-            order = "p (f t n) -> p f t n"
-            plane = tiles["yw", g][:].rearrange(order, t=4, f=FP)[:, f, t, :]
+            plane = tiles["yw", g][:].rearrange("p (f t n) -> p f t n", t=4, f=FP)[:, f, t, :]
             src = tiles["yb", g, f][:, t, :].bitcast(FP8)
             s = y_scale[:, f, t : t + 1]
             if eng == "S":
@@ -138,19 +137,15 @@ def tile_weighted_hankel_subspace_s11_kernel(
             else:
                 nc.vector.tensor_scalar(out=plane, in0=src, scalar1=s, scalar2=None, op0=MULT)
 
-        def woven(g, n0, n1):
-            shift = shifts[g]
-            return shared[:, 4 * (shift + n0) : 4 * (shift + n1)]
+        def woven(n0, n1):
+            return shared[:, 4 * n0 : 4 * n1]
 
         def weave_y(eng, g, n0, n1):
-            dst = woven(g, n0, n1).rearrange("p (n t) -> p n t", t=4)
+            dst = woven(n0, n1).rearrange("p (n t) -> p n t", t=4)
             f = n0 // N
             src = tiles["yw", g][:, 4 * N * f : 4 * N * (f + 1)].rearrange("p (t n) -> p t n", t=4)
             src = src[:, :, n0 - N * f : n1 - N * f]
-            if eng == "G":
-                pool_copy(dst.rearrange("p (c i) t -> p c t i", i=4), src.rearrange("p t (c i) -> p c t i", i=4))
-            else:
-                copy(eng, dst.rearrange("p (c i) t -> p c t i", i=4), src.rearrange("p t (c i) -> p c t i", i=4))
+            copy(eng, dst.rearrange("p (c i) t -> p c t i", i=4), src.rearrange("p t (c i) -> p c t i", i=4))
 
         def quant_y(g, n0, n1):
             if ("yc", g) not in tiles:
@@ -159,24 +154,23 @@ def tile_weighted_hankel_subspace_s11_kernel(
             nc.vector.quantize_mx(
                 out=tiles["yc", g][:, n0:n1].bitcast(FP8X4),
                 scales=tiles["ys", g][:, n0:n1],
-                in_=woven(g, n0, n1),
+                in_=woven(n0, n1),
             )
 
         def weave_z(eng, g, d, m0, m1):
             if ("zi", g, d) not in tiles:
-                if eng == "G":
-                    tiles["zi", g, d] = woven(last, 0, N)
+                if g < 2 and d == 0:
+                    tiles["zi", g, d] = woven(0, N)
                 else:
                     tiles["zi", g, d] = keep.tile([P, 4 * N], BF16, name="zi%d%d" % (g % 2, d), align_bytes=64)[:]
-            dst = tiles["zi", g, d].rearrange("p (s m j) -> p s m j", s=4, j=4)
-            src = tiles["zr", g, d][:]
+            dst, src = tiles["zi", g, d], tiles["zr", g, d][:]
             if eng == "G":
+                dst = dst.rearrange("p (s m j) -> p m j s", s=4, j=4)
                 src = src.rearrange("p j (m s) -> p m j s", s=4)
-                pool_copy(dst.rearrange("p s m j -> p m j s")[:, m0:m1], src[:, m0:m1])
             else:
-                dst = dst.rearrange("p s m (h e) -> p m h s e", e=2)[:, m0:m1]
-                src = src.rearrange("p (h e) (m s) -> p m h s e", e=2, s=4)[:, m0:m1]
-                copy(eng, dst, src)
+                dst = dst.rearrange("p (s m h e) -> p m h s e", s=4, h=2, e=2)
+                src = src.rearrange("p (h e) (m s) -> p m h s e", e=2, s=4)
+            copy(eng, dst[:, m0:m1], src[:, m0:m1])
 
         def quant_z(g, d):
             if ("zc", g) not in tiles:
@@ -210,16 +204,15 @@ def tile_weighted_hankel_subspace_s11_kernel(
         def future(g, c, i0, i1, bank):
             if i0 == 0:
                 tiles["fp", g, c] = bank_tile(bank, [P, N])
-            for i in range(i0, i1):
-                f = f_order[g][i]
+            for f in range(i0, i1):
                 nc.tensor.matmul_mx(
                     out=tiles["fp", g, c][:],
                     lhsT=wcode[:, c, f, :].bitcast(FP8X4),
                     lhsT_scale=wscale[:, c, f, :],
                     rhs=tiles["yc", g][:, N * f : N * f + N].bitcast(FP8X4),
                     rhs_scale=tiles["ys", g][:, N * f : N * f + N],
-                    start=(i == 0),
-                    stop=(i == FP - 1),
+                    start=(f == 0),
+                    stop=(f == FP - 1),
                 )
 
         def epilogue(g, c):
@@ -322,9 +315,6 @@ def tile_weighted_hankel_subspace_s11_kernel(
         def futures(first, banks, i0=0, i1=FP):
             return [(future, (first + i) // RT, (first + i) % RT, i0, i1, b) for i, b in enumerate(banks)]
 
-        def finish(eng, half, cs, slot, step):
-            return [(scale_out, eng, half, cs, i, slot) for i in range(len(cs))]
-
         def w_turns(pair, bank):
             return [(w_turn, c, bank + c % 2) for c in pairs[pair]]
 
@@ -337,88 +327,105 @@ def tile_weighted_hankel_subspace_s11_kernel(
         def a_copies(g, ps):
             return [(a_copy, "S", g, p) for p in ps]
 
-        def quants_z(g, order):
-            return [(quant_z, g, d) for d in order]
-
-        sync = [(load_y, 0, 0, 0, 2), (load_y, 0, 0, 2, 4), (load_y, 0, 1, 0, 4), (load_w, 0, 1, 0), (load_w, 1, 2, 0), (load_y, 1, 0, 0, 4)]
-        sync += [(load_w, 2, 4, 1), (load_w, 4, 6, 2), (load_y, 1, 1, 0, 4), (load_w, 6, 8, 3)]
-        sync += [(load_y, 2, 0, 0, 4), (load_level,), (load_lam, 0), (load_y, 2, 1, 0, 4), (load_y, 3, 0, 0, 4), (load_y, 3, 1, 0, 4)]
-        sync += [(load_lam, g) for g in range(1, GROUPS)]
-        zs = [(0, 2), (0, 0), (0, 1)] + [(g, d) for g in (1, 2) for d in range(DP)] + [(last, d) for d in range(DP)]
-        zl = [(load_z, g, d, (4 + i) % SLOTS) for i, (g, d) in enumerate(zs)]
-        sync += zl[:3] + [(load_wp,), (load_rho,)] + zl[3:]
-
-        b_banks = (1, 2, 3)
-        sums = [(0, cs) for cs in pairs] + [(1, pairs[0])]
-        sum_banks = (5, 4, 7, 0, 6)
-        ends = [("V", 0, pairs[0]), ("S", 0, pairs[1]), ("V", 0, pairs[2]), ("S", 0, pairs[3])]
-        ends += [("V", 1, pairs[0]), ("S", 1, pairs[1]), ("V", 1, pairs[2]), ("S", 1, (6,)), ("V", 1, (7,))]
-        outs = [[(scale_out, e, h, cs, i, k) for i in range(len(cs))] for k, (e, h, cs) in enumerate(ends)]
-        for k, (e, h, cs) in enumerate(ends):
-            sync += [(store, h, cs, i, i + 1, k) for i in range(len(cs))] if k > 5 else [(store, h, cs, 0, 2, k)]
-
-        vector = [(zero_scales,)] + planes("V", 0, 0, (1, 2, 3)) + planes("V", 0, 1, (3,)) + [(weave_y, "V", 0, 0, 384)] + planes("V", 0, 1, (2,))
-        vector += [(quant_y, 0, 0, N), (weave_y, "V", 0, N, 2 * N), (w_quant, 0), (quant_y, 0, N, 2 * N)]
-        vector += planes("V", 1, 0, (3,)) + planes("V", 1, 1, (2, 3)) + [(weave_y, "V", 1, 0, N), (w_quant, 1)]
-        vector += [(weave_y, "V", 1, N, 2 * N), (w_quant, 2), (quant_y, 1, 0, N), (w_quant, 3), (quant_y, 1, N, 2 * N)]
-        vector += epilogues(0, 11) + [(quant_y, 2, 0, N), (quant_y, 2, N, 2 * N)]
-        vector += epilogues(11, 10) + [(quant_y, 3, 0, N), (quant_y, 3, N, 2 * N)]
-        vector += epilogues(21, 6) + quants_z(0, (2, 0, 1))
-        vector += epilogues(27, 5) + [(weave_z, "V", 1, 2, 0, P)] + quants_z(1, (0, 1, 2))
-        over = {2: 32, last: 80}
-        for g in (1, 2):
-            vector += [(quant_a, g - 1, 0, 4), (quant_b, g - 1, 0, HALF), (weave_z, "V", g + 1, 2, 0, P), (quant_b, g - 1, HALF, C)]
-            vector += [(weave_z, "V", g + 1, 1, over[g + 1], P)] + quants_z(g + 1, z_order[g + 1])
-        vector += [(quant_a, 2, 0, 4), (quant_b, 2, 0, HALF), (quant_a, 3, 0, 4), (quant_b, 3, 0, HALF), (cast_rho,), (quant_b, 2, HALF, C)]
-        vector += outs[0] + [(quant_b, 3, HALF, C)] + outs[2] + outs[4] + outs[6] + outs[8]
-
-        scalar = [(load_scale,)] + planes("S", 0, 0, (0,)) + planes("S", 0, 1, (0,)) + [(weave_y, "S", 0, 384, N)] + planes("S", 0, 1, (1,)) + w_copies(0)
-        scalar += planes("S", 1, 0, (0, 1, 2)) + w_copies(1) + planes("S", 1, 1, (0, 1)) + w_copies(2)
-        scalar += planes("S", 2, 0, (0,)) + w_copies(3) + planes("S", 2, 0, (1, 2, 3)) + planes("S", 2, 1, range(4))
-        scalar += planes("S", 3, 0, range(4)) + planes("S", 3, 1, (0,)) + a_copies(0, (0, 1)) + planes("S", 3, 1, (1, 2)) + a_copies(0, (2, 3)) + planes("S", 3, 1, (3,))
-        shares = [(0, 2, P), (0, 1, P), (1, 1, P), (2, 0, P), (2, 1, over[2]), (3, 1, over[3]), (3, 0, P)]
-        rows = [(g, d, m) for g, d, n in shares for m in range(n)]
-        taken = [0]
-
-        def z_rows(n):
-            part = rows[taken[-1] : taken[-1] + n]
-            taken.append(taken[-1] + n)
-            return [(weave_z, "S", g, d, min(m for h, e, m in part if (h, e) == (g, d)), max(m for h, e, m in part if (h, e) == (g, d)) + 1) for g, d, n in shares if any(r[:2] == (g, d) for r in part)]
-
         def b_copies(g, ccs):
             return [(b_copy, "S", g, cc) for cc in ccs]
 
-        scalar += z_rows(48) + [(weave_y, "S", 3, Y_POOL, 2 * N)] + z_rows(80) + a_copies(1, range(4)) + z_rows(192) + a_copies(2, range(4))
-        scalar += z_rows(144) + b_copies(0, (0, 1, 2)) + a_copies(3, range(4)) + b_copies(0, (3,))
-        for g in (1, 2):
-            scalar += z_rows(48) + b_copies(g, (0, 1)) + z_rows(48) + b_copies(g, (2,)) + z_rows(48) + b_copies(g, (3,))
-        assert taken[-1] == len(rows)
-        scalar += [(b_copy, "S", 3, cc) for cc in range(4)] + outs[1] + outs[3] + outs[5] + outs[7]
+        def quants_y(g):
+            return [(quant_y, g, N * f, N * f + N) for f in range(FP)]
 
-        gpsimd = [(weave_y, "G", 2, 0, N), (weave_y, "G", 2, N, 2 * N), (weave_y, "G", 3, 0, N), (weave_y, "G", 3, N, Y_POOL)]
-        gpsimd += [(weave_z, "G", 0, 0, 0, P), (weave_z, "G", 1, 0, 0, P)]
+        def quants_z(g):
+            return [(quant_z, g, d) for d in z_order[g]]
+
+        def run(i):
+            return epilogues(sum(RUNS[:i]), RUNS[i])
+
+        sync = [(load_y, 0, 0, 0, 2), (load_y, 0, 0, 2, 4), (load_y, 0, 1, 0, 4), (load_w, 0, 1, 0), (load_w, 1, 2, 0)]
+        sync += [(load_y, 1, 0, 0, 4), (load_w, 2, 4, 1), (load_w, 4, 6, 2), (load_y, 1, 1, 0, 4), (load_w, 6, 8, 3)]
+        sync += [(load_y, 2, 0, 0, 4), (load_level,), (load_lam, 0), (load_y, 2, 1, 0, 4)]
+        sync += [(load_y, last, f, 0, 4) for f in range(FP)] + [(load_lam, g) for g in range(1, GROUPS)]
+        z_tiles = [(0, d) for d in z_order[0]] + [(g, d) for g in range(1, GROUPS) for d in range(DP)]
+        z_loads = [(load_z, g, d, (len(pairs) + i) % SLOTS) for i, (g, d) in enumerate(z_tiles)]
+        sync += z_loads[:DP] + [(load_wp,), (load_rho,)] + z_loads[DP:]
+
+        ends = [(0, cs) for cs in pairs] + [(1, cs) for cs in pairs[:-1]] + [(1, (c,)) for c in pairs[-1]]
+        outs = [[(scale_out, "VS"[k % 2], h, cs, i, k) for i in range(len(cs))] for k, (h, cs) in enumerate(ends)]
+        for k, (h, cs) in enumerate(ends):
+            by_tile = k >= len(ends) - 3
+            sync += [(store, h, cs, i, i + 1, k) for i in range(len(cs))] if by_tile else [(store, h, cs, 0, 2, k)]
+
+        room = P + (4 + 3 + 2 * 3) * Z_STEP
+        reach = {2: Z_STEP, last: room - 5 * P - Z_STEP}
+        shares = [(0, 2, 0, P), (0, 1, 0, P), (1, 1, 0, P), (2, 0, 0, P), (2, 1, 0, reach[2])]
+        shares += [(last, 1, 0, reach[last]), (last, 0, 0, P)]
+        rows = [(g, d, m) for g, d, m0, m1 in shares for m in range(m0, m1)]
+
+        def z_rows(n):
+            part = [rows.pop(0) for i in range(n)]
+            cut = [(g, d, [m for h, e, m in part if (h, e) == (g, d)]) for g, d, m0, m1 in shares]
+            return [(weave_z, "S", g, d, ms[0], ms[-1] + 1) for g, d, ms in cut if ms]
+
+        vector = [(zero_scales,)] + planes("V", 0, 0, (1, 2, 3)) + planes("V", 0, 1, (3,))
+        vector += [(weave_y, "V", 0, 0, Y_HEAD)] + planes("V", 0, 1, (2,))
+        vector += [(quant_y, 0, 0, N), (weave_y, "V", 0, N, 2 * N), (w_quant, 0), (quant_y, 0, N, 2 * N)]
+        vector += planes("V", 1, 0, (3,)) + planes("V", 1, 1, (2, 3)) + [(weave_y, "V", 1, 0, N), (w_quant, 1)]
+        vector += [(weave_y, "V", 1, N, 2 * N), (w_quant, 2), (quant_y, 1, 0, N), (w_quant, 3), (quant_y, 1, N, 2 * N)]
+        vector += run(0) + quants_y(2) + run(1) + quants_y(last) + run(2) + quants_z(0)
+        vector += run(3) + [(weave_z, "V", 1, 0, Z_POOL, P), (weave_z, "V", 1, 2, 0, P)] + quants_z(1)
+        for g in range(2, GROUPS):
+            vector += [(quant_a, g - 2, 0, 4), (quant_b, g - 2, 0, HALF), (weave_z, "V", g, 2, 0, P)]
+            vector += [(quant_b, g - 2, HALF, C), (weave_z, "V", g, 1, reach[g], P)] + quants_z(g)
+        for g in range(2, GROUPS):
+            vector += [(quant_a, g, 0, 4), (quant_b, g, 0, HALF)]
+        vector += [(cast_rho,), (quant_b, 2, HALF, C)] + outs[0] + [(quant_b, last, HALF, C)]
+        vector += [s for out_steps in outs[2::2] for s in out_steps]
+
+        scalar = [(load_scale,)] + planes("S", 0, 0, (0,)) + planes("S", 0, 1, (0,)) + [(weave_y, "S", 0, Y_HEAD, N)]
+        scalar += planes("S", 0, 1, (1,)) + w_copies(0) + planes("S", 1, 0, (0, 1, 2)) + w_copies(1)
+        scalar += planes("S", 1, 1, (0, 1)) + w_copies(2) + planes("S", 2, 0, (0,)) + w_copies(3)
+        scalar += planes("S", 2, 0, (1, 2, 3)) + planes("S", 2, 1, range(4))
+        scalar += planes("S", last, 0, range(4)) + planes("S", last, 1, (0,)) + a_copies(0, (0, 1))
+        scalar += planes("S", last, 1, (1, 2)) + a_copies(0, (2, 3)) + planes("S", last, 1, (3,))
+        scalar += z_rows(Z_STEP) + [(weave_y, "S", last, Y_POOL, 2 * N)] + z_rows(P - Z_STEP) + a_copies(1, range(4))
+        scalar += z_rows(4 * Z_STEP) + a_copies(2, range(4))
+        scalar += z_rows(3 * Z_STEP) + b_copies(0, (0, 1, 2)) + a_copies(last, range(4)) + b_copies(0, (3,))
+        for g in (1, 2):
+            for ccs in ((0, 1), (2,), (3,)):
+                scalar += z_rows(Z_STEP) + b_copies(g, ccs)
+        scalar += b_copies(last, range(4)) + [s for out_steps in outs[1::2] for s in out_steps]
+
+        gpsimd = [(weave_y, "G", 2, 0, N), (weave_y, "G", 2, N, 2 * N)]
+        gpsimd += [(weave_y, "G", last, 0, N), (weave_y, "G", last, N, Y_POOL)]
+        gpsimd += [(weave_z, "G", 0, 0, 0, P), (weave_z, "G", 1, 0, 0, Z_POOL)]
 
         tensor = w_turns(0, 4) + w_turns(1, 6) + w_turns(2, 4) + futures(0, (0,)) + w_turns(3, 6)
         tensor += futures(1, range(1, 8)) + futures(8, range(5)) + a_turns(0, (0, 1), (5, 6)) + futures(13, (7, 0))
-        tensor += a_turns(0, (2, 3), (1, 2)) + futures(15, (5, 6, 1, 2, 3)) + a_turns(1, range(4), (4, 7, 0, 5)) + futures(20, (6, 1, 2, 3))
-        tensor += futures(24, (4, 7, 0), 0, 1) + futures(24, (4, 7, 0), 1, 2) + futures(27, (5,)) + a_turns(2, range(4), (6, 1, 2, 3))
-        tensor += futures(28, (4, 7, 0, 6))
-        tensor += [(past, 0, cc, i, i + 1, b) for i in range(3) for cc, b in ((0, 1), (1, 2))] + [(past, 0, 2, 0, 3, 3)] + a_turns(3, range(4), (5, 4, 7, 0)) + [(past, 0, 3, 0, 3, 6)]
-        def summed(i, g):
-            return (sum_pass,) + sums[i] + (g, sum_banks[i])
-        def bb(g, cc):
-            return b_banks[(4 * g + cc - 4) % 3]
-        for g in (1, 2, 3):
-            for i in range(3):
-                tensor += [(past, g, 0, i, i + 1, bb(g, 0)), (past, g, 1, i, i + 1, bb(g, 1))]
-            if g < last:
-                tensor += [(past, g, 2, 0, 3, bb(g, 2)), summed(0, g - 1), summed(1, g - 1), summed(2, g - 1), (past, g, 3, 0, 3, bb(g, 3)), summed(3, g - 1), summed(4, g - 1)]
-        tensor += [(past, 3, 2, 0, 3, bb(3, 2)), (past, 3, 3, 0, 3, bb(3, 3))]
-        tensor += [summed(0, 2)]
-        for i in range(5):
-            tensor += [summed(i + 1, 2), summed(i, 3)] if i < 4 else [summed(i, 3)]
-        for cs, bank in ((pairs[1], bb(3, 1)), (pairs[2], bb(3, 2)), ((6,), bb(3, 3)), ((7,), sum_banks[0])):
-            tensor += [(sum_pass, 1, cs, g, bank) for g in range(GROUPS)]
+        one, two = (4, 7, 0, 5), (6, 1, 2, 3)
+        tensor += a_turns(0, (2, 3), (1, 2)) + futures(15, (5,)) + futures(16, two)
+        tensor += a_turns(1, range(4), one) + futures(20, two)
+        tensor += futures(24, one[:3], 0, 1) + futures(24, one[:3], 1, 2) + futures(27, one[3:])
+        tensor += a_turns(2, range(4), two) + futures(28, one[:3] + two[:1])
+        b_banks = two[1:]
+        sum_banks = one[3:] + one[:3] + two[:1]
+        tensor += [(past, 0, cc, i, i + 1, b_banks[cc]) for i in range(DP) for cc in range(2)]
+        tensor += [(past, 0, 2, 0, DP, b_banks[2])] + a_turns(last, range(4), sum_banks[:4])
+        tensor += [(past, 0, 3, 0, DP, sum_banks[4])]
+
+        def b_bank(g, cc):
+            return b_banks[(4 * (g - 1) + cc) % len(b_banks)]
+
+        def open_sums(ks, g):
+            return [(sum_pass,) + ends[k] + (g, sum_banks[k]) for k in ks]
+
+        for g in range(1, GROUPS):
+            tensor += [(past, g, cc, i, i + 1, b_bank(g, cc)) for i in range(DP) for cc in range(2)]
+            behind = [open_sums(ks, g - 1) if g < last else [] for ks in ((0, 1, 2), (3, 4))]
+            tensor += [(past, g, 2, 0, DP, b_bank(g, 2))] + behind[0] + [(past, g, 3, 0, DP, b_bank(g, 3))] + behind[1]
+        tensor += open_sums((0,), 2)
+        for k in range(len(sum_banks)):
+            tensor += open_sums(range(k + 1, len(sum_banks))[:1], 2) + open_sums((k,), last)
+        late_banks = [b_bank(last, cc) for cc in (1, 2, 3)] + [sum_banks[0]]
+        for end, bank in zip(ends[len(sum_banks) :], late_banks):
+            tensor += [(sum_pass,) + end + (g, bank) for g in range(GROUPS)]
 
         steps = sync + vector + scalar + gpsimd + tensor
 
@@ -447,17 +454,15 @@ def tile_weighted_hankel_subspace_s11_kernel(
                 return every(w_turn, lambda c, b: c // 2 == step[1] // 2)
             return every(weave_z, lambda e, g, d, m0, m1: (g, d) == step[1:3])
 
-        def shared_readers(step, n0, n1):
-            g = step[2] + (GROUPS if step[0] == weave_z else 0)
-            shift = shifts[min(g, last)]
-            ys = every(quant_y, lambda h, a, b: h < g and a + shifts[h] < n1 + shift and n0 + shift < b + shifts[h])
-            zs = [(quant_z, s[2], s[3]) for s in gpsimd if s[0] == weave_z and s[2] + GROUPS < g]
-            return ys + zs
+        def shared_readers(step):
+            if step[0] == weave_y:
+                return every(quant_y, lambda h, n0, n1: h < step[2] and n0 < step[4] and step[3] < n1)
+            return [(quant_y, last, 0, N)] + every(quant_z, lambda h, d: h < step[2] and d == 0)
 
         def needs(step):
             fn, a = step[0], step[1:]
             got = []
-            if step in tensor and (fn != sum_pass or a[2] == 0) and (fn not in (past, future) or a[2] == 0):
+            if step in tensor and (fn in (w_turn, a_turn) or a[2] == 0):
                 for s in before(step, lambda s: s in tensor and s[-1] == a[-1]):
                     got = got + bank_users(s)
             if fn == load_z:
@@ -474,15 +479,19 @@ def tile_weighted_hankel_subspace_s11_kernel(
                 got = got + every(weave_y, lambda e, g, n0, n1: g == a[1] - 2)
             if fn == weave_y:
                 got = got + every(widen, lambda e, g, f, t: g == a[1] and a[2] < N * f + N and N * f < a[3])
-                got = got + shared_readers(step, a[2], a[3])
+                got = got + shared_readers(step)
             if fn == quant_y:
                 got = got + every(weave_y, lambda e, g, n0, n1: g == a[0] and n0 < a[2] and a[1] < n1)
                 got = got + every(future, lambda g, c, i0, i1, b: g == a[0] - 2)
             if fn == weave_z:
                 got = got + every(load_z, lambda g, d, sl: (g, d) == a[1:3])
-                got = got + (shared_readers(step, 0, N) if a[0] == "G" else every(quant_z, lambda g, d: (g, d) == (a[1] - 2, a[2])))
+                if a[0] == "G":
+                    got = got + shared_readers(step)
+                else:
+                    got = got + every(quant_z, lambda g, d: (g, d) == (a[1] - 2, a[2]))
             if fn == quant_z:
-                got = got + every(weave_z, lambda e, g, d, m0, m1: (g, d) == a) + every(past, lambda g, cc, i0, i1, b: g == a[0] - 2)
+                got = got + every(weave_z, lambda e, g, d, m0, m1: (g, d) == a)
+                got = got + every(past, lambda g, cc, i0, i1, b: g == a[0] - 2)
             if fn == w_turn:
                 got = got + every(load_w, lambda c0, c1, sl: c0 <= a[0] < c1)
             if fn == w_copy:
@@ -490,7 +499,8 @@ def tile_weighted_hankel_subspace_s11_kernel(
             if fn == w_quant:
                 got = got + every(w_copy, lambda e, c: c // 2 == a[0])
             if fn == future:
-                got = got + [(w_quant, a[1] // 2)] + every(quant_y, lambda g, n0, n1: g == a[0] and n0 // N in f_order[g][a[2] : a[3]])
+                got = got + [(w_quant, a[1] // 2)]
+                got = got + every(quant_y, lambda g, n0, n1: g == a[0] and a[2] <= n0 // N < a[3])
             if fn == epilogue:
                 got = got + every(future, lambda g, c, i0, i1, b: (g, c) == a) + [(load_level,), (load_lam, a[0])]
                 got = got + every(a_turn, lambda g, p, b: (RT * g + 2 * p) // 2 == (RT * a[0] + a[1] - AT_BUFS) // 2)
@@ -503,7 +513,8 @@ def tile_weighted_hankel_subspace_s11_kernel(
             if fn == past:
                 got = got + [(load_wp,)] + [(quant_z, a[0], d) for d in z_order[a[0]][a[2] : a[3]]]
             if fn == b_copy:
-                got = got + every(past, lambda g, cc, i0, i1, b: (g, cc) == a[1:3]) + every(quant_b, lambda g, n0, n1: g == a[1] - 2)
+                got = got + every(past, lambda g, cc, i0, i1, b: (g, cc) == a[1:3])
+                got = got + every(quant_b, lambda g, n0, n1: g == a[1] - 2)
             if fn == quant_b:
                 got = got + every(b_copy, lambda e, g, cc: g == a[0] and a[1] <= P * cc < a[2])
             if fn == sum_pass:

from contextlib import ExitStack

import concourse.mybir as mybir
from concourse.masks import make_identity

R, F, T, D, C = 1024, 1024, 2048, 1536, 512
FLOPS = 2 * (R * F * T + T * D * C + R * T * C)

F32 = mybir.dt.float32
BF16 = mybir.dt.bfloat16
U32 = mybir.dt.uint32
I32 = mybir.dt.int32
U8 = mybir.dt.uint8
FP8 = mybir.dt.float8_e4m3fn
FP8X4 = mybir.dt.float8_e4m3fn_x4
FP4X4 = mybir.dt.float4_e2m1fn_x4
ADD = mybir.AluOpType.add
MULT = mybir.AluOpType.mult
COPY = mybir.ActivationFunctionType.Copy

P = 128
N = 512
HALF = C // 2
GROUPS = T // N
FP = F // N
DP = D // N
RT = R // P

Y_GROUPS = 3
SLOTS = 8
W_BUFS = 2
AT_BUFS = RT + RT // 2 + 1

RUNS = (11, 10, 6, 5)
Y_POOL = 928
Y_HEAD = 448
Z_POOL = 120
Z_STEP = 48


def tile_weighted_hankel_subspace_s11_kernel(
    tc, w_f, y_f_bytes, y_f_scale, z_p, w_p_words, w_p_scales, level, lam, rho, out
):
    nc = tc.nc
    with ExitStack() as ctx:
        keep = ctx.enter_context(tc.tile_pool(name="keep", bufs=1))
        psum = ctx.enter_context(tc.psum_pool(name="psum", bufs=1))

        ident = keep.tile([P, P], F32, name="ident")
        y_scale = keep.tile([P, FP, 4], F32, name="y_scale")
        lev16 = keep.tile([P, RT], BF16, name="lev16")
        rho16 = keep.tile([P, RT], BF16, name="rho16")
        rhos = keep.tile([P, RT], F32, name="rhos")
        wcode = keep.tile([P, RT, FP, P], U32, name="wcode", align_bytes=64)
        wscale = keep.tile([P, RT, FP, P], U8, name="wscale", align_bytes=64)
        pw = keep.tile([P, DP, 2 * C], U8, name="pw", align_bytes=64)
        pws = keep.tile([P, DP, C], U8, name="pws", align_bytes=64)
        acode = keep.tile([P, GROUPS, R], U32, name="acode", align_bytes=64)
        ascale = keep.tile([P, GROUPS, R], U8, name="ascale", align_bytes=64)
        bcode = keep.tile([P, GROUPS, C], U32, name="bcode", align_bytes=64)
        bscale = keep.tile([P, GROUPS, C], U8, name="bscale", align_bytes=64)
        shared = keep.tile([P, FP * N * 4], BF16, name="shared", align_bytes=64)

        y_view = y_f_bytes.rearrange("(f p t) n -> f p t n", f=FP, p=P, t=4)
        z_view = z_p.rearrange("(d p t) n -> d p t n", d=DP, p=P, t=4)
        w_view = w_f.rearrange("(p c) f -> p c f", c=RT)
        out_view = out.rearrange("(p c) n -> p c n", c=RT)

        tiles = {}
        last = GROUPS - 1
        pairs = [(c, c + 1) for c in range(0, RT, 2)]
        z_order = [(2, 0, 1), (0, 1, 2), (2, 0, 1), (2, 1, 0)]

        def bank_tile(bank, shape, dtype=F32):
            return psum.tile(shape, dtype, name="bank%d" % bank)

        def copy(eng, dst, src):
            if eng == "S":
                nc.scalar.copy(out=dst, in_=src)
            elif eng == "V":
                nc.vector.tensor_copy(out=dst, in_=src)
            else:
                nc.gpsimd.tensor_scalar(out=dst, in0=src, scalar1=1.0, scalar2=0.0, op0=MULT, op1=ADD)

        def slot_tile(slot, shape, dtype):
            return keep.tile(shape, dtype, name="slot%d" % slot, align_bytes=64)

        def load_scale():
            nc.scalar.dma_start(out=y_scale[:], in_=y_f_scale.rearrange("(f p t) o -> p f (t o)", f=FP, p=P, t=4))

        def load_y(g, f, t0, t1):
            if t0 == 0:
                tiles["yb", g, f] = keep.tile([P, 4, N], U8, name="yb%d%d" % (g % Y_GROUPS, f), align_bytes=64)
            nc.sync.dma_start(out=tiles["yb", g, f][:, t0:t1], in_=y_view[f][:, t0:t1, N * g : N * g + N])

        def load_z(g, d, slot):
            tiles["zr", g, d] = slot_tile(slot, [P, 4, N], BF16)
            nc.sync.dma_start(out=tiles["zr", g, d][:], in_=z_view[d][:, :, N * g : N * g + N])

        def load_w(c0, c1, slot):
            if c0 % 2 == 0:
                tiles["wf", c0 // 2] = slot_tile(slot, [P, 2, F], BF16)
            nc.sync.dma_start(out=tiles["wf", c0 // 2][:, c0 % 2 : c0 % 2 + c1 - c0], in_=w_view[:, c0:c1, :])

        def load_level():
            nc.sync.dma_start(out=lev16[:], in_=level.rearrange("(p c) -> p c", c=RT))

        def load_rho():
            nc.sync.dma_start(out=rho16[:], in_=rho.rearrange("(p c) -> p c", c=RT))

        def load_lam(g):
            tiles["lam", g] = keep.tile([P, N], BF16, name="lam%d" % g)
            nc.sync.dma_start(out=tiles["lam", g][:], in_=lam[N * g : N * g + N].partition_broadcast(P))

        def zero_scales():
            nc.vector.memset(pws[:].rearrange("p d n -> p (d n)").bitcast(I32), 0)

        def load_wp():
            nc.sync.dma_start(out=pw[:], in_=w_p_words.rearrange("d p n -> p d n"))
            for q in range(4):
                nc.sync.dma_start(
                    out=pws[32 * q : 32 * q + 4, :, :].bitcast(I32),
                    in_=w_p_scales[:, 4 * q : 4 * q + 4, :].rearrange("d q n -> q d n").bitcast(I32),
                )

        def cast_rho():
            nc.vector.tensor_copy(out=rhos[:], in_=rho16[:])

        def widen(eng, g, f, t):
            if ("yw", g) not in tiles:
                tiles["yw", g] = keep.tile([P, FP * 4 * N], BF16, name="yw%d" % (g % 2), align_bytes=64)
            plane = tiles["yw", g][:].rearrange("p (f t n) -> p f t n", t=4, f=FP)[:, f, t, :]
            src = tiles["yb", g, f][:, t, :].bitcast(FP8)
            s = y_scale[:, f, t : t + 1]
            if eng == "S":
                nc.scalar.activation(out=plane, in_=src, func=COPY, scale=s)
            else:
                nc.vector.tensor_scalar(out=plane, in0=src, scalar1=s, scalar2=None, op0=MULT)

        def woven(n0, n1):
            return shared[:, 4 * n0 : 4 * n1]

        def weave_y(eng, g, n0, n1):
            dst = woven(n0, n1).rearrange("p (n t) -> p n t", t=4)
            f = n0 // N
            src = tiles["yw", g][:, 4 * N * f : 4 * N * (f + 1)].rearrange("p (t n) -> p t n", t=4)
            src = src[:, :, n0 - N * f : n1 - N * f]
            copy(eng, dst.rearrange("p (c i) t -> p c t i", i=4), src.rearrange("p t (c i) -> p c t i", i=4))

        def quant_y(g, n0, n1):
            if ("yc", g) not in tiles:
                tiles["yc", g] = keep.tile([P, FP * N], U32, name="yc%d" % (g % 2), align_bytes=64)
                tiles["ys", g] = keep.tile([P, FP * N], U8, name="ys%d" % (g % 2), align_bytes=64)
            nc.vector.quantize_mx(
                out=tiles["yc", g][:, n0:n1].bitcast(FP8X4),
                scales=tiles["ys", g][:, n0:n1],
                in_=woven(n0, n1),
            )

        def weave_z(eng, g, d, m0, m1):
            if ("zi", g, d) not in tiles:
                if g < 2 and d == 0:
                    tiles["zi", g, d] = woven(0, N)
                else:
                    tiles["zi", g, d] = keep.tile([P, 4 * N], BF16, name="zi%d%d" % (g % 2, d), align_bytes=64)[:]
            dst, src = tiles["zi", g, d], tiles["zr", g, d][:]
            if eng == "G":
                dst = dst.rearrange("p (s m j) -> p m j s", s=4, j=4)
                src = src.rearrange("p j (m s) -> p m j s", s=4)
            else:
                dst = dst.rearrange("p (s m h e) -> p m h s e", s=4, h=2, e=2)
                src = src.rearrange("p (h e) (m s) -> p m h s e", e=2, s=4)
            copy(eng, dst[:, m0:m1], src[:, m0:m1])

        def quant_z(g, d):
            if ("zc", g) not in tiles:
                tiles["zc", g] = keep.tile([P, DP, N], U32, name="zc%d" % (g % 2), align_bytes=64)
                tiles["zs", g] = keep.tile([P, DP, N], U8, name="zs%d" % (g % 2), align_bytes=64)
            nc.vector.quantize_mx(
                out=tiles["zc", g][:, d].bitcast(FP8X4), scales=tiles["zs", g][:, d], in_=tiles["zi", g, d]
            )

        def w_turn(c, bank):
            wt = bank_tile(bank, [P, FP, 2, P])
            words = tiles["wf", c // 2][:, c % 2, :].bitcast(F32)
            for f in range(FP):
                for u in range(2):
                    nc.tensor.transpose(wt[:, f, u, :], words[:, 256 * f + u : 256 * (f + 1) : 2], ident[:])
            tiles["wt", c] = wt

        def w_copy(eng, c):
            if c % 2 == 0:
                name = "wi%d" % (c // 2 % W_BUFS)
                tiles["wi", c // 2] = keep.tile([P, 2, FP, P, 2], F32, name=name, align_bytes=64)
            copy(eng, tiles["wi", c // 2][:, c % 2], tiles["wt", c][:].rearrange("p f u r -> p f r u"))

        def w_quant(pair):
            nc.vector.quantize_mx(
                out=wcode[:, 2 * pair : 2 * pair + 2].rearrange("p c f r -> p (c f r)").bitcast(FP8X4),
                scales=wscale[:, 2 * pair : 2 * pair + 2].rearrange("p c f r -> p (c f r)"),
                in_=tiles["wi", pair][:].rearrange("p c f r u -> p (c f r u)").bitcast(BF16),
            )

        def future(g, c, i0, i1, bank):
            if i0 == 0:
                tiles["fp", g, c] = bank_tile(bank, [P, N])
            for f in range(i0, i1):
                nc.tensor.matmul_mx(
                    out=tiles["fp", g, c][:],
                    lhsT=wcode[:, c, f, :].bitcast(FP8X4),
                    lhsT_scale=wscale[:, c, f, :],
                    rhs=tiles["yc", g][:, N * f : N * f + N].bitcast(FP8X4),
                    rhs_scale=tiles["ys", g][:, N * f : N * f + N],
                    start=(f == 0),
                    stop=(f == FP - 1),
                )

        def epilogue(g, c):
            at = keep.tile([P, N], BF16, name="at%d" % ((RT * g + c) % AT_BUFS), align_bytes=64)
            nc.vector.scalar_tensor_tensor(
                out=at[:].rearrange("p (u q) -> p u q", u=2),
                in0=tiles["fp", g, c][:].rearrange("p (q u) -> p u q", u=2),
                scalar=lev16[:, c : c + 1],
                in1=tiles["lam", g][:].rearrange("p (q u) -> p u q", u=2),
                op0=ADD,
                op1=MULT,
            )
            tiles["at", g, c] = at

        def a_turn(g, pair, bank):
            tp = bank_tile(bank, [P, 2, 2, P])
            for i in range(2):
                words = tiles["at", g, 2 * pair + i][:].bitcast(F32)
                for u in range(2):
                    nc.tensor.transpose(tp[:, i, u, :], words[:, P * u : P * u + P], ident[:])
            tiles["tp", g, pair] = tp

        def a_copy(eng, g, pair):
            if ("ai", g) not in tiles:
                tiles["ai", g] = keep.tile([P, RT, P, 2], F32, name="ai%d" % g, align_bytes=64)
            dst = tiles["ai", g][:, 2 * pair : 2 * pair + 2]
            copy(eng, dst, tiles["tp", g, pair][:].rearrange("p c u r -> p c r u"))

        def quant_a(g, p0, p1):
            nc.vector.quantize_mx(
                out=acode[:, g, 2 * P * p0 : 2 * P * p1].bitcast(FP8X4),
                scales=ascale[:, g, 2 * P * p0 : 2 * P * p1],
                in_=tiles["ai", g][:, 2 * p0 : 2 * p1].rearrange("p c r u -> p (c r u)").bitcast(BF16),
            )

        def past(g, cc, i0, i1, bank):
            if i0 == 0:
                tiles["pp", g, cc] = bank_tile(bank, [P, 4, P])
            pp = tiles["pp", g, cc]
            for i in range(i0, i1):
                d = z_order[g][i]
                for s in range(4):
                    nc.tensor.matmul_mx(
                        out=pp[:, 2 * (s % 2) + s // 2, :],
                        lhsT=tiles["zc", g][:, d, P * s : P * s + P].bitcast(FP8X4),
                        lhsT_scale=tiles["zs", g][:, d, P * s : P * s + P],
                        rhs=pw[:, d, 2 * P * cc : 2 * P * (cc + 1)].bitcast(FP4X4),
                        rhs_scale=pws[:, d, P * cc : P * cc + P],
                        start=(i == 0 and s == 0),
                        stop=(i == DP - 1 and s == 3),
                    )

        def b_copy(eng, g, cc):
            if ("pi", g) not in tiles:
                tiles["pi", g] = keep.tile([P, C, 4], BF16, name="pi%d" % (g % 2), align_bytes=64)
            copy(eng, tiles["pi", g][:, P * cc : P * cc + P, :], tiles["pp", g, cc][:].rearrange("p s n -> p n s"))

        def quant_b(g, n0, n1):
            nc.vector.quantize_mx(
                out=bcode[:, g, n0:n1].bitcast(FP8X4),
                scales=bscale[:, g, n0:n1],
                in_=tiles["pi", g][:, n0:n1, :].rearrange("p n s -> p (n s)"),
            )

        def sum_pass(half, cs, g, bank):
            if g == 0:
                tiles["h", half, cs] = bank_tile(bank, [P, len(cs), HALF])
            for i, c in enumerate(cs):
                nc.tensor.matmul_mx(
                    out=tiles["h", half, cs][:, i, :],
                    lhsT=acode[:, g, P * c : P * c + P].bitcast(FP8X4),
                    lhsT_scale=ascale[:, g, P * c : P * c + P],
                    rhs=bcode[:, g, HALF * half : HALF * half + HALF].bitcast(FP8X4),
                    rhs_scale=bscale[:, g, HALF * half : HALF * half + HALF],
                    start=(g == 0 and i == 0),
                    stop=(g == last and i == len(cs) - 1),
                )

        def scale_out(eng, half, cs, i, slot):
            if ("ho", slot) not in tiles:
                tiles["ho", slot] = slot_tile(slot % SLOTS, [P, 2, HALF], F32)
            src = tiles["h", half, cs][:, i, :]
            dst = tiles["ho", slot][:, i, :]
            s = rhos[:, cs[i] : cs[i] + 1]
            if eng == "S":
                nc.scalar.activation(out=dst, in_=src, func=COPY, scale=s)
            else:
                nc.vector.tensor_scalar(out=dst, in0=src, scalar1=s, scalar2=None, op0=MULT)

        def store(half, cs, i0, i1, slot):
            rows = out_view[:, cs[i0] : cs[i1 - 1] + 1, HALF * half : HALF * half + HALF]
            nc.sync.dma_start(out=rows, in_=tiles["ho", slot][:, i0:i1])

        def planes(eng, g, f, ts):
            return [(widen, eng, g, f, t) for t in ts]

        def epilogues(first, count):
            return [(epilogue, i // RT, i % RT) for i in range(first, first + count)]

        def futures(first, banks, i0=0, i1=FP):
            return [(future, (first + i) // RT, (first + i) % RT, i0, i1, b) for i, b in enumerate(banks)]

        def w_turns(pair, bank):
            return [(w_turn, c, bank + c % 2) for c in pairs[pair]]

        def w_copies(pair):
            return [(w_copy, "S", c) for c in pairs[pair]]

        def a_turns(g, ps, banks):
            return [(a_turn, g, p, b) for p, b in zip(ps, banks)]

        def a_copies(g, ps):
            return [(a_copy, "S", g, p) for p in ps]

        def b_copies(g, ccs):
            return [(b_copy, "S", g, cc) for cc in ccs]

        def quants_y(g):
            return [(quant_y, g, N * f, N * f + N) for f in range(FP)]

        def quants_z(g):
            return [(quant_z, g, d) for d in z_order[g]]

        def run(i):
            return epilogues(sum(RUNS[:i]), RUNS[i])

        sync = [(load_y, 0, 0, 0, 2), (load_y, 0, 0, 2, 4), (load_y, 0, 1, 0, 4), (load_w, 0, 1, 0), (load_w, 1, 2, 0)]
        sync += [(load_y, 1, 0, 0, 4), (load_w, 2, 4, 1), (load_w, 4, 6, 2), (load_y, 1, 1, 0, 4), (load_w, 6, 8, 3)]
        sync += [(load_y, 2, 0, 0, 4), (load_level,), (load_lam, 0), (load_y, 2, 1, 0, 4)]
        sync += [(load_y, last, f, 0, 4) for f in range(FP)] + [(load_lam, g) for g in range(1, GROUPS)]
        z_tiles = [(0, d) for d in z_order[0]] + [(g, d) for g in range(1, GROUPS) for d in range(DP)]
        z_loads = [(load_z, g, d, (len(pairs) + i) % SLOTS) for i, (g, d) in enumerate(z_tiles)]
        sync += z_loads[:DP] + [(load_wp,), (load_rho,)] + z_loads[DP:]

        ends = [(0, cs) for cs in pairs] + [(1, cs) for cs in pairs[:-1]] + [(1, (c,)) for c in pairs[-1]]
        outs = [[(scale_out, "VS"[k % 2], h, cs, i, k) for i in range(len(cs))] for k, (h, cs) in enumerate(ends)]
        for k, (h, cs) in enumerate(ends):
            by_tile = k >= len(ends) - 3
            sync += [(store, h, cs, i, i + 1, k) for i in range(len(cs))] if by_tile else [(store, h, cs, 0, 2, k)]

        room = P + (4 + 3 + 2 * 3) * Z_STEP
        reach = {2: Z_STEP, last: room - 5 * P - Z_STEP}
        shares = [(0, 2, 0, P), (0, 1, 0, P), (1, 1, 0, P), (2, 0, 0, P), (2, 1, 0, reach[2])]
        shares += [(last, 1, 0, reach[last]), (last, 0, 0, P)]
        rows = [(g, d, m) for g, d, m0, m1 in shares for m in range(m0, m1)]

        def z_rows(n):
            part = [rows.pop(0) for i in range(n)]
            cut = [(g, d, [m for h, e, m in part if (h, e) == (g, d)]) for g, d, m0, m1 in shares]
            return [(weave_z, "S", g, d, ms[0], ms[-1] + 1) for g, d, ms in cut if ms]

        vector = [(zero_scales,)] + planes("V", 0, 0, (1, 2, 3)) + planes("V", 0, 1, (3,))
        vector += [(weave_y, "V", 0, 0, Y_HEAD)] + planes("V", 0, 1, (2,))
        vector += [(quant_y, 0, 0, N), (weave_y, "V", 0, N, 2 * N), (w_quant, 0), (quant_y, 0, N, 2 * N)]
        vector += planes("V", 1, 0, (3,)) + planes("V", 1, 1, (2, 3)) + [(weave_y, "V", 1, 0, N), (w_quant, 1)]
        vector += [(weave_y, "V", 1, N, 2 * N), (w_quant, 2), (quant_y, 1, 0, N), (w_quant, 3), (quant_y, 1, N, 2 * N)]
        vector += run(0) + quants_y(2) + run(1) + quants_y(last) + run(2) + quants_z(0)
        vector += run(3) + [(weave_z, "V", 1, 0, Z_POOL, P), (weave_z, "V", 1, 2, 0, P)] + quants_z(1)
        for g in range(2, GROUPS):
            vector += [(quant_a, g - 2, 0, 4), (quant_b, g - 2, 0, HALF), (weave_z, "V", g, 2, 0, P)]
            vector += [(quant_b, g - 2, HALF, C), (weave_z, "V", g, 1, reach[g], P)] + quants_z(g)
        for g in range(2, GROUPS):
            vector += [(quant_a, g, 0, 4), (quant_b, g, 0, HALF)]
        vector += [(cast_rho,), (quant_b, 2, HALF, C)] + outs[0] + [(quant_b, last, HALF, C)]
        vector += [s for out_steps in outs[2::2] for s in out_steps]

        scalar = [(load_scale,)] + planes("S", 0, 0, (0,)) + planes("S", 0, 1, (0,)) + [(weave_y, "S", 0, Y_HEAD, N)]
        scalar += planes("S", 0, 1, (1,)) + w_copies(0) + planes("S", 1, 0, (0, 1, 2)) + w_copies(1)
        scalar += planes("S", 1, 1, (0, 1)) + w_copies(2) + planes("S", 2, 0, (0,)) + w_copies(3)
        scalar += planes("S", 2, 0, (1, 2, 3)) + planes("S", 2, 1, range(4))
        scalar += planes("S", last, 0, range(4)) + planes("S", last, 1, (0,)) + a_copies(0, (0, 1))
        scalar += planes("S", last, 1, (1, 2)) + a_copies(0, (2, 3)) + planes("S", last, 1, (3,))
        scalar += z_rows(Z_STEP) + [(weave_y, "S", last, Y_POOL, 2 * N)] + z_rows(P - Z_STEP) + a_copies(1, range(4))
        scalar += z_rows(4 * Z_STEP) + a_copies(2, range(4))
        scalar += z_rows(3 * Z_STEP) + b_copies(0, (0, 1, 2)) + a_copies(last, range(4)) + b_copies(0, (3,))
        for g in (1, 2):
            for ccs in ((0, 1), (2,), (3,)):
                scalar += z_rows(Z_STEP) + b_copies(g, ccs)
        scalar += b_copies(last, range(4)) + [s for out_steps in outs[1::2] for s in out_steps]

        gpsimd = [(weave_y, "G", 2, 0, N), (weave_y, "G", 2, N, 2 * N)]
        gpsimd += [(weave_y, "G", last, 0, N), (weave_y, "G", last, N, Y_POOL)]
        gpsimd += [(weave_z, "G", 0, 0, 0, P), (weave_z, "G", 1, 0, 0, Z_POOL)]

        tensor = w_turns(0, 4) + w_turns(1, 6) + w_turns(2, 4) + futures(0, (0,)) + w_turns(3, 6)
        tensor += futures(1, range(1, 8)) + futures(8, range(5)) + a_turns(0, (0, 1), (5, 6)) + futures(13, (7, 0))
        one, two = (4, 7, 0, 5), (6, 1, 2, 3)
        tensor += a_turns(0, (2, 3), (1, 2)) + futures(15, (5,)) + futures(16, two)
        tensor += a_turns(1, range(4), one) + futures(20, two)
        tensor += futures(24, one[:3], 0, 1) + futures(24, one[:3], 1, 2) + futures(27, one[3:])
        tensor += a_turns(2, range(4), two) + futures(28, one[:3] + two[:1])
        b_banks = two[1:]
        sum_banks = one[3:] + one[:3] + two[:1]
        tensor += [(past, 0, cc, i, i + 1, b_banks[cc]) for i in range(DP) for cc in range(2)]
        tensor += [(past, 0, 2, 0, DP, b_banks[2])] + a_turns(last, range(4), sum_banks[:4])
        tensor += [(past, 0, 3, 0, DP, sum_banks[4])]

        def b_bank(g, cc):
            return b_banks[(4 * (g - 1) + cc) % len(b_banks)]

        def open_sums(ks, g):
            return [(sum_pass,) + ends[k] + (g, sum_banks[k]) for k in ks]

        for g in range(1, GROUPS):
            tensor += [(past, g, cc, i, i + 1, b_bank(g, cc)) for i in range(DP) for cc in range(2)]
            behind = [open_sums(ks, g - 1) if g < last else [] for ks in ((0, 1, 2), (3, 4))]
            tensor += [(past, g, 2, 0, DP, b_bank(g, 2))] + behind[0] + [(past, g, 3, 0, DP, b_bank(g, 3))] + behind[1]
        tensor += open_sums((0,), 2)
        for k in range(len(sum_banks)):
            tensor += open_sums(range(k + 1, len(sum_banks))[:1], 2) + open_sums((k,), last)
        late_banks = [b_bank(last, cc) for cc in (1, 2, 3)] + [sum_banks[0]]
        for end, bank in zip(ends[len(sum_banks) :], late_banks):
            tensor += [(sum_pass,) + end + (g, bank) for g in range(GROUPS)]

        steps = sync + vector + scalar + gpsimd + tensor

        def every(fn, test):
            return [s for s in steps if s[0] == fn and test(*s[1:])]

        def before(step, same):
            order = sync + tensor
            ahead = [s for s in order[: order.index(step)] if same(s)]
            return ahead[-1:]

        def bank_users(step):
            fn = step[0]
            if fn == w_turn:
                return every(w_copy, lambda e, c: c == step[1])
            if fn == future:
                return [(epilogue,) + step[1:3]]
            if fn == a_turn:
                return every(a_copy, lambda e, g, p: (g, p) == step[1:3])
            if fn == past:
                return every(b_copy, lambda e, g, cc: (g, cc) == step[1:3])
            return every(scale_out, lambda e, h, cs, i, sl: (h, cs) == step[1:3])

        def slot_users(step):
            if step[0] == load_w:
                return every(w_turn, lambda c, b: c // 2 == step[1] // 2)
            return every(weave_z, lambda e, g, d, m0, m1: (g, d) == step[1:3])

        def shared_readers(step):
            if step[0] == weave_y:
                return every(quant_y, lambda h, n0, n1: h < step[2] and n0 < step[4] and step[3] < n1)
            return [(quant_y, last, 0, N)] + every(quant_z, lambda h, d: h < step[2] and d == 0)

        def needs(step):
            fn, a = step[0], step[1:]
            got = []
            if step in tensor and (fn in (w_turn, a_turn) or a[2] == 0):
                for s in before(step, lambda s: s in tensor and s[-1] == a[-1]):
                    got = got + bank_users(s)
            if fn == load_z:
                for s in before(step, lambda s: s[0] in (load_w, load_z) and s[-1] == a[-1]):
                    got = got + slot_users(s)
            if fn == load_y:
                got = got + every(widen, lambda e, g, f, t: (g, f) == (a[0] - Y_GROUPS, a[1]))
            if fn == load_wp:
                got = got + [(zero_scales,)]
            if fn == cast_rho:
                got = got + [(load_rho,)]
            if fn == widen:
                got = got + [(load_scale,)] + every(load_y, lambda g, f, t0, t1: (g, f) == a[1:3] and t0 <= a[3])
                got = got + every(weave_y, lambda e, g, n0, n1: g == a[1] - 2)
            if fn == weave_y:
                got = got + every(widen, lambda e, g, f, t: g == a[1] and a[2] < N * f + N and N * f < a[3])
                got = got + shared_readers(step)
            if fn == quant_y:
                got = got + every(weave_y, lambda e, g, n0, n1: g == a[0] and n0 < a[2] and a[1] < n1)
                got = got + every(future, lambda g, c, i0, i1, b: g == a[0] - 2)
            if fn == weave_z:
                got = got + every(load_z, lambda g, d, sl: (g, d) == a[1:3])
                if a[0] == "G":
                    got = got + shared_readers(step)
                else:
                    got = got + every(quant_z, lambda g, d: (g, d) == (a[1] - 2, a[2]))
            if fn == quant_z:
                got = got + every(weave_z, lambda e, g, d, m0, m1: (g, d) == a)
                got = got + every(past, lambda g, cc, i0, i1, b: g == a[0] - 2)
            if fn == w_turn:
                got = got + every(load_w, lambda c0, c1, sl: c0 <= a[0] < c1)
            if fn == w_copy:
                got = got + every(w_turn, lambda c, b: c == a[1]) + every(w_quant, lambda p: p == a[1] // 2 - W_BUFS)
            if fn == w_quant:
                got = got + every(w_copy, lambda e, c: c // 2 == a[0])
            if fn == future:
                got = got + [(w_quant, a[1] // 2)]
                got = got + every(quant_y, lambda g, n0, n1: g == a[0] and a[2] <= n0 // N < a[3])
            if fn == epilogue:
                got = got + every(future, lambda g, c, i0, i1, b: (g, c) == a) + [(load_level,), (load_lam, a[0])]
                got = got + every(a_turn, lambda g, p, b: (RT * g + 2 * p) // 2 == (RT * a[0] + a[1] - AT_BUFS) // 2)
            if fn == a_turn:
                got = got + [(epilogue, a[0], c) for c in pairs[a[1]]]
            if fn == a_copy:
                got = got + every(a_turn, lambda g, p, b: (g, p) == a[1:3])
            if fn == quant_a:
                got = got + every(a_copy, lambda e, g, p: g == a[0] and a[1] <= p < a[2])
            if fn == past:
                got = got + [(load_wp,)] + [(quant_z, a[0], d) for d in z_order[a[0]][a[2] : a[3]]]
            if fn == b_copy:
                got = got + every(past, lambda g, cc, i0, i1, b: (g, cc) == a[1:3])
                got = got + every(quant_b, lambda g, n0, n1: g == a[1] - 2)
            if fn == quant_b:
                got = got + every(b_copy, lambda e, g, cc: g == a[0] and a[1] <= P * cc < a[2])
            if fn == sum_pass:
                got = got + every(quant_a, lambda g, p0, p1: g == a[2] and p0 <= a[1][0] // 2 < p1)
                got = got + every(quant_b, lambda g, n0, n1: g == a[2] and n0 <= HALF * a[0] < n1)
            if fn == scale_out:
                got = got + [(cast_rho,)] + every(sum_pass, lambda h, cs, g, b: (h, cs) == a[1:3])
                got = got + [s for z in every(load_z, lambda g, d, sl: sl == a[4] % SLOTS) for s in slot_users(z)]
                got = got + every(store, lambda h, cs, i0, i1, sl: sl == a[4] - SLOTS)
            if fn == store:
                got = got + every(scale_out, lambda e, h, cs, i, sl: (h, cs) == a[0:2] and a[2] <= i < a[3])
            return got

        with tc.manual_schedule():
            make_identity(nc, ident[:])
            queues = [list(q) for q in (sync, vector, scalar, gpsimd, tensor)]
            done = []
            while any(queues):
                ready = [q for q in queues if q and all(s in done for s in needs(q[0]))]
                step = ready[0].pop(0)
                step[0](*step[1:])
                done.append(step)
